import numpy as np, ml_dtypes
CORES = [13,21,141,149]
N = 4
import mx_ref
BF = ml_dtypes.bfloat16
def entries(a):
    return np.ascontiguousarray(a.T).reshape(-1)
def table(e):
    return np.ascontiguousarray(np.reshape(e, (-1, 16)).T).astype(np.int32)
def cols(t, e):
    v = np.concatenate([t.reshape(128, -1, 4), np.zeros((128, 1, 4), BF)], axis=1)
    return np.ascontiguousarray(v[:, e]).reshape(128, -1)
def cut(t, i, w=512):
    return t[:, w * i:w * i + w]
def f(rng, *shape):
    return mx_ref.flush((rng.standard_normal(shape, dtype=np.float32) * np.exp2(rng.integers(-2, 3, shape[:-1] + (1,)))).astype(BF))
def wide(rng, *shape, cols=0):
    v = rng.standard_normal(shape, dtype=np.float32) * np.exp2(rng.integers(-12, 13, shape)).astype(np.float32)
    if cols: v *= np.repeat(np.exp2(rng.integers(-cols, cols + 1, shape[:-2] + (1, shape[-1] // 4))) * (rng.random(shape[:-2] + (1, shape[-1] // 4)) > 0.0625), 4, axis=-1).astype(np.float32)
    return mx_ref.flush(v.astype(BF))
T, V, M, CAPP, R, O = 256, 128, 192, 48, 3, 1
START = np.repeat(np.arange(N), V)
def loose(rng, at, to, who, but=-1):
    to = to.copy(); n = np.zeros((N, N), int); np.add.at(n, (at, to), 1)
    for i in rng.permutation(who):
        q = rng.integers(0, N)
        if q != but and n[:, q].sum() < M and (q == at[i] or n[at[i], q] < CAPP): n[at[i], to[i]] -= 1; n[at[i], q] += 1; to[i] = q
    return to
def turn(rng, at):
    to = at.copy(); far = 1 + rng.permutation(N - 1)
    for s in range(N):
        k = rng.permutation(np.flatnonzero(at == s))
        for i in range(min(N - 1, len(k) // CAPP)): to[k[CAPP * i:CAPP * i + CAPP]] = (s + far[i]) % N
    return to
def collect(rng, at, e):
    to = at.copy(); k = rng.permutation(np.flatnonzero(at == e))[M - (N - 1) * CAPP:]
    to[k] = (e + 1 + np.arange(len(k)) % (N - 1)) % N
    for s in range(N):
        if s != e: to[rng.permutation(np.flatnonzero(at == s))[:CAPP]] = e
    return to
def spill(rng, at, to, who, ranks):
    to = to.copy(); n = np.zeros((N, N), int); others = np.setdiff1d(np.arange(N * V), who); np.add.at(n, (at[others], to[others]), 1)
    for i in rng.permutation(who):
        q = ranks[np.argmin(np.where(n[at[i], ranks] < CAPP, n[:, ranks].sum(axis=0), N * V))]
        n[at[i], q] += 1; to[i] = q
    return to
def lists(rng, a, share=0.25):
    nx = rng.integers(0, N * T, (N, 2 * T)); free = [list(rng.permutation(2 * T)) for r in range(N)]
    way = np.zeros((R - 1, N * V), int)
    for k in range(R - 2, -1, -1):
        goal = a[k + 1] if k == R - 2 else a[k + 1] * T + way[k + 1] // 2
        known = {}
        for i in rng.permutation(N * V):
            s = int(a[k][i]); L = known.setdefault((s, int(goal[i])), [])
            if not L or rng.random() >= share:
                L.append(free[s].pop()); way[k, i] = L[-1]
            else: way[k, i] = L[rng.integers(0, len(L))]
        if k < R - 2: nx[a[k], way[k]] = goal
    nx[a[R - 2], way[R - 2]] = a[R - 1] * T + rng.integers(0, T, N * V)
    st = (way[0] // 2).reshape(N, V); bt = sum((way[k] % 2) << k for k in range(R - 1)).reshape(N, V)
    return {"nx": np.stack([table(e) for e in nx]), "st": np.stack([table(e) for e in st]), "bt": np.stack([table(e) for e in bt])}
def setup_inputs(rng):
    a = [START]
    for k in range(R - 1): a.append(loose(rng, a[k], a[k], np.arange(N * V)))
    return {"x": f(rng, N, 128, 4 * T), "w": f(rng, N, 128, R * O * 512), **lists(rng, a)}
def setup_inputs_through(rng):
    h = rng.integers(1, N); a = [START, START.copy(), (START + h) % N]
    for s in range(N):
        for g, k in enumerate(np.array_split(V * s + rng.permutation(V), -(-V // CAPP))): a[1][k] = (s + g) % N
    return {**setup_inputs(rng), **lists(rng, a)}
def setup_inputs_far(rng):
    a = [START]
    for k in range(R - 1): a.append(turn(rng, a[k]))
    a[R - 1] = loose(rng, a[R - 2], a[R - 1], np.flatnonzero(a[R - 1] == a[R - 2]))
    return {**setup_inputs(rng), **lists(rng, a)}
def setup_inputs_gather(rng):
    p = rng.permutation(N); home, end, bare = p[:3]; a = [START, START.copy()]
    for j, s in enumerate(p[2:]): a[1][rng.permutation(np.flatnonzero(START == s))[:min(CAPP, max(0, M - V - j * CAPP))]] = home
    to = collect(rng, a[1], end)
    to = spill(rng, a[1], to, np.flatnonzero(((a[1] == end) & (to != end)) | (to == bare)), np.append(p[3:], home))
    a.append(loose(rng, a[1], to, np.flatnonzero((to == a[1]) & (a[1] != end)), but=bare))
    return {**setup_inputs(rng), **lists(rng, a, share=0.75)}
def setup_inputs_stay(rng):
    p = rng.integers(0, N); a = [START, collect(rng, START, p)]
    a.append(loose(rng, a[1], a[1], np.flatnonzero(a[1] != p)))
    return {**setup_inputs(rng), **lists(rng, a)}
def setup_inputs_spread(rng):
    d = setup_inputs(rng); d["x"] = wide(rng, N, 128, 4 * T, cols=8); return d
def follow(nx, st, bt):
    n = np.concatenate([entries(t) for t in nx]); bits = np.concatenate([entries(t) for t in bt])
    at = [np.concatenate([entries(st[r]) + r * T for r in range(N)])]
    for k in range(R - 1): at.append(n[2 * at[k] + (bits >> k & 1)])
    return at
def check_inputs(d):
    b = []
    for name, top in (("nx", N * T), ("st", T), ("bt", 2 ** (R - 1))):
        if d[name].min() < 0 or d[name].max() >= top: b.append(name)
    if b: return b
    at = [t // T for t in follow(d["nx"], d["st"], d["bt"])]
    for k in range(R):
        if np.bincount(at[k], minlength=N).max() > M: b.append("walkers on a rank at step " + str(k))
    for k in range(R - 1):
        n = np.zeros((N, N), int); np.add.at(n, (at[k], at[k + 1]), 1); np.fill_diagonal(n, 0)
        if n.max() > CAPP: b.append("walkers from a rank to another from step " + str(k))
    return b
def reference(x, w, nx, st, bt):
    nodes = np.concatenate([x[r] for r in range(N)], axis=1)
    at = follow(nx, st, bt)
    y = np.zeros((N, 128, O * M), np.float32); ids = np.full((N, 2, M), -1, np.float32)
    for e in range(N):
        m = np.flatnonzero(at[R - 1] // T == e)
        ids[e, 0, :len(m)] = m // V; ids[e, 1, :len(m)] = m % V
        for k in range(R):
            c = np.full(M, -1); c[:len(m)] = at[k][m]
            q = mx_ref.quantize(cols(nodes, c))
            for o in range(O): y[e][:, M * o:M * o + M] += mx_ref.matmul(mx_ref.quantize(np.ascontiguousarray(cut(w[e], k * O + o))), q)
    return {"y": y, "id": ids}

@@ -1,0 +1,420 @@
+from concourse.bass import DstId, RemoteDMATransfer
+from concourse.mybir import dt, AluOpType, ActivationFunctionType
+
+N, V, M, CAP, TX = 4, 128, 192, 48, 256
+F, B, I, U = "float32", "bfloat16", "int32", "uint16"
+CODE, PLANE = "float8_e4m3fn_x4", "uint8"
+
+
+def _sb(d, *s):
+    return ("sbuf", [128] + list(s), d)
+
+
+SCRATCH = {
+    "xb": _sb(B, 1024), "wb": _sb(B, 1536),
+    "xq": _sb(CODE, 256), "xs": _sb(PLANE, 256),
+    "cb": _sb(CODE, 400), "cbs": _sb(PLANE, 400),
+    "wq": _sb(CODE, 384), "ws": _sb(PLANE, 384),
+    "pk1": _sb(CODE, 144), "ps1": _sb(PLANE, 144),
+    "pk2": _sb(CODE, 288), "ps2": _sb(PLANE, 288),
+    "fc1": _sb(CODE, 48), "fs1": _sb(PLANE, 48), "fc2": _sb(CODE, 96), "fs2": _sb(PLANE, 96),
+    "fu": _sb(U, 8), "fn": ("dram", [128, 4], I),
+    "lc": _sb(CODE, 288), "ls": _sb(PLANE, 288),
+    "nat": ("dram", [128, 4], I), "natl": ("dram", [3, 128, 4], I),
+    "pi": _sb(I, 1), "ic": _sb(I, 4), "col": _sb(F, 32), "iob": _sb(F, 16),
+    "c0w": _sb(B, 512), "ic1": _sb(B, 512), "iot": _sb(B, 256),
+    "zb": _sb(B, 512), "ones": _sb(B, 512), "offsel": _sb(U, 16), "trc": _sb(F, 16), "ac": _sb(F, 16),
+    "data0": _sb(B, 512), "ki": _sb(B, 256), "kc": _sb(F, 12, 3),
+    "stb": _sb(I, 16), "b0": _sb(I, 8), "b1": _sb(I, 8), "sx": _sb(I, 8), "sy": _sb(I, 8), "sz": _sb(I, 8), "sw": _sb(I, 8),
+    "q1l": _sb(U, 8), "p1w": _sb(I, 512), "nl": _sb(F, 128), "nd": _sb(F, 16, 16), "tn": _sb(F, 8, 32), "uf": _sb(F, 8),
+    "ul": _sb(U, 32), "win2": _sb(B, 2048), "gs1": _sb(B, 256), "tg": _sb(B, 8, 32),
+    "x1": _sb(F, 4, 4), "x1b": _sb(F, 4, 2), "x1c": _sb(F, 4), "off1": _sb(U, 4),
+    "c0l": _sb(B, 128), "vs1": _sb(B, 64), "c0m": _sb(B, 64), "w1": _sb(B, 272),
+    "d1": _sb(B, 18, 16), "td1": _sb(B, 9, 32), "l1f": _sb(F, 9), "list1": _sb(U, 10),
+    "nxs": _sb(I, 32), "nxt": _sb(I, 32), "nxr": _sb(I, 16), "mk": _sb(B, 64),
+    "g2": _sb(B, 512), "s2": _sb(B, 512), "tm": _sb(B, 16, 32), "ts": _sb(B, 16, 32),
+    "x2": _sb(F, 16, 4), "x2b": _sb(F, 16, 2), "x2c": _sb(F, 16), "off2": _sb(U, 16),
+    "vsel": _sb(B, 256), "w2": _sb(B, 400), "d2": _sb(B, 18, 16), "td2": _sb(B, 9, 32),
+    "h2": _sb(F, 3, 3, 4), "nf": _sb(F, 3, 2, 3), "list2": _sb(U, 18),
+    "ui": _sb(I, 32), "ua": _sb(I, 32), "uc": _sb(I, 32), "u3": _sb(U, 32),
+    "p3w": _sb(I, 2048), "n2": _sb(I, 512), "r3": _sb(I, 512), "m3": _sb(B, 512), "s3": _sb(B, 512),
+    "tm3": _sb(B, 16, 32), "ts3": _sb(B, 16, 32), "v3": _sb(F, 16), "off3": _sb(U, 16),
+    "c2s": _sb(I, 256), "c2a": _sb(I, 256), "vselk": _sb(B, 256), "val3": _sb(B, 256), "w3": _sb(B, 448),
+    "t3": _sb(B, 6, 32), "c3": _sb(B, 6, 32), "pl": _sb(B, 192), "sc": _sb(B, 192), "idl": _sb(F, 192),
+    "dp": _sb(B, 24, 16), "ds": _sb(B, 24, 16), "tp": _sb(B, 12, 32), "tc": _sb(B, 12, 32),
+    "x3": _sb(F, 12, 5), "x3b": _sb(F, 12, 2), "x3c": _sb(F, 12), "q0": _sb(U, 12), "qb": _sb(U, 12), "qc": _sb(U, 12),
+    "ps": ("psum", [128, 2048], F), "aw": _sb(F, 648), "bw": _sb(F, 264), "cw": _sb(F, 264),
+    "t1": _sb(F, 192), "t2": _sb(F, 192), "yo": _sb(F, 192),
+}
+SEMAPHORES = ["sv", "sa", "st", "g0", "g1", "g2", "g3", "g4", "g5", "dsb", "dnx", "dns", "dx", "dw", "dnat", "dmk", "down", "drem", "dy", "did",
+              "m0", "m1", "c1", "c2", "loc", "f0", "f1", "f1c", "f1s", "f2c", "f2s"]
+
+
+def forwarder(topo, src, dst):
+    near = topo.host(src) == topo.host(dst)
+    c = [k for k in topo.cores_of(src) if topo.may_write(k, dst) and (topo.die(k) == topo.die(src)) == near]
+    return c[0]
+
+
+def mask_of(engines):
+    return sum(1 << e for e in engines)
+
+
+def hand_on(g, core, T, topo):
+    for i, src in enumerate(T.cores):
+        for j, dst in enumerate(T.cores):
+            if i == j or topo.may_write(src, dst) or forwarder(topo, src, dst) != core:
+                continue
+            k = [r for r in range(N) if r != j].index(i)
+            rid, pid = topo.addr(dst, core)
+            e = topo.engines(core, dst)
+            s = T.sem
+            for sem, out, in_, to in (
+                    (s.f0, T.natl[k], T.fn[:], s.m0),
+                    (s.f1, T.ul[:, 8 * i:8 * i + 8], T.fu[:], s.m1),
+                    (s.f1c, T.cb[:, TX + CAP * k:TX + CAP * k + CAP].bitcast(dt.uint8), T.fc1[:].bitcast(dt.uint8), s.c1),
+                    (s.f1s, T.cbs[:, TX + CAP * k:TX + CAP * k + CAP], T.fs1[:], s.c1),
+                    (s.f2c, T.lc[:, 96 * k:96 * k + 96].bitcast(dt.uint8), T.fc2[:].bitcast(dt.uint8), s.c2),
+                    (s.f2s, T.ls[:, 96 * k:96 * k + 96], T.fs2[:], s.c2)):
+                g.wait_ge(sem, 4)
+                g.remote_dma(out, in_, to, s.loc, pid, rid, mask_of(e))
+            g.wait_ge(s.loc, 6 * len(e))
+
+
+def rank_program(g, core, T, topo):
+    me = T.rank_of(core)
+    if me is None:
+        hand_on(g, core, T, topo)
+        return
+    A, C = AluOpType, ActivationFunctionType
+    others = [r for r in range(N) if r != me]
+    s, v, a = T.sem, g.vector, g.scalar
+    cnt = {"v": 0, "a": 0, "t": 0}
+
+    def vec(f, *args, **kw):
+        if cnt["v"]:
+            v.wait_ge(s.sv, cnt["v"])
+        f(*args, **kw).then_inc(s.sv, 1)
+        cnt["v"] += 1
+        return cnt["v"]
+
+    def act(*args, **kw):
+        if cnt["a"]:
+            a.wait_ge(s.sa, cnt["a"])
+        a.activation(*args, **kw).then_inc(s.sa, 1)
+        cnt["a"] += 1
+        return cnt["a"]
+
+    def mm(*args):
+        if cnt["t"]:
+            g.tensor.wait_ge(s.st, cnt["t"])
+        g.tensor.matmul_mx(*args).then_inc(s.st, 1)
+        cnt["t"] += 1
+        return cnt["t"]
+
+    def ts(out, in_, s1, op0, s2=None, op1=None):
+        if op1 is None:
+            return vec(v.tensor_scalar, out, in_, s1, None, op0)
+        return vec(v.tensor_scalar, out, in_, s1, s2, op0, op1)
+
+    def tt(out, x, y, op):
+        return vec(v.tensor_tensor, out, x, y, op)
+
+    def cp(out, in_):
+        return vec(v.tensor_copy, out, in_)
+
+    ways, used = [], []
+    for k, r in enumerate(others):
+        d = T.cores[r]
+        if topo.may_write(core, d):
+            e = topo.engines(core, d)
+            used += e
+            ways.append((k, r, d, e, True))
+    rest = [k for k, r in enumerate(others) if not topo.may_write(core, T.cores[r])]
+    for n, k in enumerate(rest):
+        r = others[k]
+        d = forwarder(topo, core, T.cores[r])
+        e = [x for x in topo.engines(core, d) if x not in used]
+        h = len(e) // len(rest)
+        ways.append((k, r, d, e[n * h:n * h + h], False))
+
+    def send(src, far, near, far_sem, near_sem):
+        tr = []
+        for k, r, d, e, straight in ways:
+            rid, pid = topo.addr(d, core)
+            mine = [q for q in range(N) if q != r].index(me)
+            tr.append(RemoteDMATransfer(dst_ids=[DstId(rid=rid, pnc=pid)], dma_engine_mask=mask_of(e),
+                                        remote_sem=far_sem if straight else near_sem,
+                                        src=src(k), dst=far(mine) if straight else near))
+        g.remote_dma_fused(tr, local_sem=s.loc)
+
+    col = {}
+
+    def new(name):
+        col[name] = T.col[:, len(col):len(col) + 1]
+        return col[name]
+
+    g.iota(T.pi[:], [[0, 1]], 0, 1).then_inc(s.g0, 1)
+    g.iota(T.ic1[:], [[1, 256], [0, 2]], 1, 0, allow_small_or_imprecise_dtypes=True).then_inc(s.g1, 1)
+    g.iota(T.c0w[:], [[1, 8], [0, 2], [8, 32]], 0, 0, allow_small_or_imprecise_dtypes=True).then_inc(s.g2, 1)
+    g.iota(T.iob[:], [[32, 16]], 0, 0, allow_small_or_imprecise_dtypes=True).then_inc(s.g3, 1)
+    g.iota(T.iot[:], [[0, 4], [32, 4], [1, 16]], 1, 0, allow_small_or_imprecise_dtypes=True).then_inc(s.g4, 1)
+
+    for q in range(8):
+        g.sync.dma_start(T.stb[16 * q:16 * q + 16, 0:8], T.st[:]).then_inc(s.dsb, 16)
+        a.dma_start(T.stb[16 * q:16 * q + 16, 8:16], T.bt[:]).then_inc(s.dsb, 16)
+    k = vec(v.memset, T.p1w[:], 0)
+    for q in range(4):
+        e = g.sync if q % 2 else a
+        e.wait_ge(s.sv, k)
+        e.dma_start(T.p1w[32 * q:32 * q + 1, :], T.nx[:]).then_inc(s.dnx, 16)
+    a.dma_start(T.nat[:], T.nx[:]).then_inc(s.dnat, 16)
+    a.dma_start(T.xb[:], T.x[:]).then_inc(s.dx, 16)
+    g.sync.dma_start(T.nxs[0:16, :], T.nx[:]).then_inc(s.dns, 16)
+    g.sync.dma_start(T.nxs[16:32, :], T.nx[:]).then_inc(s.dns, 16)
+    g.sync.dma_start(T.wb[:], T.w[:]).then_inc(s.dw, 16)
+
+    vec(v.memset, T.zb[:], 0.0)
+    vec(v.memset, T.ones[:], 1.0)
+    vec(v.memset, T.w1[:], 0.0)
+    v.wait_ge(s.g0, 1)
+    ts(T.ic[:, 0:1], T.pi[:], 15, A.bitwise_and)
+    q16 = T.ic[:, 0:1]
+    ts(new("e3"), q16, 3.0, A.is_equal)
+    ts(new("e8"), q16, 8.0, A.is_equal)
+    for k in range(3):
+        kv = ts(new("v%d" % k), q16, 4.0 + k, A.is_equal, col["e3"], A.add)
+    ts(new("vme"), q16, 7.0, A.is_equal, col["e8"], A.add)
+    a.wait_ge(s.sv, kv)
+    for k in (0, 1):
+        kw = act(T.win2[:, 512 * others[k]:512 * others[k] + 512], T.zb[:], C.Identity, bias=col["v%d" % k])
+    ts(T.win2[:, 512 * others[2]:512 * others[2] + 512], T.zb[:], col["v2"], A.add)
+    ts(new("i9"), q16, 9.0, A.is_equal)
+    ts(new("t0"), q16, 7.0, A.is_equal, -272.0, A.mult)
+    ts(new("t1"), q16, 48.0, A.mult, -193.0, A.add)
+    tt(new("init1"), col["t0"], col["t1"], A.add)
+    v.wait_ge(s.g1, 1)
+    ts(T.win2[:, 512 * me:512 * me + 512], T.ic1[:], col["i9"], A.mult, col["vme"], A.add)
+    ts(T.ic[:, 1:2], T.pi[:], 31, A.bitwise_and)
+    cp(new("q32"), T.ic[:, 1:2])
+    v.wait_ge(s.g3, 1)
+    ts(T.offsel[:], T.iob[:], col["q32"], A.add)
+
+    v.wait_ge(s.dsb, 256)
+    ts(T.b0[:], T.stb[:, 8:16], 1, A.bitwise_and)
+    ts(T.sx[:], T.stb[:, 0:8], 513.0, A.mult)
+    ts(T.sy[:], T.b0[:], 256.0, A.mult)
+    tt(T.sz[:], T.sx[:], T.sy[:], A.add)
+    ts(T.sw[:], T.sz[:], 3, A.logical_shift_right, 511, A.bitwise_and)
+    kq = cp(T.q1l[:], T.sw[:])
+    ts(T.b1[:], T.stb[:, 8:16], 1, A.logical_shift_right)
+    a.wait_ge(s.sv, kq)
+    a.wait_ge(s.g2, 1)
+    act(T.c0l[:], T.c0w[:].indirect(T.q1l[:, 0:8]), C.Copy)
+    kvs1 = act(T.vs1[:], T.c0l[:].indirect(T.offsel[:, 0:4]), C.Copy)
+    v.wait_ge(s.dnx, 64)
+    ts(T.nl[:], T.p1w[:].indirect(T.q1l[:, 0:8]), 2.0, A.mult)
+    cp(T.nd[:, 0:16:2, :], T.nl[:])
+    cp(T.nd[:, 1:16:2, :], T.nl[:])
+    vec(v.transpose, T.tn[:], T.nd[:])
+    tt(T.uf[:], T.tn[:, :, 0], T.b1[:], A.add)
+    ku = cp(T.ul[:, 8 * me:8 * me + 8], T.uf[:])
+
+    g.wait_ge(s.dnat, 16)
+    send(lambda k: T.nat[:], lambda m: T.natl[m], T.fn[:], s.m0, s.f0)
+    g.wait_ge(s.sv, ku)
+    send(lambda k: T.ul[:, 8 * me:8 * me + 8], lambda m: T.ul[:, 8 * me:8 * me + 8], T.fu[:], s.m1, s.f1)
+
+    v.wait_ge(s.sa, kw)
+    cp(T.gs1[:, 0:128], T.win2[:].indirect(T.ul[:, 8 * me:8 * me + 8]))
+    vec(v.tensor_tensor_scan, T.gs1[:, 128:256], T.ones[:, 0:128], T.gs1[:, 0:128], col["init1"], A.mult, A.add)
+    vec(v.transpose, T.tg[:], T.gs1[:])
+    tt(T.x1[:], T.tg[:, 0:4, 4:8], T.tg[:, 4:8, 4:8], A.mult)
+    tt(T.x1b[:], T.x1[:, :, 0:2], T.x1[:, :, 2:4], A.add)
+    tt(T.x1c[:], T.x1b[:, :, 0], T.x1b[:, :, 1], A.add)
+    ts(T.off1[:], T.x1c[:], 128.0, A.add)
+    v.wait_ge(s.sa, kvs1)
+    cp(T.w1[:].indirect(T.off1[:, 0:4]), T.vs1[:])
+    cp(T.d1[:, 0:18:2, :], T.w1[:, 128:272])
+    cp(T.d1[:, 1:18:2, :], T.w1[:, 128:272])
+    vec(v.transpose, T.td1[:], T.d1[:])
+    tt(T.l1f[:], T.td1[:, :, 0], T.td1[:, :, 16], A.add)
+    v.wait_ge(s.dx, 16)
+    vec(v.quantize_mx, T.xq[:], T.xs[:], T.xb[:])
+    kl = cp(T.list1[:, 0:9], T.l1f[:])
+    a.wait_ge(s.sv, kl)
+    ksc = act(T.ps1[:], T.xs[:].indirect(T.list1[:, 0:9]), C.Copy)
+    kpk = cp(T.pk1[:].bitcast(dt.uint32), T.xq[:].bitcast(dt.uint32).indirect(T.list1[:, 0:9]))
+    g.wait_ge(s.sv, kpk)
+    send(lambda k: T.pk1[:, CAP * k:CAP * k + CAP].bitcast(dt.uint8), lambda m: T.cb[:, TX + CAP * m:TX + CAP * m + CAP].bitcast(dt.uint8),
+         T.fc1[:].bitcast(dt.uint8), s.c1, s.f1c)
+    g.wait_ge(s.sa, ksc)
+    send(lambda k: T.ps1[:, CAP * k:CAP * k + CAP], lambda m: T.cbs[:, TX + CAP * m:TX + CAP * m + CAP], T.fs1[:], s.c1, s.f1s)
+    g.iota(T.p3w[:], [[0, 2048]], 0, 0).then_inc(s.g5, 1)
+
+    v.wait_ge(s.dns, 32)
+    vec(v.transpose, T.nxt[0:32, :], T.nxs[0:32, :])
+    ts(T.nxr[0:32, :], T.nxt[0:32, 0:16], 8, A.logical_shift_right)
+    for r in range(4):
+        km = ts(T.mk[0:32, 16 * r:16 * r + 16], T.nxr[0:32, :], float(others[r] if r < 3 else me), A.is_equal)
+    g.sync.wait_ge(s.sv, km)
+    for b in range(4):
+        for r in range(4):
+            g.sync.dma_start(T.win2[32 * b + r:32 * b + r + 1, 512 * me:512 * me + 512], T.mk[0:32, 16 * r:16 * r + 16]).then_inc(s.dmk, 16)
+    g.sync.wait_ge(s.g5, 1)
+    for b in range(4):
+        for r in (12, 28):
+            g.sync.dma_start(T.p3w[32 * b + r:32 * b + r + 1, 512 * me:512 * me + 512], T.nx[:]).then_inc(s.down, 16)
+    g.sync.wait_ge(s.m0, 24)
+    for k, r in enumerate(others):
+        for b in range(4):
+            for p in (12, 28):
+                g.sync.dma_start(T.p3w[32 * b + p:32 * b + p + 1, 512 * r:512 * r + 512], T.natl[k]).then_inc(s.drem, 16)
+
+    ts(new("l2"), q16, 2.0, A.is_le)
+    kd = tt(new("keep"), col["l2"], col["e8"], A.add)
+    ts(new("init2"), q16, 48.0, A.mult, -1.0, A.add)
+    ts(new("i10"), q16, 10.0, A.is_equal)
+    for r in range(N):
+        ts(new("s%d" % r), q16, 13.0, A.is_equal, r + 1.0, A.mult)
+        if r != me:
+            ts(new("k%d" % r), q16, 10.0, A.is_equal, float(TX + CAP * others.index(r)), A.mult)
+            tt(new("b%d" % r), col["k%d" % r], col["s%d" % r], A.add)
+    ts(new("q16m"), q16, 1.0, A.mult, -256.0, A.add)
+    ts(T.trc[:], T.iob[:], 0.5, A.mult, col["q16m"], A.add)
+    ts(T.c0m[:], T.vs1[:], col["i10"], A.mult, col["s%d" % me], A.add)
+    a.wait_ge(s.sv, kd)
+    for r in range(N):
+        act(T.data0[:, 128 * r:128 * r + 128], T.zb[:, 0:128], C.Identity, bias=col["l2"] if r == me else col["keep"])
+    act(T.data0[:, 0:512:128], T.zb[:, 0:4], C.Identity, bias=col["l2"])
+    act(T.w2[:], T.zb[:, 0:400], C.Copy)
+    kw2 = act(T.w3[:], T.zb[:, 0:448], C.Copy)
+    vec(v.quantize_mx, T.cb[:, 0:TX], T.cbs[:, 0:TX], T.xb[:])
+
+    v.wait_ge(s.m1, 24)
+    v.wait_ge(s.dmk, 256)
+    v.wait_ge(s.sa, kw2)
+    cp(T.g2[:], T.win2[:].indirect(T.ul[:, 0:32]))
+    ks2 = vec(v.tensor_tensor_scan, T.s2[:], T.data0[:], T.g2[:], col["init2"], A.mult, A.add)
+    a.wait_ge(s.sv, ks2)
+    for r in others:
+        kvsel = act(T.vsel[:, 64 * r:64 * r + 64], T.s2[:].indirect(T.offsel[:, 4 * r:4 * r + 4]), C.Identity, bias=col["b%d" % r])
+    vec(v.transpose, T.tm[:], T.g2[:])
+    vec(v.transpose, T.ts[:], T.s2[:])
+    tt(T.x2[:, :, 3], T.tm[:, :, 3], T.trc[:], A.mult)
+    tt(T.x2[:, :, 0:3], T.tm[:, :, 0:3], T.ts[:, :, 0:3], A.mult)
+    tt(T.x2b[:], T.x2[:, :, 0:2], T.x2[:, :, 2:4], A.add)
+    tt(T.x2c[:], T.x2b[:, :, 0], T.x2b[:, :, 1], A.add)
+    ts(T.off2[:], T.x2c[:], 256.0, A.add)
+    tt(T.vsel[:, 64 * me:64 * me + 64], T.s2[:].indirect(T.offsel[:, 4 * me:4 * me + 4]), T.c0m[:], A.add)
+    v.wait_ge(s.sa, kvsel)
+    cp(T.w2[:].indirect(T.off2[:, 0:16]), T.vsel[:])
+    cp(T.d2[:, 0:18:2, :], T.w2[:, 256:400])
+    cp(T.d2[:, 1:18:2, :], T.w2[:, 256:400])
+    vec(v.transpose, T.td2[:], T.d2[:])
+    tt(T.h2[:], T.td2[:, :, 8:12], T.td2[:, :, 24:28], A.add)
+    tt(T.nf[:, :, 0, :], T.h2[:, :, :, 0], T.h2[:, :, :, 2], A.add)
+    tt(T.nf[:, :, 1, :], T.h2[:, :, :, 1], T.h2[:, :, :, 3], A.add)
+    kl2 = ts(T.list2[:], T.nf[:], -1.0, A.add)
+    a.wait_ge(s.sv, kl2)
+    a.wait_ge(s.c1, 48)
+    ksc2 = act(T.ps2[:], T.cbs[:].indirect(T.list2[:, 0:18]), C.Copy)
+    v.wait_ge(s.c1, 48)
+    kpk2 = cp(T.pk2[:].bitcast(dt.uint32), T.cb[:].bitcast(dt.uint32).indirect(T.list2[:, 0:18]))
+    g.wait_ge(s.sv, kpk2)
+    send(lambda k: T.pk2[:, 96 * k:96 * k + 96].bitcast(dt.uint8), lambda m: T.lc[:, 96 * m:96 * m + 96].bitcast(dt.uint8),
+         T.fc2[:].bitcast(dt.uint8), s.c2, s.f2c)
+    g.wait_ge(s.sa, ksc2)
+    send(lambda k: T.ps2[:, 96 * k:96 * k + 96], lambda m: T.ls[:, 96 * m:96 * m + 96], T.fs2[:], s.c2, s.f2s)
+
+    v.wait_ge(s.dw, 16)
+    kwq = vec(v.quantize_mx, T.wq[:], T.ws[:], T.wb[:])
+
+    def w(k):
+        return T.wq[:, 128 * k:128 * k + 128], T.ws[:, 128 * k:128 * k + 128]
+    g.tensor.wait_ge(s.sv, kwq)
+    mm(T.ps[:, 512:768], *w(1), T.xq[:], T.xs[:], True, True)
+    mm(T.ps[:, 1024:1280], *w(2), T.xq[:], T.xs[:], True, True)
+    g.tensor.wait_ge(s.c1, 48)
+    m0 = mm(T.ps[:, 0:400], *w(0), T.cb[:], T.cbs[:], True, True)
+    a.wait_ge(s.st, m0)
+    act(T.aw[:, 1:401], T.ps[:, 0:400], C.Copy)
+    act(T.bw[:, 1:257], T.ps[:, 512:768], C.Copy)
+    kaw = act(T.cw[:, 1:257], T.ps[:, 1024:1280], C.Copy)
+
+    ts(T.ic[:, 2:3], T.pi[:], 16, A.bitwise_and)
+    ts(new("o16"), T.ic[:, 2:3], 1.0, A.mult)
+    ts(new("i14"), q16, 14.0, A.is_equal)
+    ts(new("i12"), q16, 12.0, A.is_equal)
+    ts(new("kic"), col["i14"], col["o16"], A.mult, col["i12"], A.add)
+    v.wait_ge(s.g4, 1)
+    ts(T.ki[:], T.iot[:], col["i14"], A.mult, col["kic"], A.add)
+    tt(T.vselk[:], T.vsel[:], T.ki[:], A.add)
+    cp(T.ui[:], T.ul[:])
+    ts(T.ua[:], T.ui[:], 511, A.bitwise_and)
+    tt(T.ui[:], T.ui[:], T.ua[:], A.subtract)
+    ts(T.uc[:], T.ua[:], 513.0, A.mult)
+    ts(T.ua[:], T.uc[:], 4, A.logical_shift_right, 511, A.bitwise_and)
+    tt(T.uc[:], T.ui[:], T.ua[:], A.add)
+    cp(T.u3[:], T.uc[:])
+    ts(T.ac[:], T.trc[:], -1.0, A.mult, -1.0, A.add)
+    vec(v.memset, T.c3[:], 0.0)
+    vec(v.memset, T.aw[:, 0:1], 0.0)
+    vec(v.memset, T.bw[:, 0:1], 0.0)
+    vec(v.memset, T.cw[:, 0:1], 0.0)
+    for k in range(3):
+        vec(v.memset, T.kc[:, :, k], 400.0 + 96.0 * k)
+    v.wait_ge(s.down, 128)
+    v.wait_ge(s.drem, 384)
+    cp(T.n2[:], T.p3w[:].indirect(T.u3[:, 0:32]))
+    ts(T.r3[:], T.n2[:], 8, A.logical_shift_right)
+    ts(T.m3[:], T.r3[:], float(me), A.is_equal)
+    vec(v.tensor_tensor_scan, T.s3[:], T.ones[:], T.m3[:], 0.0, A.mult, A.add)
+    vec(v.transpose, T.tm3[:], T.m3[:])
+    vec(v.transpose, T.ts3[:], T.s3[:])
+    tt(T.v3[:], T.ts3[:, :, 12], T.ac[:], A.add)
+    tt(T.v3[:], T.v3[:], T.tm3[:, :, 12], A.mult)
+    tt(T.v3[:], T.v3[:], T.trc[:], A.add)
+    ts(T.off3[:], T.v3[:], 256.0, A.add)
+    cp(T.c2s[:], T.n2[:].indirect(T.offsel[:, 0:16]))
+    ts(T.c2a[:], T.c2s[:], 255, A.bitwise_and)
+    tt(T.val3[:], T.vselk[:], T.c2a[:], A.add)
+    cp(T.w3[:].indirect(T.off3[:, 0:16]), T.val3[:])
+    vec(v.transpose, T.t3[:], T.w3[:, 256:448])
+    tt(T.c3[:, :, 0:16], T.t3[:, :, 0:16], T.t3[:, :, 16:32], A.add)
+    vec(v.transpose, T.pl[:], T.c3[:])
+    ki = ts(T.idl[:], T.pl[:], -1.0, A.add)
+    g.sync.wait_ge(s.sv, ki)
+    g.sync.dma_start(T.id[0:1, :], T.idl[13:14, :]).then_inc(s.did, 16)
+    g.sync.dma_start(T.id[1:2, :], T.idl[14:15, :]).then_inc(s.did, 16)
+    vec(v.tensor_tensor_scan, T.sc[:], T.ones[:, 0:192], T.pl[:], 0.0, A.mult, A.add)
+    for d, x, t in ((T.dp, T.pl, T.tp), (T.ds, T.sc, T.tc)):
+        cp(d[:, 0:24:2, :], x[:])
+        cp(d[:, 1:24:2, :], x[:])
+        vec(v.transpose, t[:], d[:])
+    tt(T.x3[:, :, 0:3], T.tc[:, :, 4:7], T.kc[:], A.add)
+    tt(T.x3[:, :, 3:5], T.tp[:, :, 8:10], T.tp[:, :, 10:12], A.add)
+    tt(T.x3[:, :, 0:4], T.x3[:, :, 0:4], T.tp[:, :, 4:8], A.mult)
+    tt(T.x3b[:], T.x3[:, :, 0:2], T.x3[:, :, 2:4], A.add)
+    tt(T.x3c[:], T.x3b[:, :, 0], T.x3b[:, :, 1], A.add)
+    cp(T.q0[:], T.x3c[:])
+    cp(T.qb[:], T.x3[:, :, 4])
+    cp(T.qc[:], T.tp[:, :, 12])
+    v.wait_ge(s.sa, kaw)
+    cp(T.t1[:], T.cw[:, 0:257].indirect(T.qc[:, 0:12]))
+    tt(T.t2[:], T.bw[:, 0:257].indirect(T.qb[:, 0:12]), T.t1[:], A.add)
+
+    g.tensor.wait_ge(s.c2, 48)
+    mm(T.ps[:, 1536:1776], *w(0), T.lc[:, 0:240], T.ls[:, 0:240], True, False)
+    m3 = mm(T.ps[:, 1536:1776], *w(1), T.lc[:, 48:288], T.ls[:, 48:288], False, True)
+    v.wait_ge(s.st, m3)
+    cp(T.aw[:, 401:641], T.ps[:, 1536:1776])
+    ky = tt(T.yo[:], T.aw[:, 0:641].indirect(T.q0[:, 0:12]), T.t2[:], A.add)
+    g.sync.wait_ge(s.sv, ky)
+    g.sync.dma_start(T.y[:], T.yo[:]).then_inc(s.dy, 16)
+
+    g.wait_ge(s.dy, 16)
+    g.wait_ge(s.did, 32)
+    g.wait_ge(s.sa, cnt["a"])
+    g.wait_ge(s.st, cnt["t"])
+    g.wait_ge(s.loc, 6 * sum(len(x[3]) for x in ways))

@@ -1,7 +1,7 @@
 from concourse.bass import DstId, RemoteDMATransfer
 from concourse.mybir import dt, AluOpType, ActivationFunctionType
 
-N, V, M, CAP, TX = 4, 128, 192, 48, 256
+N, CAP, TX = 4, 48, 256
 F, B, I, U = "float32", "bfloat16", "int32", "uint16"
 CODE, PLANE = "float8_e4m3fn_x4", "uint8"
 
@@ -12,48 +12,41 @@ def _sb(d, *s):
 
 SCRATCH = {
     "xb": _sb(B, 1024), "wb": _sb(B, 1536),
-    "xq": _sb(CODE, 256), "xs": _sb(PLANE, 256),
-    "cb": _sb(CODE, 400), "cbs": _sb(PLANE, 400),
-    "wq": _sb(CODE, 384), "ws": _sb(PLANE, 384),
-    "pk1": _sb(CODE, 144), "ps1": _sb(PLANE, 144),
-    "pk2": _sb(CODE, 288), "ps2": _sb(PLANE, 288),
+    "xq": _sb(CODE, 256), "xs": _sb(PLANE, 256), "cb": _sb(CODE, 400), "cbs": _sb(PLANE, 400), "wq": _sb(CODE, 384), "ws": _sb(PLANE, 384),
+    "pk1": _sb(CODE, 144), "ps1": _sb(PLANE, 144), "pk2": _sb(CODE, 288), "ps2": _sb(PLANE, 288),
     "fc1": _sb(CODE, 48), "fs1": _sb(PLANE, 48), "fc2": _sb(CODE, 96), "fs2": _sb(PLANE, 96),
-    "fu": _sb(U, 8), "fn": ("dram", [128, 4], I),
-    "lc": _sb(CODE, 288), "ls": _sb(PLANE, 288),
-    "nat": ("dram", [128, 4], I), "natl": ("dram", [3, 128, 4], I),
-    "pi": _sb(I, 1), "ic": _sb(I, 4), "col": _sb(F, 32), "iob": _sb(F, 16),
+    "fu": _sb(U, 8), "fn": ("dram", [128, 2], I), "lc": _sb(CODE, 288), "ls": _sb(PLANE, 288), "natl": ("dram", [8, 128, 2], I),
+    "pi": _sb(I, 1), "ic": _sb(I, 2), "col": _sb(F, 48), "iob": _sb(F, 16), "io16": _sb(F, 16), "eq": _sb(F, 16),
     "c0w": _sb(B, 512), "ic1": _sb(B, 512), "iot": _sb(B, 256),
-    "zb": _sb(B, 512), "ones": _sb(B, 512), "offsel": _sb(U, 16), "trc": _sb(F, 16), "ac": _sb(F, 16),
-    "data0": _sb(B, 512), "ki": _sb(B, 256), "kc": _sb(F, 12, 3),
+    "zb": _sb(B, 512), "ones": _sb(B, 128), "offsel": _sb(U, 16), "trc": _sb(F, 16), "ac": _sb(F, 16),
+    "data0": _sb(B, 512), "data3": _sb(B, 512), "ki": _sb(B, 256), "kc": _sb(F, 12, 3),
     "stb": _sb(I, 16), "b0": _sb(I, 8), "b1": _sb(I, 8), "sx": _sb(I, 8), "sy": _sb(I, 8), "sz": _sb(I, 8), "sw": _sb(I, 8),
     "q1l": _sb(U, 8), "p1w": _sb(I, 512), "nl": _sb(F, 128), "nd": _sb(F, 16, 16), "tn": _sb(F, 8, 32), "uf": _sb(F, 8),
     "ul": _sb(U, 32), "win2": _sb(B, 2048), "gs1": _sb(B, 256), "tg": _sb(B, 8, 32),
     "x1": _sb(F, 4, 4), "x1b": _sb(F, 4, 2), "x1c": _sb(F, 4), "off1": _sb(U, 4),
     "c0l": _sb(B, 128), "vs1": _sb(B, 64), "c0m": _sb(B, 64), "w1": _sb(B, 272),
     "d1": _sb(B, 18, 16), "td1": _sb(B, 9, 32), "l1f": _sb(F, 9), "list1": _sb(U, 10),
-    "nxs": _sb(I, 32), "nxt": _sb(I, 32), "nxr": _sb(I, 16), "mk": _sb(B, 64),
-    "g2": _sb(B, 512), "s2": _sb(B, 512), "tm": _sb(B, 16, 32), "ts": _sb(B, 16, 32),
+    "nxs": _sb(I, 32), "nxt": _sb(I, 32), "nxr": _sb(I, 16), "mk": _sb(B, 16),
+    "gs2": _sb(B, 1024), "tg2": _sb(B, 32, 32),
     "x2": _sb(F, 16, 4), "x2b": _sb(F, 16, 2), "x2c": _sb(F, 16), "off2": _sb(U, 16),
     "vsel": _sb(B, 256), "w2": _sb(B, 400), "d2": _sb(B, 18, 16), "td2": _sb(B, 9, 32),
     "h2": _sb(F, 3, 3, 4), "nf": _sb(F, 3, 2, 3), "list2": _sb(U, 18),
-    "ui": _sb(I, 32), "ua": _sb(I, 32), "uc": _sb(I, 32), "u3": _sb(U, 32),
-    "p3w": _sb(I, 2048), "n2": _sb(I, 512), "r3": _sb(I, 512), "m3": _sb(B, 512), "s3": _sb(B, 512),
-    "tm3": _sb(B, 16, 32), "ts3": _sb(B, 16, 32), "v3": _sb(F, 16), "off3": _sb(U, 16),
-    "c2s": _sb(I, 256), "c2a": _sb(I, 256), "vselk": _sb(B, 256), "val3": _sb(B, 256), "w3": _sb(B, 448),
-    "t3": _sb(B, 6, 32), "c3": _sb(B, 6, 32), "pl": _sb(B, 192), "sc": _sb(B, 192), "idl": _sb(F, 192),
-    "dp": _sb(B, 24, 16), "ds": _sb(B, 24, 16), "tp": _sb(B, 12, 32), "tc": _sb(B, 12, 32),
-    "x3": _sb(F, 12, 5), "x3b": _sb(F, 12, 2), "x3c": _sb(F, 12), "q0": _sb(U, 12), "qb": _sb(U, 12), "qc": _sb(U, 12),
+    "nx4": _sb(I, 32), "nt4": _sb(I, 32), "r4": _sb(I, 16), "c4": _sb(I, 16), "mp": _sb(B, 16), "cp4": _sb(B, 16),
+    "p3w": _sb(B, 2048), "gs3": _sb(B, 1024), "tg3": _sb(B, 32, 32), "va": _sb(F, 16), "vb": _sb(F, 16), "vc": _sb(F, 16), "off3": _sb(U, 16),
+    "vsk": _sb(B, 256), "vselk": _sb(B, 256), "val3": _sb(B, 256), "w3": _sb(B, 448),
+    "t3": _sb(B, 6, 32), "c3": _sb(B, 6, 32), "pl": _sb(B, 192), "idl": _sb(F, 192),
+    "dp": _sb(B, 24, 16), "tp": _sb(B, 12, 32), "yy": _sb(F, 12, 15),
+    "x3": _sb(F, 12, 4), "x3m": _sb(F, 12, 4), "x3b": _sb(F, 12, 2), "x3c": _sb(F, 12), "q0": _sb(U, 12), "qb": _sb(U, 12), "qc": _sb(U, 12),
     "ps": ("psum", [128, 2048], F), "aw": _sb(F, 648), "bw": _sb(F, 264), "cw": _sb(F, 264),
     "t1": _sb(F, 192), "t2": _sb(F, 192), "yo": _sb(F, 192),
 }
-SEMAPHORES = ["sv", "sa", "st", "g0", "g1", "g2", "g3", "g4", "g5", "dsb", "dnx", "dns", "dx", "dw", "dnat", "dmk", "down", "drem", "dy", "did",
+SEMAPHORES = ["sv", "sa", "st", "g0", "g1", "g2", "g3", "g4", "dsb", "dnx", "dns", "dn4", "dx", "dw", "dnat", "dmk", "drow", "dy", "did",
               "m0", "m1", "c1", "c2", "loc", "f0", "f1", "f1c", "f1s", "f2c", "f2s"]
 
 
-def forwarder(topo, src, dst):
+def forwarders(topo, src, dst):
     near = topo.host(src) == topo.host(dst)
-    c = [k for k in topo.cores_of(src) if topo.may_write(k, dst) and (topo.die(k) == topo.die(src)) == near]
-    return c[0]
+    return [k for k in topo.cores_of(src) if topo.may_write(k, dst) and (topo.die(k) == topo.die(src)) == near][:2]
 
 
 def mask_of(engines):
@@ -63,22 +56,25 @@ def mask_of(engines):
 def hand_on(g, core, T, topo):
     for i, src in enumerate(T.cores):
         for j, dst in enumerate(T.cores):
-            if i == j or topo.may_write(src, dst) or forwarder(topo, src, dst) != core:
+            if i == j or topo.may_write(src, dst) or core not in forwarders(topo, src, dst):
                 continue
+            h = forwarders(topo, src, dst).index(core)
             k = [r for r in range(N) if r != j].index(i)
             rid, pid = topo.addr(dst, core)
             e = topo.engines(core, dst)
             s = T.sem
-            for sem, out, in_, to in (
-                    (s.f0, T.natl[k], T.fn[:], s.m0),
-                    (s.f1, T.ul[:, 8 * i:8 * i + 8], T.fu[:], s.m1),
-                    (s.f1c, T.cb[:, TX + CAP * k:TX + CAP * k + CAP].bitcast(dt.uint8), T.fc1[:].bitcast(dt.uint8), s.c1),
-                    (s.f1s, T.cbs[:, TX + CAP * k:TX + CAP * k + CAP], T.fs1[:], s.c1),
-                    (s.f2c, T.lc[:, 96 * k:96 * k + 96].bitcast(dt.uint8), T.fc2[:].bitcast(dt.uint8), s.c2),
-                    (s.f2s, T.ls[:, 96 * k:96 * k + 96], T.fs2[:], s.c2)):
-                g.wait_ge(sem, 4)
+            jobs = [(s.f0, 4, T.natl[2 * i + h], T.fn[:], s.m0)]
+            if h:
+                jobs += [(s.f1, 8, T.ul[:, 8 * i:8 * i + 8], T.fu[:], s.m1),
+                         (s.f1s, 8, T.cbs[:, TX + CAP * k:TX + CAP * k + CAP], T.fs1[:], s.c1),
+                         (s.f2s, 8, T.ls[:, 96 * k:96 * k + 96], T.fs2[:], s.c2)]
+            else:
+                jobs += [(s.f1c, 8, T.cb[:, TX + CAP * k:TX + CAP * k + CAP].bitcast(dt.uint8), T.fc1[:].bitcast(dt.uint8), s.c1),
+                         (s.f2c, 8, T.lc[:, 96 * k:96 * k + 96].bitcast(dt.uint8), T.fc2[:].bitcast(dt.uint8), s.c2)]
+            for sem, n, out, in_, to in jobs:
+                g.wait_ge(sem, n)
                 g.remote_dma(out, in_, to, s.loc, pid, rid, mask_of(e))
-            g.wait_ge(s.loc, 6 * len(e))
+            g.wait_ge(s.loc, len(jobs) * len(e))
 
 
 def rank_program(g, core, T, topo):
@@ -89,19 +85,19 @@ def rank_program(g, core, T, topo):
     A, C = AluOpType, ActivationFunctionType
     others = [r for r in range(N) if r != me]
     s, v, a = T.sem, g.vector, g.scalar
-    cnt = {"v": 0, "a": 0, "t": 0}
+    cnt = {"v": 0, "a": 0, "t": 0, "loc": 0}
 
-    def vec(f, *args, **kw):
-        if cnt["v"]:
+    def vec(f, *args, free=False):
+        if cnt["v"] and not free:
             v.wait_ge(s.sv, cnt["v"])
-        f(*args, **kw).then_inc(s.sv, 1)
+        f(*args).then_inc(s.sv, 1)
         cnt["v"] += 1
         return cnt["v"]
 
-    def act(*args, **kw):
-        if cnt["a"]:
+    def act(out, in_, func=C.Identity, free=False, **kw):
+        if cnt["a"] and not free:
             a.wait_ge(s.sa, cnt["a"])
-        a.activation(*args, **kw).then_inc(s.sa, 1)
+        a.activation(out, in_, func, **kw).then_inc(s.sa, 1)
         cnt["a"] += 1
         return cnt["a"]
 
@@ -112,102 +108,113 @@ def rank_program(g, core, T, topo):
         cnt["t"] += 1
         return cnt["t"]
 
-    def ts(out, in_, s1, op0, s2=None, op1=None):
+    def ts(out, in_, s1, op0, s2=None, op1=None, free=False):
         if op1 is None:
-            return vec(v.tensor_scalar, out, in_, s1, None, op0)
-        return vec(v.tensor_scalar, out, in_, s1, s2, op0, op1)
+            return vec(v.tensor_scalar, out, in_, s1, None, op0, free=free)
+        return vec(v.tensor_scalar, out, in_, s1, s2, op0, op1, free=free)
 
-    def tt(out, x, y, op):
-        return vec(v.tensor_tensor, out, x, y, op)
+    def tt(out, x, y, op, free=False):
+        return vec(v.tensor_tensor, out, x, y, op, free=free)
 
-    def cp(out, in_):
-        return vec(v.tensor_copy, out, in_)
+    def cp(out, in_, free=False):
+        return vec(v.tensor_copy, out, in_, free=free)
 
-    ways, used = [], []
-    for k, r in enumerate(others):
-        d = T.cores[r]
-        if topo.may_write(core, d):
-            e = topo.engines(core, d)
-            used += e
-            ways.append((k, r, d, e, True))
+    def fill(out, x, free=True):
+        return vec(v.memset, out, x, free=free)
+
     rest = [k for k, r in enumerate(others) if not topo.may_write(core, T.cores[r])]
-    for n, k in enumerate(rest):
-        r = others[k]
-        d = forwarder(topo, core, T.cores[r])
-        e = [x for x in topo.engines(core, d) if x not in used]
-        h = len(e) // len(rest)
-        ways.append((k, r, d, e[n * h:n * h + h], False))
+    peer = [k for k in range(N - 1) if k not in rest]
 
-    def send(src, far, near, far_sem, near_sem):
+    def call(items):
         tr = []
-        for k, r, d, e, straight in ways:
+        for d, n, of, sem, src, dst in items:
+            e = topo.engines(core, d)
+            h = len(e) // of
             rid, pid = topo.addr(d, core)
-            mine = [q for q in range(N) if q != r].index(me)
-            tr.append(RemoteDMATransfer(dst_ids=[DstId(rid=rid, pnc=pid)], dma_engine_mask=mask_of(e),
-                                        remote_sem=far_sem if straight else near_sem,
-                                        src=src(k), dst=far(mine) if straight else near))
+            tr.append(RemoteDMATransfer(dst_ids=[DstId(rid=rid, pnc=pid)], dma_engine_mask=mask_of(e[n * h:n * h + h]), remote_sem=sem, src=src, dst=dst))
+            cnt["loc"] += h
         g.remote_dma_fused(tr, local_sem=s.loc)
+
+    def send(h, src, far, near, far_sem, near_sem):
+        call([(forwarders(topo, core, T.cores[others[k]])[h], n, len(rest), near_sem, src(k), near) for n, k in enumerate(rest)])
+        for k in peer:
+            mine = [q for q in range(N) if q != others[k]].index(me)
+            call([(T.cores[others[k]], 0, 1, far_sem, src(k), far(mine))])
 
     col = {}
 
-    def new(name):
-        col[name] = T.col[:, len(col):len(col) + 1]
-        return col[name]
+    def new(name, n=1):
+        assert name not in col
+        at = sum(col[k][1] for k in col)
+        col[name] = (T.col[:, at:at + n], n)
+        return col[name][0]
 
-    g.iota(T.pi[:], [[0, 1]], 0, 1).then_inc(s.g0, 1)
-    g.iota(T.ic1[:], [[1, 256], [0, 2]], 1, 0, allow_small_or_imprecise_dtypes=True).then_inc(s.g1, 1)
-    g.iota(T.c0w[:], [[1, 8], [0, 2], [8, 32]], 0, 0, allow_small_or_imprecise_dtypes=True).then_inc(s.g2, 1)
-    g.iota(T.iob[:], [[32, 16]], 0, 0, allow_small_or_imprecise_dtypes=True).then_inc(s.g3, 1)
-    g.iota(T.iot[:], [[0, 4], [32, 4], [1, 16]], 1, 0, allow_small_or_imprecise_dtypes=True).then_inc(s.g4, 1)
+    def c(name):
+        return col[name][0]
 
+    def eq(r, n=1):
+        return T.eq[:, r:r + n]
+
+    g.sync.dma_start(T.natl[2 * me:2 * me + 2], T.nx[:]).then_inc(s.dnat, 16)
     for q in range(8):
         g.sync.dma_start(T.stb[16 * q:16 * q + 16, 0:8], T.st[:]).then_inc(s.dsb, 16)
         a.dma_start(T.stb[16 * q:16 * q + 16, 8:16], T.bt[:]).then_inc(s.dsb, 16)
-    k = vec(v.memset, T.p1w[:], 0)
+    k = fill(T.p1w[:], 0)
     for q in range(4):
         e = g.sync if q % 2 else a
         e.wait_ge(s.sv, k)
         e.dma_start(T.p1w[32 * q:32 * q + 1, :], T.nx[:]).then_inc(s.dnx, 16)
-    a.dma_start(T.nat[:], T.nx[:]).then_inc(s.dnat, 16)
     a.dma_start(T.xb[:], T.x[:]).then_inc(s.dx, 16)
-    g.sync.dma_start(T.nxs[0:16, :], T.nx[:]).then_inc(s.dns, 16)
-    g.sync.dma_start(T.nxs[16:32, :], T.nx[:]).then_inc(s.dns, 16)
+    fill(T.nxs[:], 0, free=False)
+    k = fill(T.nx4[:], 0)
+    g.sync.wait_ge(s.sv, k)
+    for q in range(4):
+        g.sync.dma_start(T.nxs[32 * q:32 * q + 16, :], T.nx[:]).then_inc(s.dns, 16)
+    g.sync.dma_start(T.nx4[32 * me:32 * me + 16, :], T.nx[:]).then_inc(s.dn4, 16)
     g.sync.dma_start(T.wb[:], T.w[:]).then_inc(s.dw, 16)
 
-    vec(v.memset, T.zb[:], 0.0)
-    vec(v.memset, T.ones[:], 1.0)
-    vec(v.memset, T.w1[:], 0.0)
+    def iota(out, pattern, base, mult, sem):
+        g.iota(out, pattern, base, mult, allow_small_or_imprecise_dtypes=True).then_inc(sem, 1)
+    g.iota(T.pi[:], [[0, 1]], 0, 1).then_inc(s.g0, 1)
+    iota(T.io16[:], [[1, 16]], 0, 0, s.g3)
+    iota(T.iob[:], [[32, 16]], 0, 0, s.g3)
+    iota(T.c0w[:], [[1, 8], [0, 2], [8, 32]], 0, 0, s.g2)
+    g.wait_ge(s.dnat, 16)
+    call([(forwarders(topo, core, T.cores[others[k]])[h], 2 * n + h, 2 * len(rest), s.f0, T.natl[2 * me + h], T.fn[:])
+          for n, k in enumerate(rest) for h in (0, 1)])
+    for k in peer:
+        call([(T.cores[others[k]], h, 2, s.m0, T.natl[2 * me + h], T.natl[2 * me + h]) for h in (0, 1)])
+    iota(T.ic1[:], [[1, 256], [0, 2]], 1, 0, s.g1)
+
+    fill(T.zb[:], 0.0, free=False)
     v.wait_ge(s.g0, 1)
     ts(T.ic[:, 0:1], T.pi[:], 15, A.bitwise_and)
-    q16 = T.ic[:, 0:1]
-    ts(new("e3"), q16, 3.0, A.is_equal)
-    ts(new("e8"), q16, 8.0, A.is_equal)
+    ts(T.ic[:, 1:2], T.pi[:], 31, A.bitwise_and, free=True)
+    cp(new("q", 2), T.ic[:])
+    q16, q32 = T.col[:, 0:1], T.col[:, 1:2]
+    v.wait_ge(s.g3, 2)
+    ke = ts(T.eq[:], T.io16[:], q16, A.is_equal)
+    ts(T.offsel[:], T.iob[:], q32, A.add)
+    fill(T.ones[:], 1.0)
+    fill(T.w1[:], 0.0)
+    a.wait_ge(s.sv, ke)
+    act(new("v", 3), eq(4, 3), bias=eq(3))
+    act(new("vme"), eq(7), bias=eq(8), free=True)
+    act(new("u1"), q16, scale=48.0, bias=-193.0, free=True)
+    act(new("init1"), eq(7), scale=-272.0, bias=c("u1"))
     for k in range(3):
-        kv = ts(new("v%d" % k), q16, 4.0 + k, A.is_equal, col["e3"], A.add)
-    ts(new("vme"), q16, 7.0, A.is_equal, col["e8"], A.add)
-    a.wait_ge(s.sv, kv)
-    for k in (0, 1):
-        kw = act(T.win2[:, 512 * others[k]:512 * others[k] + 512], T.zb[:], C.Identity, bias=col["v%d" % k])
-    ts(T.win2[:, 512 * others[2]:512 * others[2] + 512], T.zb[:], col["v2"], A.add)
-    ts(new("i9"), q16, 9.0, A.is_equal)
-    ts(new("t0"), q16, 7.0, A.is_equal, -272.0, A.mult)
-    ts(new("t1"), q16, 48.0, A.mult, -193.0, A.add)
-    tt(new("init1"), col["t0"], col["t1"], A.add)
-    v.wait_ge(s.g1, 1)
-    ts(T.win2[:, 512 * me:512 * me + 512], T.ic1[:], col["i9"], A.mult, col["vme"], A.add)
-    ts(T.ic[:, 1:2], T.pi[:], 31, A.bitwise_and)
-    cp(new("q32"), T.ic[:, 1:2])
-    v.wait_ge(s.g3, 1)
-    ts(T.offsel[:], T.iob[:], col["q32"], A.add)
+        act(T.win2[:, 512 * others[k]:512 * others[k] + 512], T.zb[:], bias=T.col[:, 2 + k:3 + k], free=True)
+    a.wait_ge(s.g1, 1)
+    kw = act(T.win2[:, 512 * me:512 * me + 512], T.ic1[:], scale=eq(9), bias=c("vme"), free=True)
 
     v.wait_ge(s.dsb, 256)
     ts(T.b0[:], T.stb[:, 8:16], 1, A.bitwise_and)
-    ts(T.sx[:], T.stb[:, 0:8], 513.0, A.mult)
+    ts(T.sx[:], T.stb[:, 0:8], 513.0, A.mult, free=True)
+    ts(T.b1[:], T.stb[:, 8:16], 1, A.logical_shift_right, free=True)
     ts(T.sy[:], T.b0[:], 256.0, A.mult)
     tt(T.sz[:], T.sx[:], T.sy[:], A.add)
     ts(T.sw[:], T.sz[:], 3, A.logical_shift_right, 511, A.bitwise_and)
     kq = cp(T.q1l[:], T.sw[:])
-    ts(T.b1[:], T.stb[:, 8:16], 1, A.logical_shift_right)
     a.wait_ge(s.sv, kq)
     a.wait_ge(s.g2, 1)
     act(T.c0l[:], T.c0w[:].indirect(T.q1l[:, 0:8]), C.Copy)
@@ -215,106 +222,116 @@ def rank_program(g, core, T, topo):
     v.wait_ge(s.dnx, 64)
     ts(T.nl[:], T.p1w[:].indirect(T.q1l[:, 0:8]), 2.0, A.mult)
     cp(T.nd[:, 0:16:2, :], T.nl[:])
-    cp(T.nd[:, 1:16:2, :], T.nl[:])
+    cp(T.nd[:, 1:16:2, :], T.nl[:], free=True)
     vec(v.transpose, T.tn[:], T.nd[:])
     tt(T.uf[:], T.tn[:, :, 0], T.b1[:], A.add)
     ku = cp(T.ul[:, 8 * me:8 * me + 8], T.uf[:])
-
-    g.wait_ge(s.dnat, 16)
-    send(lambda k: T.nat[:], lambda m: T.natl[m], T.fn[:], s.m0, s.f0)
     g.wait_ge(s.sv, ku)
-    send(lambda k: T.ul[:, 8 * me:8 * me + 8], lambda m: T.ul[:, 8 * me:8 * me + 8], T.fu[:], s.m1, s.f1)
+    send(1, lambda k: T.ul[:, 8 * me:8 * me + 8], lambda m: T.ul[:, 8 * me:8 * me + 8], T.fu[:], s.m1, s.f1)
+
+    act(new("l1"), eq(0), bias=eq(1))
+    act(new("l2"), eq(2), bias=c("l1"))
+    act(new("keep"), eq(8), bias=c("l2"))
+    act(new("init2"), q16, scale=48.0, bias=-1.0, free=True)
+    for r in range(N):
+        act(new("t%d" % r), eq(10), C.Copy, scale=float(TX + CAP * others.index(r) if r != me else 0), free=True)
+    act(new("q16m"), q16, bias=-256.0, free=True)
+    for r in range(N):
+        act(new("b%d" % r), eq(13), scale=r + 1.0, bias=c("t%d" % r), free=r > 0)
+        act(T.data0[:, 128 * r:128 * r + 128], T.zb[:, 0:128], bias=c("l2") if r == me else c("keep"), free=True)
+    act(T.trc[:], T.iob[:], scale=0.5, bias=c("q16m"), free=True)
+    act(T.w2[:], T.zb[:, 0:400], C.Copy, free=True)
+    act(T.data0[:, 0:512:128], T.zb[:, 0:4], bias=c("l2"))
+    kw2 = act(T.c0m[:], T.vs1[:], scale=eq(10), bias=c("b%d" % me), free=True)
 
     v.wait_ge(s.sa, kw)
     cp(T.gs1[:, 0:128], T.win2[:].indirect(T.ul[:, 8 * me:8 * me + 8]))
-    vec(v.tensor_tensor_scan, T.gs1[:, 128:256], T.ones[:, 0:128], T.gs1[:, 0:128], col["init1"], A.mult, A.add)
+    vec(v.tensor_tensor_scan, T.gs1[:, 128:256], T.ones[:], T.gs1[:, 0:128], c("init1"), A.mult, A.add)
     vec(v.transpose, T.tg[:], T.gs1[:])
     tt(T.x1[:], T.tg[:, 0:4, 4:8], T.tg[:, 4:8, 4:8], A.mult)
+    v.wait_ge(s.dx, 16)
+    vec(v.quantize_mx, T.xq[:], T.xs[:], T.xb[:], free=True)
     tt(T.x1b[:], T.x1[:, :, 0:2], T.x1[:, :, 2:4], A.add)
     tt(T.x1c[:], T.x1b[:, :, 0], T.x1b[:, :, 1], A.add)
     ts(T.off1[:], T.x1c[:], 128.0, A.add)
     v.wait_ge(s.sa, kvs1)
     cp(T.w1[:].indirect(T.off1[:, 0:4]), T.vs1[:])
     cp(T.d1[:, 0:18:2, :], T.w1[:, 128:272])
-    cp(T.d1[:, 1:18:2, :], T.w1[:, 128:272])
+    cp(T.d1[:, 1:18:2, :], T.w1[:, 128:272], free=True)
     vec(v.transpose, T.td1[:], T.d1[:])
     tt(T.l1f[:], T.td1[:, :, 0], T.td1[:, :, 16], A.add)
-    v.wait_ge(s.dx, 16)
-    vec(v.quantize_mx, T.xq[:], T.xs[:], T.xb[:])
     kl = cp(T.list1[:, 0:9], T.l1f[:])
     a.wait_ge(s.sv, kl)
     ksc = act(T.ps1[:], T.xs[:].indirect(T.list1[:, 0:9]), C.Copy)
     kpk = cp(T.pk1[:].bitcast(dt.uint32), T.xq[:].bitcast(dt.uint32).indirect(T.list1[:, 0:9]))
     g.wait_ge(s.sv, kpk)
-    send(lambda k: T.pk1[:, CAP * k:CAP * k + CAP].bitcast(dt.uint8), lambda m: T.cb[:, TX + CAP * m:TX + CAP * m + CAP].bitcast(dt.uint8),
+    send(0, lambda k: T.pk1[:, CAP * k:CAP * k + CAP].bitcast(dt.uint8), lambda m: T.cb[:, TX + CAP * m:TX + CAP * m + CAP].bitcast(dt.uint8),
          T.fc1[:].bitcast(dt.uint8), s.c1, s.f1c)
     g.wait_ge(s.sa, ksc)
-    send(lambda k: T.ps1[:, CAP * k:CAP * k + CAP], lambda m: T.cbs[:, TX + CAP * m:TX + CAP * m + CAP], T.fs1[:], s.c1, s.f1s)
-    g.iota(T.p3w[:], [[0, 2048]], 0, 0).then_inc(s.g5, 1)
+    send(1, lambda k: T.ps1[:, CAP * k:CAP * k + CAP], lambda m: T.cbs[:, TX + CAP * m:TX + CAP * m + CAP], T.fs1[:], s.c1, s.f1s)
+    iota(T.iot[:], [[0, 4], [32, 4], [1, 16]], 1, 0, s.g4)
 
-    v.wait_ge(s.dns, 32)
-    vec(v.transpose, T.nxt[0:32, :], T.nxs[0:32, :])
-    ts(T.nxr[0:32, :], T.nxt[0:32, 0:16], 8, A.logical_shift_right)
+    v.wait_ge(s.dns, 64)
+    vec(v.transpose, T.nxt[:], T.nxs[:])
+    ts(T.nxr[:], T.nxt[:, 0:16], 8, A.logical_shift_right)
     for r in range(4):
-        km = ts(T.mk[0:32, 16 * r:16 * r + 16], T.nxr[0:32, :], float(others[r] if r < 3 else me), A.is_equal)
+        km = ts(T.mk[32 * r:32 * r + 32, :], T.nxr[32 * r:32 * r + 32, :], float(others[r] if r < 3 else me), A.is_equal, free=r > 0)
     g.sync.wait_ge(s.sv, km)
     for b in range(4):
-        for r in range(4):
-            g.sync.dma_start(T.win2[32 * b + r:32 * b + r + 1, 512 * me:512 * me + 512], T.mk[0:32, 16 * r:16 * r + 16]).then_inc(s.dmk, 16)
-    g.sync.wait_ge(s.g5, 1)
-    for b in range(4):
-        for r in (12, 28):
-            g.sync.dma_start(T.p3w[32 * b + r:32 * b + r + 1, 512 * me:512 * me + 512], T.nx[:]).then_inc(s.down, 16)
-    g.sync.wait_ge(s.m0, 24)
-    for k, r in enumerate(others):
-        for b in range(4):
-            for p in (12, 28):
-                g.sync.dma_start(T.p3w[32 * b + p:32 * b + p + 1, 512 * r:512 * r + 512], T.natl[k]).then_inc(s.drem, 16)
-
-    ts(new("l2"), q16, 2.0, A.is_le)
-    kd = tt(new("keep"), col["l2"], col["e8"], A.add)
-    ts(new("init2"), q16, 48.0, A.mult, -1.0, A.add)
-    ts(new("i10"), q16, 10.0, A.is_equal)
-    for r in range(N):
-        ts(new("s%d" % r), q16, 13.0, A.is_equal, r + 1.0, A.mult)
-        if r != me:
-            ts(new("k%d" % r), q16, 10.0, A.is_equal, float(TX + CAP * others.index(r)), A.mult)
-            tt(new("b%d" % r), col["k%d" % r], col["s%d" % r], A.add)
-    ts(new("q16m"), q16, 1.0, A.mult, -256.0, A.add)
-    ts(T.trc[:], T.iob[:], 0.5, A.mult, col["q16m"], A.add)
-    ts(T.c0m[:], T.vs1[:], col["i10"], A.mult, col["s%d" % me], A.add)
-    a.wait_ge(s.sv, kd)
-    for r in range(N):
-        act(T.data0[:, 128 * r:128 * r + 128], T.zb[:, 0:128], C.Identity, bias=col["l2"] if r == me else col["keep"])
-    act(T.data0[:, 0:512:128], T.zb[:, 0:4], C.Identity, bias=col["l2"])
-    act(T.w2[:], T.zb[:, 0:400], C.Copy)
-    kw2 = act(T.w3[:], T.zb[:, 0:448], C.Copy)
+        g.sync.dma_start(T.win2[32 * b:32 * b + 4, 512 * me:512 * me + 512], T.mk[:]).then_inc(s.dmk, 16)
+    g.sync.wait_ge(s.m0, 40)
+    for r in others:
+        g.sync.dma_start(T.nx4[32 * r:32 * r + 16, :], T.natl[2 * r:2 * r + 2]).then_inc(s.dn4, 16)
     vec(v.quantize_mx, T.cb[:, 0:TX], T.cbs[:, 0:TX], T.xb[:])
 
+    for r in range(4):
+        kp3 = act(T.p3w[:, 512 * r:512 * r + 512], T.zb[:], C.Copy, free=r > 0)
+    act(new("keep3"), eq(15), bias=c("l2"))
+    act(new("o16"), q16, scale=-1.0, bias=q32, free=True)
+    act(new("nzt"), c("l2"), scale=-1.0, bias=1.0, free=True)
+    act(T.ac[:], T.trc[:], scale=-1.0, bias=-1.0, free=True)
+    act(T.w3[:], T.zb[:, 0:448], C.Copy, free=True)
+    act(T.c3[:], T.zb[:, 0:192], C.Copy, free=True)
+    for x in (T.aw, T.bw, T.cw):
+        act(x[:, 0:1], T.zb[:, 0:1], C.Copy, free=True)
+    for k in range(3):
+        act(T.kc[:, :, k], T.zb[:, 0:12], bias=400.0 + 96.0 * k, free=True)
+    act(new("kic"), eq(14), C.Copy, scale=c("o16"))
+    act(new("nz"), eq(3), scale=-1.0, bias=c("nzt"), free=True)
+    act(T.data3[:], T.zb[:], bias=c("keep3"), free=True)
+    a.wait_ge(s.g4, 1)
+    act(T.ki[:], T.iot[:], scale=eq(14), bias=c("kic"))
+
+    g2, s2 = T.gs2[:, 0:512], T.gs2[:, 512:1024]
     v.wait_ge(s.m1, 24)
-    v.wait_ge(s.dmk, 256)
+    v.wait_ge(s.dmk, 64)
     v.wait_ge(s.sa, kw2)
-    cp(T.g2[:], T.win2[:].indirect(T.ul[:, 0:32]))
-    ks2 = vec(v.tensor_tensor_scan, T.s2[:], T.data0[:], T.g2[:], col["init2"], A.mult, A.add)
+    cp(g2, T.win2[:].indirect(T.ul[:, 0:32]))
+    ks2 = vec(v.tensor_tensor_scan, s2, T.data0[:], g2, c("init2"), A.mult, A.add)
     a.wait_ge(s.sv, ks2)
-    for r in others:
-        kvsel = act(T.vsel[:, 64 * r:64 * r + 64], T.s2[:].indirect(T.offsel[:, 4 * r:4 * r + 4]), C.Identity, bias=col["b%d" % r])
-    vec(v.transpose, T.tm[:], T.g2[:])
-    vec(v.transpose, T.ts[:], T.s2[:])
-    tt(T.x2[:, :, 3], T.tm[:, :, 3], T.trc[:], A.mult)
-    tt(T.x2[:, :, 0:3], T.tm[:, :, 0:3], T.ts[:, :, 0:3], A.mult)
+    for n, r in enumerate(others):
+        kvsel = act(T.vsel[:, 64 * r:64 * r + 64], s2.indirect(T.offsel[:, 4 * r:4 * r + 4]), bias=c("b%d" % r), free=n > 0)
+    vec(v.transpose, T.tg2[:], T.gs2[:])
+    tt(T.vsel[:, 64 * me:64 * me + 64], s2.indirect(T.offsel[:, 4 * me:4 * me + 4]), T.c0m[:], A.add, free=True)
+    tt(T.x2[:, :, 3], T.tg2[:, 0:16, 3], T.trc[:], A.mult)
+    tt(T.x2[:, :, 0:3], T.tg2[:, 0:16, 0:3], T.tg2[:, 16:32, 0:3], A.mult, free=True)
     tt(T.x2b[:], T.x2[:, :, 0:2], T.x2[:, :, 2:4], A.add)
     tt(T.x2c[:], T.x2b[:, :, 0], T.x2b[:, :, 1], A.add)
     ts(T.off2[:], T.x2c[:], 256.0, A.add)
-    tt(T.vsel[:, 64 * me:64 * me + 64], T.s2[:].indirect(T.offsel[:, 4 * me:4 * me + 4]), T.c0m[:], A.add)
     v.wait_ge(s.sa, kvsel)
     cp(T.w2[:].indirect(T.off2[:, 0:16]), T.vsel[:])
     cp(T.d2[:, 0:18:2, :], T.w2[:, 256:400])
-    cp(T.d2[:, 1:18:2, :], T.w2[:, 256:400])
+    cp(T.d2[:, 1:18:2, :], T.w2[:, 256:400], free=True)
     vec(v.transpose, T.td2[:], T.d2[:])
+    v.wait_ge(s.dn4, 64)
+    vec(v.transpose, T.nt4[:], T.nx4[:], free=True)
     tt(T.h2[:], T.td2[:, :, 8:12], T.td2[:, :, 24:28], A.add)
+    ts(T.r4[:], T.nt4[:, 0:16], 8, A.logical_shift_right, free=True)
+    ts(T.c4[:], T.nt4[:, 0:16], 255, A.bitwise_and, free=True)
     tt(T.nf[:, :, 0, :], T.h2[:, :, :, 0], T.h2[:, :, :, 2], A.add)
-    tt(T.nf[:, :, 1, :], T.h2[:, :, :, 1], T.h2[:, :, :, 3], A.add)
+    tt(T.nf[:, :, 1, :], T.h2[:, :, :, 1], T.h2[:, :, :, 3], A.add, free=True)
+    ts(T.mp[:], T.r4[:], float(me), A.is_equal, free=True)
+    ts(T.cp4[:], T.c4[:], 1.0, A.add, free=True)
     kl2 = ts(T.list2[:], T.nf[:], -1.0, A.add)
     a.wait_ge(s.sv, kl2)
     a.wait_ge(s.c1, 48)
@@ -322,13 +339,25 @@ def rank_program(g, core, T, topo):
     v.wait_ge(s.c1, 48)
     kpk2 = cp(T.pk2[:].bitcast(dt.uint32), T.cb[:].bitcast(dt.uint32).indirect(T.list2[:, 0:18]))
     g.wait_ge(s.sv, kpk2)
-    send(lambda k: T.pk2[:, 96 * k:96 * k + 96].bitcast(dt.uint8), lambda m: T.lc[:, 96 * m:96 * m + 96].bitcast(dt.uint8),
+    send(0, lambda k: T.pk2[:, 96 * k:96 * k + 96].bitcast(dt.uint8), lambda m: T.lc[:, 96 * m:96 * m + 96].bitcast(dt.uint8),
          T.fc2[:].bitcast(dt.uint8), s.c2, s.f2c)
     g.wait_ge(s.sa, ksc2)
-    send(lambda k: T.ps2[:, 96 * k:96 * k + 96], lambda m: T.ls[:, 96 * m:96 * m + 96], T.fs2[:], s.c2, s.f2s)
+    send(1, lambda k: T.ps2[:, 96 * k:96 * k + 96], lambda m: T.ls[:, 96 * m:96 * m + 96], T.fs2[:], s.c2, s.f2s)
+    kvsk = act(T.vsk[:], T.vsel[:], C.Copy, scale=c("nz"))
+
+    g.sync.wait_ge(s.sv, kl2)
+    g.sync.wait_ge(s.sa, kp3)
+    for b in range(0, 128, 32):
+        g.sync.dma_start(T.p3w[b + 15:b + 16, :], T.mp[:]).then_inc(s.drow, 16)
+        for h in (0, 16):
+            g.sync.dma_start(T.p3w[b + h + 12:b + h + 13, :], T.cp4[:]).then_inc(s.drow, 16)
+            for k, r in enumerate(others):
+                g.sync.dma_start(T.p3w[b + h + k:b + h + k + 1, 512 * r:512 * r + 512], T.mp[32 * r:32 * r + 32, :]).then_inc(s.drow, 16)
 
     v.wait_ge(s.dw, 16)
     kwq = vec(v.quantize_mx, T.wq[:], T.ws[:], T.wb[:])
+    v.wait_ge(s.sa, kvsk)
+    tt(T.vselk[:], T.vsk[:], T.ki[:], A.add)
 
     def w(k):
         return T.wq[:, 128 * k:128 * k + 128], T.ws[:, 128 * k:128 * k + 128]
@@ -339,76 +368,48 @@ def rank_program(g, core, T, topo):
     m0 = mm(T.ps[:, 0:400], *w(0), T.cb[:], T.cbs[:], True, True)
     a.wait_ge(s.st, m0)
     act(T.aw[:, 1:401], T.ps[:, 0:400], C.Copy)
-    act(T.bw[:, 1:257], T.ps[:, 512:768], C.Copy)
-    kaw = act(T.cw[:, 1:257], T.ps[:, 1024:1280], C.Copy)
+    act(T.bw[:, 1:257], T.ps[:, 512:768], C.Copy, free=True)
+    kaw = act(T.cw[:, 1:257], T.ps[:, 1024:1280], C.Copy, free=True)
 
-    ts(T.ic[:, 2:3], T.pi[:], 16, A.bitwise_and)
-    ts(new("o16"), T.ic[:, 2:3], 1.0, A.mult)
-    ts(new("i14"), q16, 14.0, A.is_equal)
-    ts(new("i12"), q16, 12.0, A.is_equal)
-    ts(new("kic"), col["i14"], col["o16"], A.mult, col["i12"], A.add)
-    v.wait_ge(s.g4, 1)
-    ts(T.ki[:], T.iot[:], col["i14"], A.mult, col["kic"], A.add)
-    tt(T.vselk[:], T.vsel[:], T.ki[:], A.add)
-    cp(T.ui[:], T.ul[:])
-    ts(T.ua[:], T.ui[:], 511, A.bitwise_and)
-    tt(T.ui[:], T.ui[:], T.ua[:], A.subtract)
-    ts(T.uc[:], T.ua[:], 513.0, A.mult)
-    ts(T.ua[:], T.uc[:], 4, A.logical_shift_right, 511, A.bitwise_and)
-    tt(T.uc[:], T.ui[:], T.ua[:], A.add)
-    cp(T.u3[:], T.uc[:])
-    ts(T.ac[:], T.trc[:], -1.0, A.mult, -1.0, A.add)
-    vec(v.memset, T.c3[:], 0.0)
-    vec(v.memset, T.aw[:, 0:1], 0.0)
-    vec(v.memset, T.bw[:, 0:1], 0.0)
-    vec(v.memset, T.cw[:, 0:1], 0.0)
-    for k in range(3):
-        vec(v.memset, T.kc[:, :, k], 400.0 + 96.0 * k)
-    v.wait_ge(s.down, 128)
-    v.wait_ge(s.drem, 384)
-    cp(T.n2[:], T.p3w[:].indirect(T.u3[:, 0:32]))
-    ts(T.r3[:], T.n2[:], 8, A.logical_shift_right)
-    ts(T.m3[:], T.r3[:], float(me), A.is_equal)
-    vec(v.tensor_tensor_scan, T.s3[:], T.ones[:], T.m3[:], 0.0, A.mult, A.add)
-    vec(v.transpose, T.tm3[:], T.m3[:])
-    vec(v.transpose, T.ts3[:], T.s3[:])
-    tt(T.v3[:], T.ts3[:, :, 12], T.ac[:], A.add)
-    tt(T.v3[:], T.v3[:], T.tm3[:, :, 12], A.mult)
-    tt(T.v3[:], T.v3[:], T.trc[:], A.add)
-    ts(T.off3[:], T.v3[:], 256.0, A.add)
-    cp(T.c2s[:], T.n2[:].indirect(T.offsel[:, 0:16]))
-    ts(T.c2a[:], T.c2s[:], 255, A.bitwise_and)
-    tt(T.val3[:], T.vselk[:], T.c2a[:], A.add)
+    g3, s3 = T.gs3[:, 0:512], T.gs3[:, 512:1024]
+    v.wait_ge(s.drow, 576)
+    cp(g3, T.p3w[:].indirect(T.ul[:, 0:32]))
+    vec(v.tensor_tensor_scan, s3, T.data3[:], g3, 0.0, A.mult, A.add)
+    vec(v.transpose, T.tg3[:], T.gs3[:])
+    tt(T.val3[:], s3.indirect(T.offsel[:, 0:16]), T.vselk[:], A.add, free=True)
+    tt(T.va[:], T.tg3[:, 16:32, 15], T.ac[:], A.add)
+    tt(T.vb[:], T.va[:], T.tg3[:, 0:16, 15], A.mult)
+    tt(T.vc[:], T.vb[:], T.trc[:], A.add)
+    ts(T.off3[:], T.vc[:], 256.0, A.add)
     cp(T.w3[:].indirect(T.off3[:, 0:16]), T.val3[:])
-    vec(v.transpose, T.t3[:], T.w3[:, 256:448])
-    tt(T.c3[:, :, 0:16], T.t3[:, :, 0:16], T.t3[:, :, 16:32], A.add)
-    vec(v.transpose, T.pl[:], T.c3[:])
-    ki = ts(T.idl[:], T.pl[:], -1.0, A.add)
+    cp(T.dp[:, 0:24:2, :], T.w3[:, 256:448])
+    cp(T.dp[:, 1:24:2, :], T.w3[:, 256:448], free=True)
+    vec(v.transpose, T.t3[:], T.w3[:, 256:448], free=True)
+    vec(v.transpose, T.tp[:], T.dp[:])
+    tt(T.c3[:, :, 13:15], T.t3[:, :, 13:15], T.t3[:, :, 29:31], A.add, free=True)
+    tt(T.yy[:], T.tp[:, :, 0:15], T.tp[:, :, 16:31], A.add)
+    vec(v.transpose, T.pl[:], T.c3[:], free=True)
+    tt(T.x3[:, :, 0:3], T.yy[:, :, 0:3], T.kc[:], A.add)
+    tt(T.x3[:, :, 3], T.yy[:, :, 8], T.yy[:, :, 10], A.add, free=True)
+    ki = ts(T.idl[:], T.pl[:], -1.0, A.add, free=True)
+    tt(T.x3m[:], T.x3[:], T.yy[:, :, 4:8], A.mult)
     g.sync.wait_ge(s.sv, ki)
     g.sync.dma_start(T.id[0:1, :], T.idl[13:14, :]).then_inc(s.did, 16)
     g.sync.dma_start(T.id[1:2, :], T.idl[14:15, :]).then_inc(s.did, 16)
-    vec(v.tensor_tensor_scan, T.sc[:], T.ones[:, 0:192], T.pl[:], 0.0, A.mult, A.add)
-    for d, x, t in ((T.dp, T.pl, T.tp), (T.ds, T.sc, T.tc)):
-        cp(d[:, 0:24:2, :], x[:])
-        cp(d[:, 1:24:2, :], x[:])
-        vec(v.transpose, t[:], d[:])
-    tt(T.x3[:, :, 0:3], T.tc[:, :, 4:7], T.kc[:], A.add)
-    tt(T.x3[:, :, 3:5], T.tp[:, :, 8:10], T.tp[:, :, 10:12], A.add)
-    tt(T.x3[:, :, 0:4], T.x3[:, :, 0:4], T.tp[:, :, 4:8], A.mult)
-    tt(T.x3b[:], T.x3[:, :, 0:2], T.x3[:, :, 2:4], A.add)
-    tt(T.x3c[:], T.x3b[:, :, 0], T.x3b[:, :, 1], A.add)
-    cp(T.q0[:], T.x3c[:])
-    cp(T.qb[:], T.x3[:, :, 4])
-    cp(T.qc[:], T.tp[:, :, 12])
+    cp(T.qb[:], T.yy[:, :, 9], free=True)
+    cp(T.qc[:], T.yy[:, :, 12], free=True)
+    tt(T.x3b[:], T.x3m[:, :, 0:2], T.x3m[:, :, 2:4], A.add)
     v.wait_ge(s.sa, kaw)
-    cp(T.t1[:], T.cw[:, 0:257].indirect(T.qc[:, 0:12]))
-    tt(T.t2[:], T.bw[:, 0:257].indirect(T.qb[:, 0:12]), T.t1[:], A.add)
+    cp(T.t1[:], T.cw[:, 0:257].indirect(T.qc[:, 0:12]), free=True)
+    tt(T.x3c[:], T.x3b[:, :, 0], T.x3b[:, :, 1], A.add)
+    tt(T.t2[:], T.bw[:, 0:257].indirect(T.qb[:, 0:12]), T.t1[:], A.add, free=True)
+    cp(T.q0[:], T.x3c[:])
 
     g.tensor.wait_ge(s.c2, 48)
     mm(T.ps[:, 1536:1776], *w(0), T.lc[:, 0:240], T.ls[:, 0:240], True, False)
     m3 = mm(T.ps[:, 1536:1776], *w(1), T.lc[:, 48:288], T.ls[:, 48:288], False, True)
     v.wait_ge(s.st, m3)
-    cp(T.aw[:, 401:641], T.ps[:, 1536:1776])
+    cp(T.aw[:, 401:641], T.ps[:, 1536:1776], free=True)
     ky = tt(T.yo[:], T.aw[:, 0:641].indirect(T.q0[:, 0:12]), T.t2[:], A.add)
     g.sync.wait_ge(s.sv, ky)
     g.sync.dma_start(T.y[:], T.yo[:]).then_inc(s.dy, 16)
@@ -417,4 +418,4 @@ def rank_program(g, core, T, topo):
     g.wait_ge(s.did, 32)
     g.wait_ge(s.sa, cnt["a"])
     g.wait_ge(s.st, cnt["t"])
-    g.wait_ge(s.loc, 6 * sum(len(x[3]) for x in ways))
+    g.wait_ge(s.loc, cnt["loc"])

@@ -17,9 +17,8 @@ SCRATCH = {
     "fc1": _sb(CODE, 48), "fs1": _sb(PLANE, 48), "fc2": _sb(CODE, 96), "fs2": _sb(PLANE, 96),
     "fu": _sb(U, 8), "fn": ("dram", [128, 2], I), "lc": _sb(CODE, 288), "ls": _sb(PLANE, 288), "natl": ("dram", [8, 128, 2], I),
     "pi": _sb(I, 1), "ic": _sb(I, 2), "col": _sb(F, 48), "iob": _sb(F, 16), "io16": _sb(F, 16), "eq": _sb(F, 16),
-    "c0w": _sb(B, 512), "ic1": _sb(B, 512), "iot": _sb(B, 256),
-    "zb": _sb(B, 512), "ones": _sb(B, 128), "offsel": _sb(U, 16), "trc": _sb(F, 16), "ac": _sb(F, 16),
-    "data0": _sb(B, 512), "data3": _sb(B, 512), "ki": _sb(B, 256), "kc": _sb(F, 12, 3),
+    "c0w": _sb(B, 512), "ic1": _sb(B, 512), "zb": _sb(B, 512), "ones": _sb(B, 128), "offsel": _sb(U, 16), "trc": _sb(F, 16), "ac": _sb(F, 16),
+    "data0": _sb(B, 512), "data3": _sb(B, 512), "kc": _sb(F, 12, 3),
     "stb": _sb(I, 16), "b0": _sb(I, 8), "b1": _sb(I, 8), "sx": _sb(I, 8), "sy": _sb(I, 8), "sz": _sb(I, 8), "sw": _sb(I, 8),
     "q1l": _sb(U, 8), "p1w": _sb(I, 512), "nl": _sb(F, 128), "nd": _sb(F, 16, 16), "tn": _sb(F, 8, 32), "uf": _sb(F, 8),
     "ul": _sb(U, 32), "win2": _sb(B, 2048), "gs1": _sb(B, 256), "tg": _sb(B, 8, 32),
@@ -29,18 +28,18 @@ SCRATCH = {
     "nxs": _sb(I, 32), "nxt": _sb(I, 32), "nxr": _sb(I, 16), "mk": _sb(B, 16),
     "gs2": _sb(B, 1024), "tg2": _sb(B, 32, 32),
     "x2": _sb(F, 16, 4), "x2b": _sb(F, 16, 2), "x2c": _sb(F, 16), "off2": _sb(U, 16),
-    "vsel": _sb(B, 256), "w2": _sb(B, 400), "d2": _sb(B, 18, 16), "td2": _sb(B, 9, 32),
+    "vown": _sb(B, 64), "vsel": _sb(B, 256), "w2": _sb(B, 400), "d2": _sb(B, 18, 16), "td2": _sb(B, 9, 32),
     "h2": _sb(F, 3, 3, 4), "nf": _sb(F, 3, 2, 3), "list2": _sb(U, 18),
     "nx4": _sb(I, 32), "nt4": _sb(I, 32), "r4": _sb(I, 16), "c4": _sb(I, 16), "mp": _sb(B, 16), "cp4": _sb(B, 16),
     "p3w": _sb(B, 2048), "gs3": _sb(B, 1024), "tg3": _sb(B, 32, 32), "va": _sb(F, 16), "vb": _sb(F, 16), "vc": _sb(F, 16), "off3": _sb(U, 16),
-    "vsk": _sb(B, 256), "vselk": _sb(B, 256), "val3": _sb(B, 256), "w3": _sb(B, 448),
+    "val3": _sb(B, 256), "w3": _sb(B, 448),
     "t3": _sb(B, 6, 32), "c3": _sb(B, 6, 32), "pl": _sb(B, 192), "idl": _sb(F, 192),
     "dp": _sb(B, 24, 16), "tp": _sb(B, 12, 32), "yy": _sb(F, 12, 15),
     "x3": _sb(F, 12, 4), "x3m": _sb(F, 12, 4), "x3b": _sb(F, 12, 2), "x3c": _sb(F, 12), "q0": _sb(U, 12), "qb": _sb(U, 12), "qc": _sb(U, 12),
     "ps": ("psum", [128, 2048], F), "aw": _sb(F, 648), "bw": _sb(F, 264), "cw": _sb(F, 264),
     "t1": _sb(F, 192), "t2": _sb(F, 192), "yo": _sb(F, 192),
 }
-SEMAPHORES = ["sv", "sa", "st", "g0", "g1", "g2", "g3", "g4", "dsb", "dnx", "dns", "dn4", "dx", "dw", "dnat", "dmk", "drow", "dy", "did",
+SEMAPHORES = ["sv", "sa", "st", "g0", "g1", "g2", "g3", "dsb", "dnx", "dns", "dn4", "dx", "dw", "dnat", "dmk", "drow", "dy", "did",
               "m0", "m1", "c1", "c2", "loc", "f0", "f1", "f1c", "f1s", "f2c", "f2s"]
 
 
@@ -101,8 +100,8 @@ def rank_program(g, core, T, topo):
         cnt["a"] += 1
         return cnt["a"]
 
-    def mm(*args):
-        if cnt["t"]:
+    def mm(*args, free=False):
+        if cnt["t"] and not free:
             g.tensor.wait_ge(s.st, cnt["t"])
         g.tensor.matmul_mx(*args).then_inc(s.st, 1)
         cnt["t"] += 1
@@ -135,11 +134,14 @@ def rank_program(g, core, T, topo):
             cnt["loc"] += h
         g.remote_dma_fused(tr, local_sem=s.loc)
 
-    def send(h, src, far, near, far_sem, near_sem):
-        call([(forwarders(topo, core, T.cores[others[k]])[h], n, len(rest), near_sem, src(k), near) for n, k in enumerate(rest)])
-        for k in peer:
-            mine = [q for q in range(N) if q != others[k]].index(me)
-            call([(T.cores[others[k]], 0, 1, far_sem, src(k), far(mine))])
+    def send(msgs):
+        for h, sem, n, src, far, near, far_sem, near_sem in msgs:
+            g.wait_ge(sem, n)
+            call([(forwarders(topo, core, T.cores[others[k]])[h], n, len(rest), near_sem, src(k), near) for n, k in enumerate(rest)])
+        for h, sem, n, src, far, near, far_sem, near_sem in msgs:
+            for k in peer:
+                mine = [q for q in range(N) if q != others[k]].index(me)
+                call([(T.cores[others[k]], 0, 1, far_sem, src(k), far(mine))])
 
     col = {}
 
@@ -173,18 +175,18 @@ def rank_program(g, core, T, topo):
     g.sync.dma_start(T.nx4[32 * me:32 * me + 16, :], T.nx[:]).then_inc(s.dn4, 16)
     g.sync.dma_start(T.wb[:], T.w[:]).then_inc(s.dw, 16)
 
-    def iota(out, pattern, base, mult, sem):
-        g.iota(out, pattern, base, mult, allow_small_or_imprecise_dtypes=True).then_inc(sem, 1)
+    def iota(out, pattern, sem, base=0):
+        g.iota(out, pattern, base, 0, allow_small_or_imprecise_dtypes=True).then_inc(sem, 1)
     g.iota(T.pi[:], [[0, 1]], 0, 1).then_inc(s.g0, 1)
-    iota(T.io16[:], [[1, 16]], 0, 0, s.g3)
-    iota(T.iob[:], [[32, 16]], 0, 0, s.g3)
-    iota(T.c0w[:], [[1, 8], [0, 2], [8, 32]], 0, 0, s.g2)
+    iota(T.io16[:], [[1, 16]], s.g3)
+    iota(T.iob[:], [[32, 16]], s.g3)
+    iota(T.c0w[:], [[1, 8], [0, 2], [8, 32]], s.g2)
+    iota(T.ic1[:], [[1, 256], [0, 2]], s.g1, 1)
     g.wait_ge(s.dnat, 16)
     call([(forwarders(topo, core, T.cores[others[k]])[h], 2 * n + h, 2 * len(rest), s.f0, T.natl[2 * me + h], T.fn[:])
           for n, k in enumerate(rest) for h in (0, 1)])
     for k in peer:
         call([(T.cores[others[k]], h, 2, s.m0, T.natl[2 * me + h], T.natl[2 * me + h]) for h in (0, 1)])
-    iota(T.ic1[:], [[1, 256], [0, 2]], 1, 0, s.g1)
 
     fill(T.zb[:], 0.0, free=False)
     v.wait_ge(s.g0, 1)
@@ -226,12 +228,12 @@ def rank_program(g, core, T, topo):
     vec(v.transpose, T.tn[:], T.nd[:])
     tt(T.uf[:], T.tn[:, :, 0], T.b1[:], A.add)
     ku = cp(T.ul[:, 8 * me:8 * me + 8], T.uf[:])
-    g.wait_ge(s.sv, ku)
-    send(1, lambda k: T.ul[:, 8 * me:8 * me + 8], lambda m: T.ul[:, 8 * me:8 * me + 8], T.fu[:], s.m1, s.f1)
+    send([(1, s.sv, ku, lambda k: T.ul[:, 8 * me:8 * me + 8], lambda m: T.ul[:, 8 * me:8 * me + 8], T.fu[:], s.m1, s.f1)])
 
     act(new("l1"), eq(0), bias=eq(1))
     act(new("l2"), eq(2), bias=c("l1"))
     act(new("keep"), eq(8), bias=c("l2"))
+    act(new("nzt"), c("l2"), scale=-1.0, bias=1.0, free=True)
     act(new("init2"), q16, scale=48.0, bias=-1.0, free=True)
     for r in range(N):
         act(new("t%d" % r), eq(10), C.Copy, scale=float(TX + CAP * others.index(r) if r != me else 0), free=True)
@@ -239,6 +241,7 @@ def rank_program(g, core, T, topo):
     for r in range(N):
         act(new("b%d" % r), eq(13), scale=r + 1.0, bias=c("t%d" % r), free=r > 0)
         act(T.data0[:, 128 * r:128 * r + 128], T.zb[:, 0:128], bias=c("l2") if r == me else c("keep"), free=True)
+    act(new("nz"), eq(3), scale=-1.0, bias=c("nzt"), free=True)
     act(T.trc[:], T.iob[:], scale=0.5, bias=c("q16m"), free=True)
     act(T.w2[:], T.zb[:, 0:400], C.Copy, free=True)
     act(T.data0[:, 0:512:128], T.zb[:, 0:4], bias=c("l2"))
@@ -264,12 +267,9 @@ def rank_program(g, core, T, topo):
     a.wait_ge(s.sv, kl)
     ksc = act(T.ps1[:], T.xs[:].indirect(T.list1[:, 0:9]), C.Copy)
     kpk = cp(T.pk1[:].bitcast(dt.uint32), T.xq[:].bitcast(dt.uint32).indirect(T.list1[:, 0:9]))
-    g.wait_ge(s.sv, kpk)
-    send(0, lambda k: T.pk1[:, CAP * k:CAP * k + CAP].bitcast(dt.uint8), lambda m: T.cb[:, TX + CAP * m:TX + CAP * m + CAP].bitcast(dt.uint8),
-         T.fc1[:].bitcast(dt.uint8), s.c1, s.f1c)
-    g.wait_ge(s.sa, ksc)
-    send(1, lambda k: T.ps1[:, CAP * k:CAP * k + CAP], lambda m: T.cbs[:, TX + CAP * m:TX + CAP * m + CAP], T.fs1[:], s.c1, s.f1s)
-    iota(T.iot[:], [[0, 4], [32, 4], [1, 16]], 1, 0, s.g4)
+    send([(0, s.sv, kpk, lambda k: T.pk1[:, CAP * k:CAP * k + CAP].bitcast(dt.uint8), lambda m: T.cb[:, TX + CAP * m:TX + CAP * m + CAP].bitcast(dt.uint8),
+           T.fc1[:].bitcast(dt.uint8), s.c1, s.f1c),
+          (1, s.sa, ksc, lambda k: T.ps1[:, CAP * k:CAP * k + CAP], lambda m: T.cbs[:, TX + CAP * m:TX + CAP * m + CAP], T.fs1[:], s.c1, s.f1s)])
 
     v.wait_ge(s.dns, 64)
     vec(v.transpose, T.nxt[:], T.nxs[:])
@@ -283,12 +283,18 @@ def rank_program(g, core, T, topo):
     for r in others:
         g.sync.dma_start(T.nx4[32 * r:32 * r + 16, :], T.natl[2 * r:2 * r + 2]).then_inc(s.dn4, 16)
     vec(v.quantize_mx, T.cb[:, 0:TX], T.cbs[:, 0:TX], T.xb[:])
+    v.wait_ge(s.dw, 16)
+    vec(v.quantize_mx, T.wq[:], T.ws[:], T.wb[:], free=True)
+    v.wait_ge(s.dn4, 64)
+    vec(v.transpose, T.nt4[:], T.nx4[:], free=True)
+    ts(T.r4[:], T.nt4[:, 0:16], 8, A.logical_shift_right)
+    ts(T.c4[:], T.nt4[:, 0:16], 255, A.bitwise_and, free=True)
+    ts(T.mp[:], T.r4[:], float(me), A.is_equal)
+    kc4 = ts(T.cp4[:], T.c4[:], 1.0, A.add, free=True)
 
     for r in range(4):
-        kp3 = act(T.p3w[:, 512 * r:512 * r + 512], T.zb[:], C.Copy, free=r > 0)
-    act(new("keep3"), eq(15), bias=c("l2"))
-    act(new("o16"), q16, scale=-1.0, bias=q32, free=True)
-    act(new("nzt"), c("l2"), scale=-1.0, bias=1.0, free=True)
+        kp3 = act(T.p3w[:, 512 * r:512 * r + 512], T.zb[:], bias=eq(14), free=r > 0)
+    act(new("kp"), eq(15), bias=c("l2"))
     act(T.ac[:], T.trc[:], scale=-1.0, bias=-1.0, free=True)
     act(T.w3[:], T.zb[:, 0:448], C.Copy, free=True)
     act(T.c3[:], T.zb[:, 0:192], C.Copy, free=True)
@@ -296,11 +302,18 @@ def rank_program(g, core, T, topo):
         act(x[:, 0:1], T.zb[:, 0:1], C.Copy, free=True)
     for k in range(3):
         act(T.kc[:, :, k], T.zb[:, 0:12], bias=400.0 + 96.0 * k, free=True)
-    act(new("kic"), eq(14), C.Copy, scale=c("o16"))
-    act(new("nz"), eq(3), scale=-1.0, bias=c("nzt"), free=True)
-    act(T.data3[:], T.zb[:], bias=c("keep3"), free=True)
-    a.wait_ge(s.g4, 1)
-    act(T.ki[:], T.iot[:], scale=eq(14), bias=c("kic"))
+    act(new("keep3"), eq(14), bias=c("kp"))
+    act(T.data3[:], T.zb[:], bias=c("keep3"))
+    act(T.data3[:, 0:512:128], T.zb[:, 0:4], bias=c("kp"))
+
+    g.sync.wait_ge(s.sv, kc4)
+    g.sync.wait_ge(s.sa, kp3)
+    for b in range(0, 128, 32):
+        g.sync.dma_start(T.p3w[b + 15:b + 16, :], T.mp[:]).then_inc(s.drow, 16)
+        for h in (0, 16):
+            g.sync.dma_start(T.p3w[b + h + 12:b + h + 13, :], T.cp4[:]).then_inc(s.drow, 16)
+            for k, r in enumerate(others):
+                g.sync.dma_start(T.p3w[b + h + k:b + h + k + 1, 512 * r:512 * r + 512], T.mp[32 * r:32 * r + 32, :]).then_inc(s.drow, 16)
 
     g2, s2 = T.gs2[:, 0:512], T.gs2[:, 512:1024]
     v.wait_ge(s.m1, 24)
@@ -309,10 +322,12 @@ def rank_program(g, core, T, topo):
     cp(g2, T.win2[:].indirect(T.ul[:, 0:32]))
     ks2 = vec(v.tensor_tensor_scan, s2, T.data0[:], g2, c("init2"), A.mult, A.add)
     a.wait_ge(s.sv, ks2)
+    kvo = act(T.vown[:], s2.indirect(T.offsel[:, 4 * me:4 * me + 4]), C.Copy, scale=c("nz"))
     for n, r in enumerate(others):
-        kvsel = act(T.vsel[:, 64 * r:64 * r + 64], s2.indirect(T.offsel[:, 4 * r:4 * r + 4]), bias=c("b%d" % r), free=n > 0)
+        kvsel = act(T.vsel[:, 64 * r:64 * r + 64], s2.indirect(T.offsel[:, 4 * r:4 * r + 4]), scale=c("nz"), bias=c("b%d" % r), free=n > 0)
     vec(v.transpose, T.tg2[:], T.gs2[:])
-    tt(T.vsel[:, 64 * me:64 * me + 64], s2.indirect(T.offsel[:, 4 * me:4 * me + 4]), T.c0m[:], A.add, free=True)
+    v.wait_ge(s.sa, kvo)
+    tt(T.vsel[:, 64 * me:64 * me + 64], T.vown[:], T.c0m[:], A.add, free=True)
     tt(T.x2[:, :, 3], T.tg2[:, 0:16, 3], T.trc[:], A.mult)
     tt(T.x2[:, :, 0:3], T.tg2[:, 0:16, 0:3], T.tg2[:, 16:32, 0:3], A.mult, free=True)
     tt(T.x2b[:], T.x2[:, :, 0:2], T.x2[:, :, 2:4], A.add)
@@ -323,45 +338,22 @@ def rank_program(g, core, T, topo):
     cp(T.d2[:, 0:18:2, :], T.w2[:, 256:400])
     cp(T.d2[:, 1:18:2, :], T.w2[:, 256:400], free=True)
     vec(v.transpose, T.td2[:], T.d2[:])
-    v.wait_ge(s.dn4, 64)
-    vec(v.transpose, T.nt4[:], T.nx4[:], free=True)
     tt(T.h2[:], T.td2[:, :, 8:12], T.td2[:, :, 24:28], A.add)
-    ts(T.r4[:], T.nt4[:, 0:16], 8, A.logical_shift_right, free=True)
-    ts(T.c4[:], T.nt4[:, 0:16], 255, A.bitwise_and, free=True)
     tt(T.nf[:, :, 0, :], T.h2[:, :, :, 0], T.h2[:, :, :, 2], A.add)
     tt(T.nf[:, :, 1, :], T.h2[:, :, :, 1], T.h2[:, :, :, 3], A.add, free=True)
-    ts(T.mp[:], T.r4[:], float(me), A.is_equal, free=True)
-    ts(T.cp4[:], T.c4[:], 1.0, A.add, free=True)
     kl2 = ts(T.list2[:], T.nf[:], -1.0, A.add)
     a.wait_ge(s.sv, kl2)
     a.wait_ge(s.c1, 48)
     ksc2 = act(T.ps2[:], T.cbs[:].indirect(T.list2[:, 0:18]), C.Copy)
     v.wait_ge(s.c1, 48)
     kpk2 = cp(T.pk2[:].bitcast(dt.uint32), T.cb[:].bitcast(dt.uint32).indirect(T.list2[:, 0:18]))
-    g.wait_ge(s.sv, kpk2)
-    send(0, lambda k: T.pk2[:, 96 * k:96 * k + 96].bitcast(dt.uint8), lambda m: T.lc[:, 96 * m:96 * m + 96].bitcast(dt.uint8),
-         T.fc2[:].bitcast(dt.uint8), s.c2, s.f2c)
-    g.wait_ge(s.sa, ksc2)
-    send(1, lambda k: T.ps2[:, 96 * k:96 * k + 96], lambda m: T.ls[:, 96 * m:96 * m + 96], T.fs2[:], s.c2, s.f2s)
-    kvsk = act(T.vsk[:], T.vsel[:], C.Copy, scale=c("nz"))
-
-    g.sync.wait_ge(s.sv, kl2)
-    g.sync.wait_ge(s.sa, kp3)
-    for b in range(0, 128, 32):
-        g.sync.dma_start(T.p3w[b + 15:b + 16, :], T.mp[:]).then_inc(s.drow, 16)
-        for h in (0, 16):
-            g.sync.dma_start(T.p3w[b + h + 12:b + h + 13, :], T.cp4[:]).then_inc(s.drow, 16)
-            for k, r in enumerate(others):
-                g.sync.dma_start(T.p3w[b + h + k:b + h + k + 1, 512 * r:512 * r + 512], T.mp[32 * r:32 * r + 32, :]).then_inc(s.drow, 16)
-
-    v.wait_ge(s.dw, 16)
-    kwq = vec(v.quantize_mx, T.wq[:], T.ws[:], T.wb[:])
-    v.wait_ge(s.sa, kvsk)
-    tt(T.vselk[:], T.vsk[:], T.ki[:], A.add)
+    send([(0, s.sv, kpk2, lambda k: T.pk2[:, 96 * k:96 * k + 96].bitcast(dt.uint8), lambda m: T.lc[:, 96 * m:96 * m + 96].bitcast(dt.uint8),
+           T.fc2[:].bitcast(dt.uint8), s.c2, s.f2c),
+          (1, s.sa, ksc2, lambda k: T.ps2[:, 96 * k:96 * k + 96], lambda m: T.ls[:, 96 * m:96 * m + 96], T.fs2[:], s.c2, s.f2s)])
 
     def w(k):
         return T.wq[:, 128 * k:128 * k + 128], T.ws[:, 128 * k:128 * k + 128]
-    g.tensor.wait_ge(s.sv, kwq)
+    g.tensor.wait_ge(s.sv, kc4)
     mm(T.ps[:, 512:768], *w(1), T.xq[:], T.xs[:], True, True)
     mm(T.ps[:, 1024:1280], *w(2), T.xq[:], T.xs[:], True, True)
     g.tensor.wait_ge(s.c1, 48)
@@ -374,9 +366,10 @@ def rank_program(g, core, T, topo):
     g3, s3 = T.gs3[:, 0:512], T.gs3[:, 512:1024]
     v.wait_ge(s.drow, 576)
     cp(g3, T.p3w[:].indirect(T.ul[:, 0:32]))
+    v.wait_ge(s.sa, kaw)
     vec(v.tensor_tensor_scan, s3, T.data3[:], g3, 0.0, A.mult, A.add)
     vec(v.transpose, T.tg3[:], T.gs3[:])
-    tt(T.val3[:], s3.indirect(T.offsel[:, 0:16]), T.vselk[:], A.add, free=True)
+    tt(T.val3[:], s3.indirect(T.offsel[:, 0:16]), T.vsel[:], A.add, free=True)
     tt(T.va[:], T.tg3[:, 16:32, 15], T.ac[:], A.add)
     tt(T.vb[:], T.va[:], T.tg3[:, 0:16, 15], A.mult)
     tt(T.vc[:], T.vb[:], T.trc[:], A.add)
@@ -399,7 +392,6 @@ def rank_program(g, core, T, topo):
     cp(T.qb[:], T.yy[:, :, 9], free=True)
     cp(T.qc[:], T.yy[:, :, 12], free=True)
     tt(T.x3b[:], T.x3m[:, :, 0:2], T.x3m[:, :, 2:4], A.add)
-    v.wait_ge(s.sa, kaw)
     cp(T.t1[:], T.cw[:, 0:257].indirect(T.qc[:, 0:12]), free=True)
     tt(T.x3c[:], T.x3b[:, :, 0], T.x3b[:, :, 1], A.add)
     tt(T.t2[:], T.bw[:, 0:257].indirect(T.qb[:, 0:12]), T.t1[:], A.add, free=True)
@@ -407,7 +399,7 @@ def rank_program(g, core, T, topo):
 
     g.tensor.wait_ge(s.c2, 48)
     mm(T.ps[:, 1536:1776], *w(0), T.lc[:, 0:240], T.ls[:, 0:240], True, False)
-    m3 = mm(T.ps[:, 1536:1776], *w(1), T.lc[:, 48:288], T.ls[:, 48:288], False, True)
+    m3 = mm(T.ps[:, 1536:1776], *w(1), T.lc[:, 48:288], T.ls[:, 48:288], False, True, free=True)
     v.wait_ge(s.st, m3)
     cp(T.aw[:, 401:641], T.ps[:, 1536:1776], free=True)
     ky = tt(T.yo[:], T.aw[:, 0:641].indirect(T.q0[:, 0:12]), T.t2[:], A.add)

@@ -2,6 +2,7 @@ from concourse.bass import DstId, RemoteDMATransfer
 from concourse.mybir import dt, AluOpType, ActivationFunctionType
 
 N, CAP, TX = 4, 48, 256
+LAND = 3 * CAP
 F, B, I, U = "float32", "bfloat16", "int32", "uint16"
 CODE, PLANE = "float8_e4m3fn_x4", "uint8"
 
@@ -15,32 +16,37 @@ SCRATCH = {
     "xq": _sb(CODE, 256), "xs": _sb(PLANE, 256), "cb": _sb(CODE, 400), "cbs": _sb(PLANE, 400), "wq": _sb(CODE, 384), "ws": _sb(PLANE, 384),
     "pk1": _sb(CODE, 144), "ps1": _sb(PLANE, 144), "pk2": _sb(CODE, 288), "ps2": _sb(PLANE, 288),
     "fc1": _sb(CODE, 48), "fs1": _sb(PLANE, 48), "fc2": _sb(CODE, 96), "fs2": _sb(PLANE, 96),
-    "fu": _sb(U, 8), "fn": ("dram", [128, 2], I), "lc": _sb(CODE, 288), "ls": _sb(PLANE, 288), "natl": ("dram", [8, 128, 2], I),
-    "pi": _sb(I, 1), "ic": _sb(I, 2), "col": _sb(F, 48), "iob": _sb(F, 16), "io16": _sb(F, 16), "eq": _sb(F, 16),
-    "c0w": _sb(B, 512), "ic1": _sb(B, 512), "zb": _sb(B, 512), "ones": _sb(B, 128), "offsel": _sb(U, 16), "trc": _sb(F, 16), "ac": _sb(F, 16),
-    "data0": _sb(B, 512), "data3": _sb(B, 512), "kc": _sb(F, 12, 3),
+    "fu": _sb(U, 8), "fn": ("dram", [128, 2], I), "natl": ("dram", [8, 128, 2], I),
+    "lr": _sb(CODE, 192), "lrs": _sb(PLANE, 192), "lp": _sb(CODE, 176), "lps": _sb(PLANE, 176),
+    "pi": _sb(I, 1), "ic": _sb(I, 2), "col": _sb(F, 48), "iob": _sb(F, 16), "io16": _sb(F, 16), "eq": _sb(F, 16), "eqh": _sb(F, 16),
+    "io256": _sb(B, 256), "zb": _sb(B, 512), "d01": _sb(B, 128), "offsel": _sb(U, 16), "trc": _sb(F, 16), "ac": _sb(F, 16),
+    "data0": _sb(B, 256), "data3": _sb(B, 512), "kc": _sb(F, 12, 3), "rs": _sb(F, 64),
     "stb": _sb(I, 16), "b0": _sb(I, 8), "b1": _sb(I, 8), "sx": _sb(I, 8), "sy": _sb(I, 8), "sz": _sb(I, 8), "sw": _sb(I, 8),
-    "q1l": _sb(U, 8), "p1w": _sb(I, 512), "nl": _sb(F, 128), "nd": _sb(F, 16, 16), "tn": _sb(F, 8, 32), "uf": _sb(F, 8),
-    "ul": _sb(U, 32), "win2": _sb(B, 2048), "gs1": _sb(B, 256), "tg": _sb(B, 8, 32),
-    "x1": _sb(F, 4, 4), "x1b": _sb(F, 4, 2), "x1c": _sb(F, 4), "off1": _sb(U, 4),
+    "q1l": _sb(U, 8), "qst": _sb(U, 8), "p1w": _sb(I, 512), "nl": _sb(F, 128), "nd": _sb(F, 16, 16), "tn": _sb(F, 8, 32), "uf": _sb(F, 8),
+    "ul": _sb(U, 32), "win2": _sb(B, 2048), "gg1": _sb(B, 128), "gs1": _sb(B, 128), "tg": _sb(B, 4, 32),
+    "x1": _sb(F, 16), "y1": _sb(F, 16), "off1": _sb(U, 4),
     "c0l": _sb(B, 128), "vs1": _sb(B, 64), "c0m": _sb(B, 64), "w1": _sb(B, 272),
     "d1": _sb(B, 18, 16), "td1": _sb(B, 9, 32), "l1f": _sb(F, 9), "list1": _sb(U, 10),
     "nxs": _sb(I, 32), "nxt": _sb(I, 32), "nxr": _sb(I, 16), "mk": _sb(B, 16),
-    "gs2": _sb(B, 1024), "tg2": _sb(B, 32, 32),
-    "x2": _sb(F, 16, 4), "x2b": _sb(F, 16, 2), "x2c": _sb(F, 16), "off2": _sb(U, 16),
-    "vown": _sb(B, 64), "vsel": _sb(B, 256), "w2": _sb(B, 400), "d2": _sb(B, 18, 16), "td2": _sb(B, 9, 32),
-    "h2": _sb(F, 3, 3, 4), "nf": _sb(F, 3, 2, 3), "list2": _sb(U, 18),
+    "g2": _sb(B, 512), "s2": _sb(B, 512), "tg2": _sb(B, 16, 32),
+    "x2": _sb(F, 64), "y2": _sb(F, 64), "off2": _sb(U, 16),
+    "vown": _sb(B, 64), "vsel": _sb(B, 256), "w2": _sb(B, 400), "d2": _sb(B, 18, 16), "td2": _sb(B, 3, 3, 32),
+    "nf": _sb(F, 3, 2, 3), "list2": _sb(U, 18),
     "nx4": _sb(I, 32), "nt4": _sb(I, 32), "r4": _sb(I, 16), "c4": _sb(I, 16), "mp": _sb(B, 16), "cp4": _sb(B, 16),
-    "p3w": _sb(B, 2048), "gs3": _sb(B, 1024), "tg3": _sb(B, 32, 32), "va": _sb(F, 16), "vb": _sb(F, 16), "vc": _sb(F, 16), "off3": _sb(U, 16),
-    "val3": _sb(B, 256), "w3": _sb(B, 448),
+    "p3w": _sb(B, 2048), "g3": _sb(B, 512), "s3": _sb(B, 512), "tg3": _sb(B, 16, 32), "e3": _sb(F, 32), "f3": _sb(F, 32), "y3": _sb(F, 32),
+    "off3": _sb(U, 16), "val3": _sb(B, 256), "w3": _sb(B, 448),
     "t3": _sb(B, 6, 32), "c3": _sb(B, 6, 32), "pl": _sb(B, 192), "idl": _sb(F, 192),
-    "dp": _sb(B, 24, 16), "tp": _sb(B, 12, 32), "yy": _sb(F, 12, 15),
-    "x3": _sb(F, 12, 4), "x3m": _sb(F, 12, 4), "x3b": _sb(F, 12, 2), "x3c": _sb(F, 12), "q0": _sb(U, 12), "qb": _sb(U, 12), "qc": _sb(U, 12),
-    "ps": ("psum", [128, 2048], F), "aw": _sb(F, 648), "bw": _sb(F, 264), "cw": _sb(F, 264),
+    "dp": _sb(B, 24, 16), "tp": _sb(B, 12, 32), "yy": _sb(F, 12, 13),
+    "x3": _sb(F, 12, 4), "x3m": _sb(F, 48), "y4": _sb(F, 48), "q0": _sb(U, 12), "qb": _sb(U, 12), "qc": _sb(U, 12),
+    "ps": ("psum", [128, 2560], F), "aw": _sb(F, 600), "bw": _sb(F, 264), "cw": _sb(F, 264),
     "t1": _sb(F, 192), "t2": _sb(F, 192), "yo": _sb(F, 192),
 }
-SEMAPHORES = ["sv", "sa", "st", "g0", "g1", "g2", "g3", "dsb", "dnx", "dns", "dn4", "dx", "dw", "dnat", "dmk", "drow", "dy", "did",
-              "m0", "m1", "c1", "c2", "loc", "f0", "f1", "f1c", "f1s", "f2c", "f2s"]
+SEMAPHORES = ["sv", "su", "so", "sz", "sa", "sb", "sk", "sp", "st", "g0", "g1", "g2", "g3", "g4", "dsb", "dnx", "dns", "dn4", "dx", "dw", "dnat",
+              "dmk", "dcb", "drow", "dz", "dy", "did", "m0", "m1", "c1", "c2", "c2p", "loc", "f0", "f1", "f1c", "f1s", "f2c", "f2s"]
+
+
+def order(topo, cores, r):
+    return sorted([k for k in range(N) if k != r], key=lambda k: topo.may_write(cores[r], cores[k]))
 
 
 def forwarders(topo, src, dst):
@@ -58,18 +64,18 @@ def hand_on(g, core, T, topo):
             if i == j or topo.may_write(src, dst) or core not in forwarders(topo, src, dst):
                 continue
             h = forwarders(topo, src, dst).index(core)
-            k = [r for r in range(N) if r != j].index(i)
+            k = order(topo, T.cores, j).index(i)
             rid, pid = topo.addr(dst, core)
             e = topo.engines(core, dst)
             s = T.sem
             jobs = [(s.f0, 4, T.natl[2 * i + h], T.fn[:], s.m0)]
             if h:
                 jobs += [(s.f1, 8, T.ul[:, 8 * i:8 * i + 8], T.fu[:], s.m1),
-                         (s.f1s, 8, T.cbs[:, TX + CAP * k:TX + CAP * k + CAP], T.fs1[:], s.c1),
-                         (s.f2s, 8, T.ls[:, 96 * k:96 * k + 96], T.fs2[:], s.c2)]
+                         (s.f1s, 8, T.cbs[:, CAP * k:CAP * k + CAP], T.fs1[:], s.c1),
+                         (s.f2s, 8, T.lrs[:, 96 * k:96 * k + 96], T.fs2[:], s.c2)]
             else:
-                jobs += [(s.f1c, 8, T.cb[:, TX + CAP * k:TX + CAP * k + CAP].bitcast(dt.uint8), T.fc1[:].bitcast(dt.uint8), s.c1),
-                         (s.f2c, 8, T.lc[:, 96 * k:96 * k + 96].bitcast(dt.uint8), T.fc2[:].bitcast(dt.uint8), s.c2)]
+                jobs += [(s.f1c, 8, T.cb[:, CAP * k:CAP * k + CAP].bitcast(dt.uint8), T.fc1[:].bitcast(dt.uint8), s.c1),
+                         (s.f2c, 8, T.lr[:, 96 * k:96 * k + 96].bitcast(dt.uint8), T.fc2[:].bitcast(dt.uint8), s.c2)]
             for sem, n, out, in_, to in jobs:
                 g.wait_ge(sem, n)
                 g.remote_dma(out, in_, to, s.loc, pid, rid, mask_of(e))
@@ -82,47 +88,52 @@ def rank_program(g, core, T, topo):
         hand_on(g, core, T, topo)
         return
     A, C = AluOpType, ActivationFunctionType
-    others = [r for r in range(N) if r != me]
+    others = order(topo, T.cores, me)
     s, v, a = T.sem, g.vector, g.scalar
-    cnt = {"v": 0, "a": 0, "t": 0, "loc": 0}
+    cnt = {}
+    known = {}
 
-    def vec(f, *args, free=False):
-        if cnt["v"] and not free:
-            v.wait_ge(s.sv, cnt["v"])
-        f(*args).then_inc(s.sv, 1)
-        cnt["v"] += 1
-        return cnt["v"]
+    def wait(q, name, sem, n):
+        if known.get((name, sem), 0) < n:
+            q.wait_ge(s[sem], n)
+            known[(name, sem)] = n
 
-    def act(out, in_, func=C.Identity, free=False, **kw):
-        if cnt["a"] and not free:
-            a.wait_ge(s.sa, cnt["a"])
-        a.activation(out, in_, func, **kw).then_inc(s.sa, 1)
-        cnt["a"] += 1
-        return cnt["a"]
+    def put(q, name, chain, free, after, f, *args, **kw):
+        for sem, n in after:
+            wait(q, name, sem, n)
+        if not free:
+            wait(q, name, chain, cnt.get(chain, 0))
+        f(*args, **kw).then_inc(s[chain], 1)
+        cnt[chain] = cnt.get(chain, 0) + 1
+        return (chain, cnt[chain])
 
-    def mm(*args, free=False):
-        if cnt["t"] and not free:
-            g.tensor.wait_ge(s.st, cnt["t"])
-        g.tensor.matmul_mx(*args).then_inc(s.st, 1)
-        cnt["t"] += 1
-        return cnt["t"]
+    def vec(f, *args, free=False, on="sv", after=()):
+        return put(v, "v", on, free, after, f, *args)
 
-    def ts(out, in_, s1, op0, s2=None, op1=None, free=False):
+    def act(out, in_, func=C.Identity, free=False, on="sk", after=(), **kw):
+        return put(a, "a", on, free, after, a.activation, out, in_, func, **kw)
+
+    def mm(*args, free=False, after=()):
+        return put(g.tensor, "t", "st", free, after, g.tensor.matmul_mx, *args)
+
+    def ts(out, in_, s1, op0, s2=None, op1=None, **kw):
         if op1 is None:
-            return vec(v.tensor_scalar, out, in_, s1, None, op0, free=free)
-        return vec(v.tensor_scalar, out, in_, s1, s2, op0, op1, free=free)
+            return vec(v.tensor_scalar, out, in_, s1, None, op0, **kw)
+        return vec(v.tensor_scalar, out, in_, s1, s2, op0, op1, **kw)
 
-    def tt(out, x, y, op, free=False):
-        return vec(v.tensor_tensor, out, x, y, op, free=free)
+    def tt(out, x, y, op, **kw):
+        return vec(v.tensor_tensor, out, x, y, op, **kw)
 
-    def cp(out, in_, free=False):
-        return vec(v.tensor_copy, out, in_, free=free)
+    def cp(out, in_, **kw):
+        return vec(v.tensor_copy, out, in_, **kw)
 
-    def fill(out, x, free=True):
-        return vec(v.memset, out, x, free=free)
+    def fill(out, x, free=True, on="so"):
+        return vec(v.memset, out, x, free=free, on=on)
 
-    rest = [k for k, r in enumerate(others) if not topo.may_write(core, T.cores[r])]
-    peer = [k for k in range(N - 1) if k not in rest]
+    def scan(out, d0, d1, init, **kw):
+        return vec(v.tensor_tensor_scan, out, d0, d1, init, A.mult, A.add, **kw)
+
+    rest, peer = [0, 1], 2
 
     def call(items):
         tr = []
@@ -131,24 +142,23 @@ def rank_program(g, core, T, topo):
             h = len(e) // of
             rid, pid = topo.addr(d, core)
             tr.append(RemoteDMATransfer(dst_ids=[DstId(rid=rid, pnc=pid)], dma_engine_mask=mask_of(e[n * h:n * h + h]), remote_sem=sem, src=src, dst=dst))
-            cnt["loc"] += h
+            cnt["loc"] = cnt.get("loc", 0) + h
         g.remote_dma_fused(tr, local_sem=s.loc)
 
-    def send(msgs):
-        for h, sem, n, src, far, near, far_sem, near_sem in msgs:
-            g.wait_ge(sem, n)
-            call([(forwarders(topo, core, T.cores[others[k]])[h], n, len(rest), near_sem, src(k), near) for n, k in enumerate(rest)])
-        for h, sem, n, src, far, near, far_sem, near_sem in msgs:
-            for k in peer:
-                mine = [q for q in range(N) if q != others[k]].index(me)
-                call([(T.cores[others[k]], 0, 1, far_sem, src(k), far(mine))])
+    def to_rest(h, after, sem, src, dst):
+        wait(g, "g", *after)
+        call([(forwarders(topo, core, T.cores[others[k]])[h], k, len(rest), sem, src(k), dst) for k in rest])
+
+    def to_peer(after, sem, src, dst):
+        wait(g, "g", *after)
+        call([(T.cores[others[peer]], 0, 1, sem, src(peer), dst)])
 
     col = {}
 
     def new(name, n=1):
         assert name not in col
         at = sum(col[k][1] for k in col)
-        col[name] = (T.col[:, at:at + n], n)
+        col[name] = (T.col[:, at:at + n], n, at)
         return col[name][0]
 
     def c(name):
@@ -161,253 +171,272 @@ def rank_program(g, core, T, topo):
     for q in range(8):
         g.sync.dma_start(T.stb[16 * q:16 * q + 16, 0:8], T.st[:]).then_inc(s.dsb, 16)
         a.dma_start(T.stb[16 * q:16 * q + 16, 8:16], T.bt[:]).then_inc(s.dsb, 16)
-    k = fill(T.p1w[:], 0)
+    k = fill(T.p1w[:], 0, on="sz")
     for q in range(4):
-        e = g.sync if q % 2 else a
-        e.wait_ge(s.sv, k)
+        e, n = (g.sync, "s") if q % 2 else (a, "a")
+        wait(e, n, *k)
         e.dma_start(T.p1w[32 * q:32 * q + 1, :], T.nx[:]).then_inc(s.dnx, 16)
-    a.dma_start(T.xb[:], T.x[:]).then_inc(s.dx, 16)
-    fill(T.nxs[:], 0, free=False)
-    k = fill(T.nx4[:], 0)
-    g.sync.wait_ge(s.sv, k)
+    kz = fill(T.zb[:], 0.0, on="sp")
+    fill(T.nxs[:], 0, free=False, on="sz")
+    k = fill(T.nx4[:], 0, on="sz")
+    wait(g.sync, "s", *k)
     for q in range(4):
         g.sync.dma_start(T.nxs[32 * q:32 * q + 16, :], T.nx[:]).then_inc(s.dns, 16)
+    a.dma_start(T.xb[:], T.x[:]).then_inc(s.dx, 16)
     g.sync.dma_start(T.nx4[32 * me:32 * me + 16, :], T.nx[:]).then_inc(s.dn4, 16)
-    g.sync.dma_start(T.wb[:], T.w[:]).then_inc(s.dw, 16)
+    wait(g.sync, "s", *kz)
+    for r in range(4):
+        g.sync.dma_start(T.p3w[:, 512 * r:512 * r + 512], T.zb[:]).then_inc(s.dz, 16)
 
     def iota(out, pattern, sem, base=0):
         g.iota(out, pattern, base, 0, allow_small_or_imprecise_dtypes=True).then_inc(sem, 1)
     g.iota(T.pi[:], [[0, 1]], 0, 1).then_inc(s.g0, 1)
     iota(T.io16[:], [[1, 16]], s.g3)
     iota(T.iob[:], [[32, 16]], s.g3)
-    iota(T.c0w[:], [[1, 8], [0, 2], [8, 32]], s.g2)
-    iota(T.ic1[:], [[1, 256], [0, 2]], s.g1, 1)
+    iota(T.io256[:], [[1, 256]], s.g1, 1)
     g.wait_ge(s.dnat, 16)
-    call([(forwarders(topo, core, T.cores[others[k]])[h], 2 * n + h, 2 * len(rest), s.f0, T.natl[2 * me + h], T.fn[:])
-          for n, k in enumerate(rest) for h in (0, 1)])
-    for k in peer:
-        call([(T.cores[others[k]], h, 2, s.m0, T.natl[2 * me + h], T.natl[2 * me + h]) for h in (0, 1)])
+    call([(forwarders(topo, core, T.cores[others[k]])[h], 2 * k + h, 2 * len(rest), s.f0, T.natl[2 * me + h], T.fn[:]) for k in rest for h in (0, 1)])
+    call([(T.cores[others[peer]], h, 2, s.m0, T.natl[2 * me + h], T.natl[2 * me + h]) for h in (0, 1)])
 
-    fill(T.zb[:], 0.0, free=False)
-    v.wait_ge(s.g0, 1)
-    ts(T.ic[:, 0:1], T.pi[:], 15, A.bitwise_and)
+    wait(v, "v", "g0", 1)
+    ts(T.ic[:, 0:1], T.pi[:], 15, A.bitwise_and, free=True)
     ts(T.ic[:, 1:2], T.pi[:], 31, A.bitwise_and, free=True)
     cp(new("q", 2), T.ic[:])
     q16, q32 = T.col[:, 0:1], T.col[:, 1:2]
-    v.wait_ge(s.g3, 2)
-    ke = ts(T.eq[:], T.io16[:], q16, A.is_equal)
-    ts(T.offsel[:], T.iob[:], q32, A.add)
-    fill(T.ones[:], 1.0)
-    fill(T.w1[:], 0.0)
-    a.wait_ge(s.sv, ke)
-    act(new("v", 3), eq(4, 3), bias=eq(3))
-    act(new("vme"), eq(7), bias=eq(8), free=True)
+    wait(v, "v", "g3", 2)
+    ts(T.eq[:], T.io16[:], q16, A.is_equal)
+    ts(T.eqh[:], T.io16[:], q32, A.is_equal, free=True)
+    ke = ts(new("even"), q32, 16.0, A.is_lt, free=True)
+    fill(T.rs[:], 1.0)
+    fill(T.w1[:, 128:272], 0.0)
+    ko = ts(T.offsel[:], T.iob[:], q32, A.add, on="sp")
+    fill(T.f3[:], 0.0)
+    kfill = fill(T.rs[:, 0:64:4], 0.0, free=False)
+    wait(a, "a", *ke)
+    wait(a, "a", *kz)
+    act(new("z3"), eq(3), bias=eq(14), free=True)
+    act(new("z7"), eq(7), bias=eq(14), free=True)
     act(new("u1"), q16, scale=48.0, bias=-193.0, free=True)
-    act(new("init1"), eq(7), scale=-272.0, bias=c("u1"))
+    act(T.d01[:], T.zb[:, 0:128], bias=c("even"), free=True)
+    act(new("v", 3), eq(4, 3), bias=c("z3"))
+    act(new("vme"), eq(8), bias=c("z7"), free=True)
+    act(new("init1"), eq(7), scale=-272.0, bias=c("u1"), free=True)
+    v0 = col["v"][2]
     for k in range(3):
-        act(T.win2[:, 512 * others[k]:512 * others[k] + 512], T.zb[:], bias=T.col[:, 2 + k:3 + k], free=True)
-    a.wait_ge(s.g1, 1)
-    kw = act(T.win2[:, 512 * me:512 * me + 512], T.ic1[:], scale=eq(9), bias=c("vme"), free=True)
+        act(T.win2[:, 512 * others[k]:512 * others[k] + 512], T.zb[:], bias=T.col[:, v0 + k:v0 + k + 1], free=k > 0)
+    wait(a, "a", "g1", 1)
+    for h in range(2):
+        kw = act(T.win2[:, 512 * me + h:512 * me + 512:2], T.io256[:], scale=eq(9), bias=c("vme"), free=True)
 
-    v.wait_ge(s.dsb, 256)
+    wait(v, "v", "dsb", 256)
     ts(T.b0[:], T.stb[:, 8:16], 1, A.bitwise_and)
     ts(T.sx[:], T.stb[:, 0:8], 513.0, A.mult, free=True)
-    ts(T.b1[:], T.stb[:, 8:16], 1, A.logical_shift_right, free=True)
     ts(T.sy[:], T.b0[:], 256.0, A.mult)
+    kq = cp(T.qst[:], T.stb[:, 0:8], on="sp")
     tt(T.sz[:], T.sx[:], T.sy[:], A.add)
+    ts(T.b1[:], T.stb[:, 8:16], 1, A.logical_shift_right, free=True, on="su")
     ts(T.sw[:], T.sz[:], 3, A.logical_shift_right, 511, A.bitwise_and)
-    kq = cp(T.q1l[:], T.sw[:])
-    a.wait_ge(s.sv, kq)
-    a.wait_ge(s.g2, 1)
-    act(T.c0l[:], T.c0w[:].indirect(T.q1l[:, 0:8]), C.Copy)
-    kvs1 = act(T.vs1[:], T.c0l[:].indirect(T.offsel[:, 0:4]), C.Copy)
-    v.wait_ge(s.dnx, 64)
+    cp(T.q1l[:], T.sw[:])
+    wait(v, "v", "dnx", 64)
     ts(T.nl[:], T.p1w[:].indirect(T.q1l[:, 0:8]), 2.0, A.mult)
     cp(T.nd[:, 0:16:2, :], T.nl[:])
     cp(T.nd[:, 1:16:2, :], T.nl[:], free=True)
     vec(v.transpose, T.tn[:], T.nd[:])
-    tt(T.uf[:], T.tn[:, :, 0], T.b1[:], A.add)
+    tt(T.uf[:], T.tn[:, :, 0], T.b1[:], A.add, after=[("su", cnt["su"])])
     ku = cp(T.ul[:, 8 * me:8 * me + 8], T.uf[:])
-    send([(1, s.sv, ku, lambda k: T.ul[:, 8 * me:8 * me + 8], lambda m: T.ul[:, 8 * me:8 * me + 8], T.fu[:], s.m1, s.f1)])
+    mine = T.ul[:, 8 * me:8 * me + 8]
+    to_rest(1, ku, s.f1, lambda k: mine, T.fu[:])
+    to_peer(ku, s.m1, lambda k: mine, mine)
+    iota(T.w2[:, 256:400], [[0, 144]], s.g2)
 
-    act(new("l1"), eq(0), bias=eq(1))
-    act(new("l2"), eq(2), bias=c("l1"))
-    act(new("keep"), eq(8), bias=c("l2"))
-    act(new("nzt"), c("l2"), scale=-1.0, bias=1.0, free=True)
+    act(T.c0l[:], T.io256[:].indirect(T.qst[:, 0:8]), C.Copy, free=True, on="sa", after=[kq])
+    kvs1 = act(T.vs1[:], T.c0l[:].indirect(T.offsel[:, 0:4]), C.Copy, on="sa", after=[ko])
+    act(new("lh1"), T.eqh[:, 0:1], bias=T.eqh[:, 1:2])
+    act(new("l1"), eq(0), bias=eq(1), free=True)
     act(new("init2"), q16, scale=48.0, bias=-1.0, free=True)
-    for r in range(N):
-        act(new("t%d" % r), eq(10), C.Copy, scale=float(TX + CAP * others.index(r) if r != me else 0), free=True)
+    act(new("nt"), eq(3), scale=-1.0, bias=1.0, free=True)
+    for k in range(3):
+        act(new("t%d" % k), eq(8), C.Copy, scale=float(CAP * k - LAND), free=True)
     act(new("q16m"), q16, bias=-256.0, free=True)
-    for r in range(N):
-        act(new("b%d" % r), eq(13), scale=r + 1.0, bias=c("t%d" % r), free=r > 0)
-        act(T.data0[:, 128 * r:128 * r + 128], T.zb[:, 0:128], bias=c("l2") if r == me else c("keep"), free=True)
-    act(new("nz"), eq(3), scale=-1.0, bias=c("nzt"), free=True)
+    act(new("b%d" % me), eq(13), C.Copy, scale=me + 1.0, free=True)
+    act(new("l2h"), T.eqh[:, 2:3], bias=c("lh1"))
+    act(new("l2"), eq(2), bias=c("l1"), free=True)
+    for k in range(3):
+        act(new("b%d" % others[k]), eq(13), scale=others[k] + 1.0, bias=c("t%d" % k), free=True)
     act(T.trc[:], T.iob[:], scale=0.5, bias=c("q16m"), free=True)
-    act(T.w2[:], T.zb[:, 0:400], C.Copy, free=True)
-    act(T.data0[:, 0:512:128], T.zb[:, 0:4], bias=c("l2"))
-    kw2 = act(T.c0m[:], T.vs1[:], scale=eq(10), bias=c("b%d" % me), free=True)
+    act(T.c0m[:], T.vs1[:], scale=eq(8), bias=c("b%d" % me), free=True, after=[kvs1])
+    act(new("k8"), eq(8), bias=eq(14), free=True)
+    act(new("keep"), c("k8"), bias=c("l2h"))
+    act(new("nz"), c("l2"), scale=-1.0, bias=c("nt"), free=True)
+    act(T.data0[:], T.zb[:, 0:256], bias=c("keep"))
+    act(new("nz8"), eq(8), scale=-1.0, bias=c("nz"), free=True)
+    kw2 = act(T.data0[:, 0:256:128], T.zb[:, 0:2], bias=c("l2h"))
+    act(T.ac[:], T.trc[:], scale=-1.0, bias=-1.0, free=True, on="sb")
+    act(T.e3[:, 1:32:2], T.trc[:], C.Copy, free=True, on="sb")
+    act(new("kp"), T.eqh[:, 15:16], bias=c("l2"), free=True, on="sb")
+    k3 = act(T.data3[:], T.zb[:], bias=c("kp"), on="sb")
 
-    v.wait_ge(s.sa, kw)
-    cp(T.gs1[:, 0:128], T.win2[:].indirect(T.ul[:, 8 * me:8 * me + 8]))
-    vec(v.tensor_tensor_scan, T.gs1[:, 128:256], T.ones[:], T.gs1[:, 0:128], c("init1"), A.mult, A.add)
+    vec(v.transpose, T.nxt[:], T.nxs[:], free=True, on="su", after=[("dns", 64)])
+    kg1 = cp(T.gg1[:], T.win2[:].indirect(mine), after=[kw])
+    ts(T.nxr[:], T.nxt[:, 0:16], 8, A.logical_shift_right, on="su")
+    scan(T.gs1[:], T.d01[:], T.gg1[:], c("init1"))
+    for r in range(4):
+        km = ts(T.mk[32 * r:32 * r + 32, :], T.nxr[32 * r:32 * r + 32, :], float(others[r] if r < 3 else me), A.is_equal, free=r > 0, on="su")
     vec(v.transpose, T.tg[:], T.gs1[:])
-    tt(T.x1[:], T.tg[:, 0:4, 4:8], T.tg[:, 4:8, 4:8], A.mult)
-    v.wait_ge(s.dx, 16)
-    vec(v.quantize_mx, T.xq[:], T.xs[:], T.xb[:], free=True)
-    tt(T.x1b[:], T.x1[:, :, 0:2], T.x1[:, :, 2:4], A.add)
-    tt(T.x1c[:], T.x1b[:, :, 0], T.x1b[:, :, 1], A.add)
-    ts(T.off1[:], T.x1c[:], 128.0, A.add)
-    v.wait_ge(s.sa, kvs1)
-    cp(T.w1[:].indirect(T.off1[:, 0:4]), T.vs1[:])
+    tt(T.x1[:], T.tg[:, :, 4:8], T.tg[:, :, 20:24], A.mult)
+    kxq = vec(v.quantize_mx, T.xq[:], T.xs[:], T.xb[:], free=True, on="sz", after=[("dx", 16)])
+    scan(T.y1[:], T.rs[:, 0:16], T.x1[:], 0.0, after=[kfill])
+    ts(T.off1[:], T.y1[:, 3:16:4], 128.0, A.add)
+    cp(T.w1[:].indirect(T.off1[:, 0:4]), T.vs1[:], after=[kvs1])
     cp(T.d1[:, 0:18:2, :], T.w1[:, 128:272])
     cp(T.d1[:, 1:18:2, :], T.w1[:, 128:272], free=True)
     vec(v.transpose, T.td1[:], T.d1[:])
     tt(T.l1f[:], T.td1[:, :, 0], T.td1[:, :, 16], A.add)
-    kl = cp(T.list1[:, 0:9], T.l1f[:])
-    a.wait_ge(s.sv, kl)
-    ksc = act(T.ps1[:], T.xs[:].indirect(T.list1[:, 0:9]), C.Copy)
-    kpk = cp(T.pk1[:].bitcast(dt.uint32), T.xq[:].bitcast(dt.uint32).indirect(T.list1[:, 0:9]))
-    send([(0, s.sv, kpk, lambda k: T.pk1[:, CAP * k:CAP * k + CAP].bitcast(dt.uint8), lambda m: T.cb[:, TX + CAP * m:TX + CAP * m + CAP].bitcast(dt.uint8),
-           T.fc1[:].bitcast(dt.uint8), s.c1, s.f1c),
-          (1, s.sa, ksc, lambda k: T.ps1[:, CAP * k:CAP * k + CAP], lambda m: T.cbs[:, TX + CAP * m:TX + CAP * m + CAP], T.fs1[:], s.c1, s.f1s)])
+    kl = ts(T.list1[:, 0:9], T.l1f[:], -1.0, A.add)
+    kpk = cp(T.pk1[:].bitcast(dt.uint32), T.xq[:].bitcast(dt.uint32).indirect(T.list1[:, 0:9]), after=[kxq])
+    ksc = act(T.ps1[:], T.xs[:].indirect(T.list1[:, 0:9]), C.Copy, on="sa", after=[kl, kxq])
+    at = order(topo, T.cores, others[peer]).index(me)
+    to_rest(0, kpk, s.f1c, lambda k: T.pk1[:, CAP * k:CAP * k + CAP].bitcast(dt.uint8), T.fc1[:].bitcast(dt.uint8))
+    to_rest(1, ksc, s.f1s, lambda k: T.ps1[:, CAP * k:CAP * k + CAP], T.fs1[:])
+    to_peer(kpk, s.c1, lambda k: T.pk1[:, CAP * k:CAP * k + CAP].bitcast(dt.uint8), T.cb[:, CAP * at:CAP * at + CAP].bitcast(dt.uint8))
+    to_peer(ksc, s.c1, lambda k: T.ps1[:, CAP * k:CAP * k + CAP], T.cbs[:, CAP * at:CAP * at + CAP])
+    iota(T.w3[:, 256:448], [[0, 192]], s.g4)
+    iota(T.c3[:], [[0, 192]], s.g4)
 
-    v.wait_ge(s.dns, 64)
-    vec(v.transpose, T.nxt[:], T.nxs[:])
-    ts(T.nxr[:], T.nxt[:, 0:16], 8, A.logical_shift_right)
-    for r in range(4):
-        km = ts(T.mk[32 * r:32 * r + 32, :], T.nxr[32 * r:32 * r + 32, :], float(others[r] if r < 3 else me), A.is_equal, free=r > 0)
-    g.sync.wait_ge(s.sv, km)
-    for b in range(4):
-        g.sync.dma_start(T.win2[32 * b:32 * b + 4, 512 * me:512 * me + 512], T.mk[:]).then_inc(s.dmk, 16)
+    wait(g.sync, "s", *km)
+    wait(g.sync, "s", *kg1)
+    for b in range(0, 128, 32):
+        g.sync.dma_start(T.win2[b:b + 4, 512 * me:512 * me + 512], T.mk[:]).then_inc(s.dmk, 16)
+        g.sync.dma_start(T.win2[b + 16:b + 19, 512 * me:512 * me + 512], T.mk[0:96, :]).then_inc(s.dmk, 16)
+    g.sync.dma_start(T.wb[:], T.w[:]).then_inc(s.dw, 16)
     g.sync.wait_ge(s.m0, 40)
     for r in others:
         g.sync.dma_start(T.nx4[32 * r:32 * r + 16, :], T.natl[2 * r:2 * r + 2]).then_inc(s.dn4, 16)
-    vec(v.quantize_mx, T.cb[:, 0:TX], T.cbs[:, 0:TX], T.xb[:])
-    v.wait_ge(s.dw, 16)
-    vec(v.quantize_mx, T.wq[:], T.ws[:], T.wb[:], free=True)
-    v.wait_ge(s.dn4, 64)
-    vec(v.transpose, T.nt4[:], T.nx4[:], free=True)
-    ts(T.r4[:], T.nt4[:, 0:16], 8, A.logical_shift_right)
-    ts(T.c4[:], T.nt4[:, 0:16], 255, A.bitwise_and, free=True)
-    ts(T.mp[:], T.r4[:], float(me), A.is_equal)
-    kc4 = ts(T.cp4[:], T.c4[:], 1.0, A.add, free=True)
+    wait(g.sync, "s", *kxq)
+    g.sync.dma_start(T.cb[:, LAND:LAND + TX].bitcast(dt.uint8), T.xq[:].bitcast(dt.uint8)).then_inc(s.dcb, 16)
+    g.sync.dma_start(T.cbs[:, LAND:LAND + TX], T.xs[:]).then_inc(s.dcb, 16)
+    g.sync.dma_start(T.lp[:, 96:176].bitcast(dt.uint8), T.xq[:, 0:80].bitcast(dt.uint8)).then_inc(s.dcb, 16)
+    g.sync.dma_start(T.lps[:, 96:176], T.xs[:, 0:80]).then_inc(s.dcb, 16)
+    vec(v.transpose, T.nt4[:], T.nx4[:], free=True, on="su", after=[("dn4", 64)])
+    ts(T.r4[:], T.nt4[:, 0:16], 8, A.logical_shift_right, on="su")
+    ts(T.c4[:], T.nt4[:, 0:16], 255, A.bitwise_and, free=True, on="su")
+    ts(T.mp[:], T.r4[:], float(me), A.is_equal, on="su")
+    kc4 = ts(T.cp4[:], T.c4[:], 1.0, A.add, free=True, on="su")
 
-    for r in range(4):
-        kp3 = act(T.p3w[:, 512 * r:512 * r + 512], T.zb[:], bias=eq(14), free=r > 0)
-    act(new("kp"), eq(15), bias=c("l2"))
-    act(T.ac[:], T.trc[:], scale=-1.0, bias=-1.0, free=True)
-    act(T.w3[:], T.zb[:, 0:448], C.Copy, free=True)
-    act(T.c3[:], T.zb[:, 0:192], C.Copy, free=True)
-    for x in (T.aw, T.bw, T.cw):
-        act(x[:, 0:1], T.zb[:, 0:1], C.Copy, free=True)
-    for k in range(3):
-        act(T.kc[:, :, k], T.zb[:, 0:12], bias=400.0 + 96.0 * k, free=True)
-    act(new("keep3"), eq(14), bias=c("kp"))
-    act(T.data3[:], T.zb[:], bias=c("keep3"))
-    act(T.data3[:, 0:512:128], T.zb[:, 0:4], bias=c("kp"))
-
-    g.sync.wait_ge(s.sv, kc4)
-    g.sync.wait_ge(s.sa, kp3)
-    for b in range(0, 128, 32):
+    wait(g.sync, "s", *kc4)
+    wait(g.sync, "s", "dz", 64)
+    for b in range(0, 128, 16):
         g.sync.dma_start(T.p3w[b + 15:b + 16, :], T.mp[:]).then_inc(s.drow, 16)
-        for h in (0, 16):
-            g.sync.dma_start(T.p3w[b + h + 12:b + h + 13, :], T.cp4[:]).then_inc(s.drow, 16)
-            for k, r in enumerate(others):
-                g.sync.dma_start(T.p3w[b + h + k:b + h + k + 1, 512 * r:512 * r + 512], T.mp[32 * r:32 * r + 32, :]).then_inc(s.drow, 16)
+        g.sync.dma_start(T.p3w[b + 12:b + 13, :], T.cp4[:]).then_inc(s.drow, 16)
+        for k, r in enumerate(others):
+            g.sync.dma_start(T.p3w[b + k:b + k + 1, 512 * r:512 * r + 512], T.mp[32 * r:32 * r + 32, :]).then_inc(s.drow, 16)
 
-    g2, s2 = T.gs2[:, 0:512], T.gs2[:, 512:1024]
-    v.wait_ge(s.m1, 24)
-    v.wait_ge(s.dmk, 64)
-    v.wait_ge(s.sa, kw2)
-    cp(g2, T.win2[:].indirect(T.ul[:, 0:32]))
-    ks2 = vec(v.tensor_tensor_scan, s2, T.data0[:], g2, c("init2"), A.mult, A.add)
-    a.wait_ge(s.sv, ks2)
-    kvo = act(T.vown[:], s2.indirect(T.offsel[:, 4 * me:4 * me + 4]), C.Copy, scale=c("nz"))
-    for n, r in enumerate(others):
-        kvsel = act(T.vsel[:, 64 * r:64 * r + 64], s2.indirect(T.offsel[:, 4 * r:4 * r + 4]), scale=c("nz"), bias=c("b%d" % r), free=n > 0)
-    vec(v.transpose, T.tg2[:], T.gs2[:])
-    v.wait_ge(s.sa, kvo)
-    tt(T.vsel[:, 64 * me:64 * me + 64], T.vown[:], T.c0m[:], A.add, free=True)
-    tt(T.x2[:, :, 3], T.tg2[:, 0:16, 3], T.trc[:], A.mult)
-    tt(T.x2[:, :, 0:3], T.tg2[:, 0:16, 0:3], T.tg2[:, 16:32, 0:3], A.mult, free=True)
-    tt(T.x2b[:], T.x2[:, :, 0:2], T.x2[:, :, 2:4], A.add)
-    tt(T.x2c[:], T.x2b[:, :, 0], T.x2b[:, :, 1], A.add)
-    ts(T.off2[:], T.x2c[:], 256.0, A.add)
-    v.wait_ge(s.sa, kvsel)
-    cp(T.w2[:].indirect(T.off2[:, 0:16]), T.vsel[:])
+    wait(a, "a", "m1", 24)
+    wait(a, "a", "dmk", 128)
+    kgb = act(T.g2[:, 256:512], T.win2[:].indirect(T.ul[:, 16:32]), C.Copy, on="sa")
+    wait(v, "v", "m1", 24)
+    wait(v, "v", "dmk", 128)
+    wait(v, "v", *kw2)
+    cp(T.g2[:, 0:256], T.win2[:].indirect(T.ul[:, 0:16]))
+    ksA = scan(T.s2[:, 0:256], T.data0[:], T.g2[:, 0:256], c("init2"))
+    ksB = scan(T.s2[:, 256:512], T.data0[:], T.g2[:, 256:512], T.s2[:, 255:256], after=[kgb])
+    vec(v.transpose, T.tg2[:, 0:8, :], T.s2[:, 0:256], free=True, on="sz")
+    vec(v.transpose, T.tg2[:, 8:16, :], T.s2[:, 256:512], free=True, on="sz", after=[ksB])
+    for n, r in enumerate(sorted(range(4), key=lambda r: (r >= 2, r != me))):
+        kvsel = act(T.vown[:] if r == me else T.vsel[:, 64 * r:64 * r + 64], T.s2[:, 128 * r:128 * r + 128].indirect(T.offsel[:, 0:4]), free=n > 0, on="sa",
+                    after=[ksB if r >= 2 else ksA], scale=c("nz8" if r == me else "nz"), **({} if r == me else {"bias": c("b%d" % r)}))
+    tt(T.x2[:, 3:64:4], T.tg2[:, :, 3], T.trc[:], A.mult, on="sz")
+    for k in range(3):
+        tt(T.x2[:, k:64:4], T.tg2[:, :, k], T.tg2[:, :, 16 + k], A.mult, free=True, on="sz")
+    scan(T.y2[:], T.rs[:], T.x2[:], 0.0, on="sz")
+    tt(T.vsel[:, 64 * me:64 * me + 64], T.vown[:], T.c0m[:], A.add, free=True, after=[kvsel])
+    ts(T.off2[:], T.y2[:, 3:64:4], 256.0, A.add, on="sz")
+    wait(v, "v", "g2", 1)
+    cp(T.w2[:].indirect(T.off2[:, 0:16]), T.vsel[:], after=[("sz", cnt["sz"])])
     cp(T.d2[:, 0:18:2, :], T.w2[:, 256:400])
     cp(T.d2[:, 1:18:2, :], T.w2[:, 256:400], free=True)
     vec(v.transpose, T.td2[:], T.d2[:])
-    tt(T.h2[:], T.td2[:, :, 8:12], T.td2[:, :, 24:28], A.add)
-    tt(T.nf[:, :, 0, :], T.h2[:, :, :, 0], T.h2[:, :, :, 2], A.add)
-    tt(T.nf[:, :, 1, :], T.h2[:, :, :, 1], T.h2[:, :, :, 3], A.add, free=True)
-    kl2 = ts(T.list2[:], T.nf[:], -1.0, A.add)
-    a.wait_ge(s.sv, kl2)
-    a.wait_ge(s.c1, 48)
-    ksc2 = act(T.ps2[:], T.cbs[:].indirect(T.list2[:, 0:18]), C.Copy)
-    v.wait_ge(s.c1, 48)
-    kpk2 = cp(T.pk2[:].bitcast(dt.uint32), T.cb[:].bitcast(dt.uint32).indirect(T.list2[:, 0:18]))
-    send([(0, s.sv, kpk2, lambda k: T.pk2[:, 96 * k:96 * k + 96].bitcast(dt.uint8), lambda m: T.lc[:, 96 * m:96 * m + 96].bitcast(dt.uint8),
-           T.fc2[:].bitcast(dt.uint8), s.c2, s.f2c),
-          (1, s.sa, ksc2, lambda k: T.ps2[:, 96 * k:96 * k + 96], lambda m: T.ls[:, 96 * m:96 * m + 96], T.fs2[:], s.c2, s.f2s)])
+    for h in range(2):
+        tt(T.nf[:, :, h, :], T.td2[:, :, :, 8 + h], T.td2[:, :, :, 24 + h], A.add, free=h > 0)
+    kl2 = ts(T.list2[:], T.nf[:], LAND - 1.0, A.add)
+
+    for x in (T.aw, T.bw, T.cw):
+        act(x[:, 0:1], T.zb[:, 0:1], C.Copy, free=x is not T.aw, on="sb")
+    for k in range(3):
+        kkc = act(T.kc[:, :, k], T.zb[:, 0:12], bias=float([400, 496, 544][k]), free=True, on="sb")
+    wait(a, "a", "c1", 48)
+    wait(a, "a", "dcb", 64)
+    ksa = act(T.ps2[:, 0:192], T.cbs[:].indirect(T.list2[:, 0:12]), C.Copy, on="sa", after=[kl2])
+    ksb = act(T.ps2[:, 192:288], T.cbs[:].indirect(T.list2[:, 12:18]), C.Copy, on="sa")
+    wait(a, "a", "drow", 16 * 40)
+    kg3 = act(T.g3[:, 256:512], T.p3w[:].indirect(T.ul[:, 16:32]), C.Copy, on="sa")
+    wait(v, "v", "c1", 48)
+    wait(v, "v", "dcb", 64)
+    kpa = cp(T.pk2[:, 0:192].bitcast(dt.uint32), T.cb[:].bitcast(dt.uint32).indirect(T.list2[:, 0:12]))
+    kpb = cp(T.pk2[:, 192:288].bitcast(dt.uint32), T.cb[:].bitcast(dt.uint32).indirect(T.list2[:, 12:18]), free=True, on="so")
+    to_rest(0, kpa, s.f2c, lambda k: T.pk2[:, 96 * k:96 * k + 96].bitcast(dt.uint8), T.fc2[:].bitcast(dt.uint8))
+    to_rest(1, ksa, s.f2s, lambda k: T.ps2[:, 96 * k:96 * k + 96], T.fs2[:])
+    to_peer(kpb, s.c2p, lambda k: T.pk2[:, 96 * k:96 * k + 96].bitcast(dt.uint8), T.lp[:, 0:96].bitcast(dt.uint8))
+    to_peer(ksb, s.c2p, lambda k: T.ps2[:, 96 * k:96 * k + 96], T.lps[:, 0:96])
+
+    kwq = vec(v.quantize_mx, T.wq[:], T.ws[:], T.wb[:], on="su", after=[("dw", 16)])
+    wait(v, "v", "drow", 16 * 40)
+    cp(T.g3[:, 0:256], T.p3w[:].indirect(T.ul[:, 0:16]))
+    scan(T.s3[:], T.data3[:], T.g3[:], 0.0, after=[kg3, k3])
+    vec(v.transpose, T.tg3[:], T.s3[:])
+    tt(T.val3[:], T.s3[:].indirect(T.offsel[:, 0:16]), T.vsel[:], A.add, free=True, on="sz")
+    tt(T.e3[:, 0:32:2], T.tg3[:, :, 15], T.ac[:], A.add)
+    cp(T.f3[:, 1:32:2], T.tg3[:, :, 31], free=True)
+    scan(T.y3[:], T.f3[:], T.e3[:], 0.0)
+    ts(T.off3[:], T.y3[:, 1:32:2], 256.0, A.add)
+    wait(v, "v", "g4", 2)
+    cp(T.w3[:].indirect(T.off3[:, 0:16]), T.val3[:], after=[("sz", cnt["sz"])])
+    cp(T.dp[:, 0:24:2, :], T.w3[:, 256:448])
+    cp(T.dp[:, 1:24:2, :], T.w3[:, 256:448], free=True)
+    vec(v.transpose, T.t3[:], T.w3[:, 256:448], on="su")
+    vec(v.transpose, T.tp[:], T.dp[:])
+    tt(T.c3[:, :, 13:15], T.t3[:, :, 13:15], T.t3[:, :, 29:31], A.add, on="su")
+    tt(T.yy[:], T.tp[:, :, 0:13], T.tp[:, :, 16:29], A.add)
+    kpl = vec(v.transpose, T.pl[:], T.c3[:], on="su")
+    kqc = cp(T.qc[:], T.yy[:, :, 12], on="so", after=[("sv", cnt["sv"])])
+    kqb = cp(T.qb[:], T.yy[:, :, 9], on="su", after=[kpl])
+    tt(T.x3[:, :, 0:3], T.yy[:, :, 0:3], T.kc[:], A.add, after=[kkc])
+    ts(T.x3[:, :, 3], T.yy[:, :, 8], float(LAND), A.add, free=True)
+    tt(T.x3m[:], T.x3[:], T.yy[:, :, 4:8], A.mult)
+    scan(T.y4[:], T.rs[:, 0:48], T.x3m[:], 0.0)
+    kq0 = cp(T.q0[:], T.y4[:, 3:48:4])
 
     def w(k):
         return T.wq[:, 128 * k:128 * k + 128], T.ws[:, 128 * k:128 * k + 128]
-    g.tensor.wait_ge(s.sv, kc4)
-    mm(T.ps[:, 512:768], *w(1), T.xq[:], T.xs[:], True, True)
-    mm(T.ps[:, 1024:1280], *w(2), T.xq[:], T.xs[:], True, True)
-    g.tensor.wait_ge(s.c1, 48)
+    m2 = mm(T.ps[:, 1024:1280], *w(2), T.xq[:], T.xs[:], True, True, free=True, after=[kwq])
+    m1 = mm(T.ps[:, 512:768], *w(1), T.xq[:], T.xs[:], True, True)
+    wait(g.tensor, "t", "c1", 48)
+    wait(g.tensor, "t", "dcb", 64)
     m0 = mm(T.ps[:, 0:400], *w(0), T.cb[:], T.cbs[:], True, True)
-    a.wait_ge(s.st, m0)
-    act(T.aw[:, 1:401], T.ps[:, 0:400], C.Copy)
-    act(T.bw[:, 1:257], T.ps[:, 512:768], C.Copy, free=True)
-    kaw = act(T.cw[:, 1:257], T.ps[:, 1024:1280], C.Copy, free=True)
-
-    g3, s3 = T.gs3[:, 0:512], T.gs3[:, 512:1024]
-    v.wait_ge(s.drow, 576)
-    cp(g3, T.p3w[:].indirect(T.ul[:, 0:32]))
-    v.wait_ge(s.sa, kaw)
-    vec(v.tensor_tensor_scan, s3, T.data3[:], g3, 0.0, A.mult, A.add)
-    vec(v.transpose, T.tg3[:], T.gs3[:])
-    tt(T.val3[:], s3.indirect(T.offsel[:, 0:16]), T.vsel[:], A.add, free=True)
-    tt(T.va[:], T.tg3[:, 16:32, 15], T.ac[:], A.add)
-    tt(T.vb[:], T.va[:], T.tg3[:, 0:16, 15], A.mult)
-    tt(T.vc[:], T.vb[:], T.trc[:], A.add)
-    ts(T.off3[:], T.vc[:], 256.0, A.add)
-    cp(T.w3[:].indirect(T.off3[:, 0:16]), T.val3[:])
-    cp(T.dp[:, 0:24:2, :], T.w3[:, 256:448])
-    cp(T.dp[:, 1:24:2, :], T.w3[:, 256:448], free=True)
-    vec(v.transpose, T.t3[:], T.w3[:, 256:448], free=True)
-    vec(v.transpose, T.tp[:], T.dp[:])
-    tt(T.c3[:, :, 13:15], T.t3[:, :, 13:15], T.t3[:, :, 29:31], A.add, free=True)
-    tt(T.yy[:], T.tp[:, :, 0:15], T.tp[:, :, 16:31], A.add)
-    vec(v.transpose, T.pl[:], T.c3[:], free=True)
-    tt(T.x3[:, :, 0:3], T.yy[:, :, 0:3], T.kc[:], A.add)
-    tt(T.x3[:, :, 3], T.yy[:, :, 8], T.yy[:, :, 10], A.add, free=True)
-    ki = ts(T.idl[:], T.pl[:], -1.0, A.add, free=True)
-    tt(T.x3m[:], T.x3[:], T.yy[:, :, 4:8], A.mult)
-    g.sync.wait_ge(s.sv, ki)
+    act(T.cw[:, 1:257], T.ps[:, 1024:1280], C.Copy, on="sb", after=[m2])
+    act(T.bw[:, 1:257], T.ps[:, 512:768], C.Copy, free=True, on="sb", after=[m1])
+    kaw = act(T.aw[:, 1:401], T.ps[:, 0:400], C.Copy, free=True, on="sb", after=[m0])
+    kid = act(T.idl[:], T.pl[:], bias=-1.0, on="sa", after=[kpl])
+    wait(a, "a", *kaw)
+    kt1 = act(T.t1[:], T.cw[:, 0:257].indirect(T.qc[:, 0:12]), C.Copy, on="sa", after=[kqc])
+    wait(g.sync, "s", *kid)
     g.sync.dma_start(T.id[0:1, :], T.idl[13:14, :]).then_inc(s.did, 16)
     g.sync.dma_start(T.id[1:2, :], T.idl[14:15, :]).then_inc(s.did, 16)
-    cp(T.qb[:], T.yy[:, :, 9], free=True)
-    cp(T.qc[:], T.yy[:, :, 12], free=True)
-    tt(T.x3b[:], T.x3m[:, :, 0:2], T.x3m[:, :, 2:4], A.add)
-    cp(T.t1[:], T.cw[:, 0:257].indirect(T.qc[:, 0:12]), free=True)
-    tt(T.x3c[:], T.x3b[:, :, 0], T.x3b[:, :, 1], A.add)
-    tt(T.t2[:], T.bw[:, 0:257].indirect(T.qb[:, 0:12]), T.t1[:], A.add, free=True)
-    cp(T.q0[:], T.x3c[:])
+    tt(T.t2[:], T.bw[:, 0:257].indirect(T.qb[:, 0:12]), T.t1[:], A.add, on="so", after=[kaw, kqb, kt1])
 
-    g.tensor.wait_ge(s.c2, 48)
-    mm(T.ps[:, 1536:1776], *w(0), T.lc[:, 0:240], T.ls[:, 0:240], True, False)
-    m3 = mm(T.ps[:, 1536:1776], *w(1), T.lc[:, 48:288], T.ls[:, 48:288], False, True, free=True)
-    v.wait_ge(s.st, m3)
-    cp(T.aw[:, 401:641], T.ps[:, 1536:1776], free=True)
-    ky = tt(T.yo[:], T.aw[:, 0:641].indirect(T.q0[:, 0:12]), T.t2[:], A.add)
-    g.sync.wait_ge(s.sv, ky)
+    wait(g.tensor, "t", "c2p", 16)
+    mm(T.ps[:, 2048:2176], *w(0), T.lp[:, 0:128], T.lps[:, 0:128], True, False)
+    mp = mm(T.ps[:, 2048:2176], *w(1), T.lp[:, 48:176], T.lps[:, 48:176], False, True, free=True)
+    wait(g.tensor, "t", "c2", 32)
+    mm(T.ps[:, 1536:1680], *w(0), T.lr[:, 0:144], T.lrs[:, 0:144], True, False)
+    mr = mm(T.ps[:, 1536:1680], *w(1), T.lr[:, 48:192], T.lrs[:, 48:192], False, True, free=True)
+    cp(T.aw[:, 545:593], T.ps[:, 2048:2096], free=True, on="so", after=[mp])
+    cp(T.aw[:, 401:545], T.ps[:, 1536:1680], free=True, on="so", after=[mr])
+    ky = tt(T.yo[:], T.aw[:, 0:593].indirect(T.q0[:, 0:12]), T.t2[:], A.add, on="so", after=[kq0])
+    wait(g.sync, "s", *ky)
     g.sync.dma_start(T.y[:], T.yo[:]).then_inc(s.dy, 16)
 
     g.wait_ge(s.dy, 16)
     g.wait_ge(s.did, 32)
-    g.wait_ge(s.sa, cnt["a"])
-    g.wait_ge(s.st, cnt["t"])
-    g.wait_ge(s.loc, cnt["loc"])
+    for x in ("sv", "su", "so", "sz", "sa", "sb", "sk", "sp", "st", "loc"):
+        wait(g, "g", x, cnt[x])

@@ -22,7 +22,7 @@ SCRATCH = {
     "io256": _sb(B, 256), "zb": _sb(B, 512), "d01": _sb(B, 128), "offsel": _sb(U, 16), "trc": _sb(F, 16), "ac": _sb(F, 16),
     "data0": _sb(B, 256), "data3": _sb(B, 512), "kc": _sb(F, 12, 3), "rs": _sb(F, 64),
     "stb": _sb(I, 16), "b0": _sb(I, 8), "b1": _sb(I, 8), "sx": _sb(I, 8), "sy": _sb(I, 8), "sz": _sb(I, 8), "sw": _sb(I, 8),
-    "q1l": _sb(U, 8), "qst": _sb(U, 8), "p1w": _sb(I, 512), "nl": _sb(F, 128), "nd": _sb(F, 16, 16), "tn": _sb(F, 8, 32), "uf": _sb(F, 8),
+    "q1l": _sb(U, 16), "qst": _sb(U, 8), "p1w": _sb(I, 512), "nd": _sb(F, 256), "tn": _sb(F, 8, 32), "uf": _sb(F, 8),
     "ul": _sb(U, 32), "win2": _sb(B, 2048), "gg1": _sb(B, 128), "gs1": _sb(B, 128), "tg": _sb(B, 4, 32),
     "x1": _sb(F, 16), "y1": _sb(F, 16), "off1": _sb(U, 4),
     "c0l": _sb(B, 128), "vs1": _sb(B, 64), "c0m": _sb(B, 64), "w1": _sb(B, 272),
@@ -32,16 +32,16 @@ SCRATCH = {
     "x2": _sb(F, 64), "y2": _sb(F, 64), "off2": _sb(U, 16),
     "vown": _sb(B, 64), "vsel": _sb(B, 256), "w2": _sb(B, 400), "d2": _sb(B, 18, 16), "td2": _sb(B, 3, 3, 32),
     "nf": _sb(F, 3, 2, 3), "list2": _sb(U, 18),
-    "nx4": _sb(I, 32), "nt4": _sb(I, 32), "r4": _sb(I, 16), "c4": _sb(I, 16), "mp": _sb(B, 16), "cp4": _sb(B, 16),
+    "nx4": _sb(I, 32), "nt4": _sb(I, 32), "r4": _sb(I, 16), "mp": _sb(B, 16), "cp4": _sb(B, 16),
     "p3w": _sb(B, 2048), "g3": _sb(B, 512), "s3": _sb(B, 512), "tg3": _sb(B, 16, 32), "e3": _sb(F, 32), "f3": _sb(F, 32), "y3": _sb(F, 32),
     "off3": _sb(U, 16), "val3": _sb(B, 256), "w3": _sb(B, 448),
     "t3": _sb(B, 6, 32), "c3": _sb(B, 6, 32), "pl": _sb(B, 192), "idl": _sb(F, 192),
-    "dp": _sb(B, 24, 16), "tp": _sb(B, 12, 32), "yy": _sb(F, 12, 13),
-    "x3": _sb(F, 12, 4), "x3m": _sb(F, 48), "y4": _sb(F, 48), "q0": _sb(U, 12), "qb": _sb(U, 12), "qc": _sb(U, 12),
+    "dp": _sb(B, 24, 16), "tp": _sb(B, 12, 32), "yy": _sb(F, 12, 10),
+    "x3": _sb(F, 12, 4), "x3m": _sb(F, 48), "y4": _sb(F, 48), "q0": _sb(U, 12), "qbc": _sb(U, 24),
     "ps": ("psum", [128, 2560], F), "aw": _sb(F, 600), "bw": _sb(F, 264), "cw": _sb(F, 264),
     "t1": _sb(F, 192), "t2": _sb(F, 192), "yo": _sb(F, 192),
 }
-SEMAPHORES = ["sv", "su", "so", "sz", "sa", "sb", "sk", "sp", "st", "g0", "g1", "g2", "g3", "g4", "dsb", "dnx", "dns", "dn4", "dx", "dw", "dnat",
+SEMAPHORES = ["sv", "su", "so", "sz", "sq", "sa", "sb", "sk", "sp", "st", "g0", "g1", "g2", "g3", "g4", "dsb", "dnx", "dns", "dn4", "dx", "dw", "dnat",
               "dmk", "dcb", "drow", "dz", "dy", "did", "m0", "m1", "c1", "c2", "c2p", "loc", "f0", "f1", "f1c", "f1s", "f2c", "f2s"]
 
 
@@ -133,6 +133,10 @@ def rank_program(g, core, T, topo):
     def scan(out, d0, d1, init, **kw):
         return vec(v.tensor_tensor_scan, out, d0, d1, init, A.mult, A.add, **kw)
 
+    def quant(k):
+        return vec(v.quantize_mx, T.wq[:, 128 * k:128 * k + 128], T.ws[:, 128 * k:128 * k + 128], T.wb[:, 512 * k:512 * k + 512], free=True, on="sq",
+                   after=[("dw", 16)])
+
     rest, peer = [0, 1], 2
 
     def call(items):
@@ -214,33 +218,33 @@ def rank_program(g, core, T, topo):
     kfill = fill(T.rs[:, 0:64:4], 0.0, free=False)
     wait(a, "a", *ke)
     wait(a, "a", *kz)
-    act(new("z3"), eq(3), bias=eq(14), free=True)
+    kz3 = act(new("z3"), eq(3), bias=eq(14), free=True)
     act(new("z7"), eq(7), bias=eq(14), free=True)
     act(new("u1"), q16, scale=48.0, bias=-193.0, free=True)
     act(T.d01[:], T.zb[:, 0:128], bias=c("even"), free=True)
-    act(new("v", 3), eq(4, 3), bias=c("z3"))
+    act(new("v", 2), eq(4, 2), bias=c("z3"))
     act(new("vme"), eq(8), bias=c("z7"), free=True)
     act(new("init1"), eq(7), scale=-272.0, bias=c("u1"), free=True)
     v0 = col["v"][2]
-    for k in range(3):
+    for k in range(2):
         act(T.win2[:, 512 * others[k]:512 * others[k] + 512], T.zb[:], bias=T.col[:, v0 + k:v0 + k + 1], free=k > 0)
     wait(a, "a", "g1", 1)
     for h in range(2):
         kw = act(T.win2[:, 512 * me + h:512 * me + 512:2], T.io256[:], scale=eq(9), bias=c("vme"), free=True)
 
     wait(v, "v", "dsb", 256)
-    ts(T.b0[:], T.stb[:, 8:16], 1, A.bitwise_and)
     ts(T.sx[:], T.stb[:, 0:8], 513.0, A.mult, free=True)
-    ts(T.sy[:], T.b0[:], 256.0, A.mult)
+    ts(T.b0[:], T.stb[:, 8:16], 32.0, A.mult, free=True)
     kq = cp(T.qst[:], T.stb[:, 0:8], on="sp")
-    tt(T.sz[:], T.sx[:], T.sy[:], A.add)
+    ts(T.sw[:], T.sx[:], 3, A.logical_shift_right, 511, A.bitwise_and)
+    ts(T.sy[:], T.b0[:], 32, A.bitwise_and, free=True)
     ts(T.b1[:], T.stb[:, 8:16], 1, A.logical_shift_right, free=True, on="su")
-    ts(T.sw[:], T.sz[:], 3, A.logical_shift_right, 511, A.bitwise_and)
-    cp(T.q1l[:], T.sw[:])
+    tt(T.sz[:], T.sw[:], T.sy[:], A.add)
+    ts(T.win2[:, 512 * others[2]:512 * others[2] + 512], T.zb[:], eq(6), A.add, c("z3"), A.add, free=True, on="sp", after=[kz3])
+    cp(T.q1l[:, 0:16:2], T.sz[:])
+    cp(T.q1l[:, 1:16:2], T.sz[:], free=True)
     wait(v, "v", "dnx", 64)
-    ts(T.nl[:], T.p1w[:].indirect(T.q1l[:, 0:8]), 2.0, A.mult)
-    cp(T.nd[:, 0:16:2, :], T.nl[:])
-    cp(T.nd[:, 1:16:2, :], T.nl[:], free=True)
+    ts(T.nd[:], T.p1w[:].indirect(T.q1l[:]), 2.0, A.mult)
     vec(v.transpose, T.tn[:], T.nd[:])
     tt(T.uf[:], T.tn[:, :, 0], T.b1[:], A.add, after=[("su", cnt["su"])])
     ku = cp(T.ul[:, 8 * me:8 * me + 8], T.uf[:])
@@ -277,7 +281,7 @@ def rank_program(g, core, T, topo):
     k3 = act(T.data3[:], T.zb[:], bias=c("kp"), on="sb")
 
     vec(v.transpose, T.nxt[:], T.nxs[:], free=True, on="su", after=[("dns", 64)])
-    kg1 = cp(T.gg1[:], T.win2[:].indirect(mine), after=[kw])
+    kg1 = cp(T.gg1[:], T.win2[:].indirect(mine), after=[kw, ("sp", cnt["sp"])])
     ts(T.nxr[:], T.nxt[:, 0:16], 8, A.logical_shift_right, on="su")
     scan(T.gs1[:], T.d01[:], T.gg1[:], c("init1"))
     for r in range(4):
@@ -317,19 +321,6 @@ def rank_program(g, core, T, topo):
     g.sync.dma_start(T.cbs[:, LAND:LAND + TX], T.xs[:]).then_inc(s.dcb, 16)
     g.sync.dma_start(T.lp[:, 96:176].bitcast(dt.uint8), T.xq[:, 0:80].bitcast(dt.uint8)).then_inc(s.dcb, 16)
     g.sync.dma_start(T.lps[:, 96:176], T.xs[:, 0:80]).then_inc(s.dcb, 16)
-    vec(v.transpose, T.nt4[:], T.nx4[:], free=True, on="su", after=[("dn4", 64)])
-    ts(T.r4[:], T.nt4[:, 0:16], 8, A.logical_shift_right, on="su")
-    ts(T.c4[:], T.nt4[:, 0:16], 255, A.bitwise_and, free=True, on="su")
-    ts(T.mp[:], T.r4[:], float(me), A.is_equal, on="su")
-    kc4 = ts(T.cp4[:], T.c4[:], 1.0, A.add, free=True, on="su")
-
-    wait(g.sync, "s", *kc4)
-    wait(g.sync, "s", "dz", 64)
-    for b in range(0, 128, 16):
-        g.sync.dma_start(T.p3w[b + 15:b + 16, :], T.mp[:]).then_inc(s.drow, 16)
-        g.sync.dma_start(T.p3w[b + 12:b + 13, :], T.cp4[:]).then_inc(s.drow, 16)
-        for k, r in enumerate(others):
-            g.sync.dma_start(T.p3w[b + k:b + k + 1, 512 * r:512 * r + 512], T.mp[32 * r:32 * r + 32, :]).then_inc(s.drow, 16)
 
     wait(a, "a", "m1", 24)
     wait(a, "a", "dmk", 128)
@@ -338,73 +329,89 @@ def rank_program(g, core, T, topo):
     wait(v, "v", "dmk", 128)
     wait(v, "v", *kw2)
     cp(T.g2[:, 0:256], T.win2[:].indirect(T.ul[:, 0:16]))
+    vec(v.transpose, T.nt4[:], T.nx4[:], free=True, on="su", after=[("dn4", 64)])
     ksA = scan(T.s2[:, 0:256], T.data0[:], T.g2[:, 0:256], c("init2"))
+    ts(T.r4[:], T.nt4[:, 0:16], 8, A.logical_shift_right, on="su")
+    ts(T.cp4[:], T.nt4[:, 0:16], 1.0 - 256.0 * me, A.add, free=True, on="su")
     ksB = scan(T.s2[:, 256:512], T.data0[:], T.g2[:, 256:512], T.s2[:, 255:256], after=[kgb])
     vec(v.transpose, T.tg2[:, 0:8, :], T.s2[:, 0:256], free=True, on="sz")
+    kmp = ts(T.mp[:], T.r4[:], float(me), A.is_equal, on="su")
     vec(v.transpose, T.tg2[:, 8:16, :], T.s2[:, 256:512], free=True, on="sz", after=[ksB])
+    quant(0)
     for n, r in enumerate(sorted(range(4), key=lambda r: (r >= 2, r != me))):
         kvsel = act(T.vown[:] if r == me else T.vsel[:, 64 * r:64 * r + 64], T.s2[:, 128 * r:128 * r + 128].indirect(T.offsel[:, 0:4]), free=n > 0, on="sa",
                     after=[ksB if r >= 2 else ksA], scale=c("nz8" if r == me else "nz"), **({} if r == me else {"bias": c("b%d" % r)}))
     tt(T.x2[:, 3:64:4], T.tg2[:, :, 3], T.trc[:], A.mult, on="sz")
     for k in range(3):
         tt(T.x2[:, k:64:4], T.tg2[:, :, k], T.tg2[:, :, 16 + k], A.mult, free=True, on="sz")
+    quant(1)
     scan(T.y2[:], T.rs[:], T.x2[:], 0.0, on="sz")
     tt(T.vsel[:, 64 * me:64 * me + 64], T.vown[:], T.c0m[:], A.add, free=True, after=[kvsel])
     ts(T.off2[:], T.y2[:, 3:64:4], 256.0, A.add, on="sz")
+    kwq = quant(2)
     wait(v, "v", "g2", 1)
     cp(T.w2[:].indirect(T.off2[:, 0:16]), T.vsel[:], after=[("sz", cnt["sz"])])
-    cp(T.d2[:, 0:18:2, :], T.w2[:, 256:400])
-    cp(T.d2[:, 1:18:2, :], T.w2[:, 256:400], free=True)
-    vec(v.transpose, T.td2[:], T.d2[:])
-    for h in range(2):
-        tt(T.nf[:, :, h, :], T.td2[:, :, :, 8 + h], T.td2[:, :, :, 24 + h], A.add, free=h > 0)
-    kl2 = ts(T.list2[:], T.nf[:], LAND - 1.0, A.add)
+
+    wait(g.sync, "s", "dz", 64)
+    wait(g.sync, "s", *kmp)
+    for b in (0, 16):
+        g.sync.dma_start(T.p3w[b + 15:b + 16, :], T.mp[:]).then_inc(s.drow, 16)
+        g.sync.dma_start(T.p3w[b + 3:b + 4, :], T.cp4[:]).then_inc(s.drow, 16)
+        for k, r in enumerate(others):
+            g.sync.dma_start(T.p3w[b + k:b + k + 1, 512 * r:512 * r + 512], T.mp[32 * r:32 * r + 32, :]).then_inc(s.drow, 16)
 
     for x in (T.aw, T.bw, T.cw):
         act(x[:, 0:1], T.zb[:, 0:1], C.Copy, free=x is not T.aw, on="sb")
     for k in range(3):
         kkc = act(T.kc[:, :, k], T.zb[:, 0:12], bias=float([400, 496, 544][k]), free=True, on="sb")
+    wait(a, "a", "drow", 16 * 10)
+    kg3 = act(T.g3[:], T.p3w[:].indirect(T.ul[:]), C.Copy, on="sa")
+
+    cp(T.d2[:, 0:18:2, :], T.w2[:, 256:400])
+    cp(T.d2[:, 1:18:2, :], T.w2[:, 256:400], free=True)
+    vec(v.transpose, T.td2[:], T.d2[:])
+    scan(T.s3[:], T.data3[:], T.g3[:], 0.0, free=True, on="sz", after=[kg3, k3])
+    for h in range(2):
+        tt(T.nf[:, :, h, :], T.td2[:, :, :, 8 + h], T.td2[:, :, :, 24 + h], A.add, free=h > 0)
+    vec(v.transpose, T.tg3[:], T.s3[:], on="sz")
+    kl2 = ts(T.list2[:], T.nf[:], LAND - 1.0, A.add)
+    tt(T.e3[:, 0:32:2], T.tg3[:, :, 15], T.ac[:], A.add, on="sz")
+    cp(T.f3[:, 1:32:2], T.tg3[:, :, 31], free=True, on="sz")
     wait(a, "a", "c1", 48)
     wait(a, "a", "dcb", 64)
     ksa = act(T.ps2[:, 0:192], T.cbs[:].indirect(T.list2[:, 0:12]), C.Copy, on="sa", after=[kl2])
     ksb = act(T.ps2[:, 192:288], T.cbs[:].indirect(T.list2[:, 12:18]), C.Copy, on="sa")
-    wait(a, "a", "drow", 16 * 40)
-    kg3 = act(T.g3[:, 256:512], T.p3w[:].indirect(T.ul[:, 16:32]), C.Copy, on="sa")
     wait(v, "v", "c1", 48)
     wait(v, "v", "dcb", 64)
     kpa = cp(T.pk2[:, 0:192].bitcast(dt.uint32), T.cb[:].bitcast(dt.uint32).indirect(T.list2[:, 0:12]))
+    scan(T.y3[:], T.f3[:], T.e3[:], 0.0, on="sz")
     kpb = cp(T.pk2[:, 192:288].bitcast(dt.uint32), T.cb[:].bitcast(dt.uint32).indirect(T.list2[:, 12:18]), free=True, on="so")
+    ts(T.off3[:], T.y3[:, 1:32:2], 256.0, A.add, on="sz")
     to_rest(0, kpa, s.f2c, lambda k: T.pk2[:, 96 * k:96 * k + 96].bitcast(dt.uint8), T.fc2[:].bitcast(dt.uint8))
     to_rest(1, ksa, s.f2s, lambda k: T.ps2[:, 96 * k:96 * k + 96], T.fs2[:])
     to_peer(kpb, s.c2p, lambda k: T.pk2[:, 96 * k:96 * k + 96].bitcast(dt.uint8), T.lp[:, 0:96].bitcast(dt.uint8))
     to_peer(ksb, s.c2p, lambda k: T.ps2[:, 96 * k:96 * k + 96], T.lps[:, 0:96])
 
-    kwq = vec(v.quantize_mx, T.wq[:], T.ws[:], T.wb[:], on="su", after=[("dw", 16)])
-    wait(v, "v", "drow", 16 * 40)
-    cp(T.g3[:, 0:256], T.p3w[:].indirect(T.ul[:, 0:16]))
-    scan(T.s3[:], T.data3[:], T.g3[:], 0.0, after=[kg3, k3])
-    vec(v.transpose, T.tg3[:], T.s3[:])
-    tt(T.val3[:], T.s3[:].indirect(T.offsel[:, 0:16]), T.vsel[:], A.add, free=True, on="sz")
-    tt(T.e3[:, 0:32:2], T.tg3[:, :, 15], T.ac[:], A.add)
-    cp(T.f3[:, 1:32:2], T.tg3[:, :, 31], free=True)
-    scan(T.y3[:], T.f3[:], T.e3[:], 0.0)
-    ts(T.off3[:], T.y3[:, 1:32:2], 256.0, A.add)
+    tt(T.val3[:], T.s3[:].indirect(T.offsel[:, 0:16]), T.vsel[:], A.add, free=True)
     wait(v, "v", "g4", 2)
     cp(T.w3[:].indirect(T.off3[:, 0:16]), T.val3[:], after=[("sz", cnt["sz"])])
     cp(T.dp[:, 0:24:2, :], T.w3[:, 256:448])
     cp(T.dp[:, 1:24:2, :], T.w3[:, 256:448], free=True)
-    vec(v.transpose, T.t3[:], T.w3[:, 256:448], on="su")
+    vec(v.transpose, T.t3[:], T.w3[:, 256:448], free=True, on="su")
     vec(v.transpose, T.tp[:], T.dp[:])
     tt(T.c3[:, :, 13:15], T.t3[:, :, 13:15], T.t3[:, :, 29:31], A.add, on="su")
-    tt(T.yy[:], T.tp[:, :, 0:13], T.tp[:, :, 16:29], A.add)
+    kyy = tt(T.yy[:], T.tp[:, :, 0:10], T.tp[:, :, 16:26], A.add)
     kpl = vec(v.transpose, T.pl[:], T.c3[:], on="su")
-    kqc = cp(T.qc[:], T.yy[:, :, 12], on="so", after=[("sv", cnt["sv"])])
-    kqb = cp(T.qb[:], T.yy[:, :, 9], on="su", after=[kpl])
+    cp(T.qbc[0:32, 0:12], T.yy[0:32, :, 3], free=True, on="so", after=[kyy])
+    cp(T.qbc[0:32, 12:24], T.yy[0:32, :, 9], free=True, on="so")
     tt(T.x3[:, :, 0:3], T.yy[:, :, 0:3], T.kc[:], A.add, after=[kkc])
     ts(T.x3[:, :, 3], T.yy[:, :, 8], float(LAND), A.add, free=True)
+    cp(T.qbc[32:64, :], T.qbc[0:32, :], on="so")
     tt(T.x3m[:], T.x3[:], T.yy[:, :, 4:8], A.mult)
-    scan(T.y4[:], T.rs[:, 0:48], T.x3m[:], 0.0)
-    kq0 = cp(T.q0[:], T.y4[:, 3:48:4])
+    kqbc = cp(T.qbc[64:128, :], T.qbc[0:64, :], on="so")
+    ky4 = scan(T.y4[:], T.rs[:, 0:48], T.x3m[:], 0.0)
+    for b in range(0, 128, 32):
+        kq0 = cp(T.q0[b:b + 32, :], T.y4[0:32, 3:48:4], free=True, on="so", after=[ky4])
 
     def w(k):
         return T.wq[:, 128 * k:128 * k + 128], T.ws[:, 128 * k:128 * k + 128]
@@ -416,13 +423,13 @@ def rank_program(g, core, T, topo):
     act(T.cw[:, 1:257], T.ps[:, 1024:1280], C.Copy, on="sb", after=[m2])
     act(T.bw[:, 1:257], T.ps[:, 512:768], C.Copy, free=True, on="sb", after=[m1])
     kaw = act(T.aw[:, 1:401], T.ps[:, 0:400], C.Copy, free=True, on="sb", after=[m0])
-    kid = act(T.idl[:], T.pl[:], bias=-1.0, on="sa", after=[kpl])
     wait(a, "a", *kaw)
-    kt1 = act(T.t1[:], T.cw[:, 0:257].indirect(T.qc[:, 0:12]), C.Copy, on="sa", after=[kqc])
+    kt1 = act(T.t1[:], T.cw[:, 0:257].indirect(T.qbc[:, 0:12]), C.Copy, on="sa", after=[kqbc])
+    kid = act(T.idl[:], T.pl[:], bias=-1.0, on="sa", after=[kpl])
     wait(g.sync, "s", *kid)
     g.sync.dma_start(T.id[0:1, :], T.idl[13:14, :]).then_inc(s.did, 16)
     g.sync.dma_start(T.id[1:2, :], T.idl[14:15, :]).then_inc(s.did, 16)
-    tt(T.t2[:], T.bw[:, 0:257].indirect(T.qb[:, 0:12]), T.t1[:], A.add, on="so", after=[kaw, kqb, kt1])
+    tt(T.t2[:], T.bw[:, 0:257].indirect(T.qbc[:, 12:24]), T.t1[:], A.add, on="so", after=[kaw, kqbc, kt1])
 
     wait(g.tensor, "t", "c2p", 16)
     mm(T.ps[:, 2048:2176], *w(0), T.lp[:, 0:128], T.lps[:, 0:128], True, False)
@@ -430,13 +437,13 @@ def rank_program(g, core, T, topo):
     wait(g.tensor, "t", "c2", 32)
     mm(T.ps[:, 1536:1680], *w(0), T.lr[:, 0:144], T.lrs[:, 0:144], True, False)
     mr = mm(T.ps[:, 1536:1680], *w(1), T.lr[:, 48:192], T.lrs[:, 48:192], False, True, free=True)
-    cp(T.aw[:, 545:593], T.ps[:, 2048:2096], free=True, on="so", after=[mp])
+    kpw = act(T.aw[:, 545:593], T.ps[:, 2048:2096], C.Copy, free=True, on="sb", after=[mp])
     cp(T.aw[:, 401:545], T.ps[:, 1536:1680], free=True, on="so", after=[mr])
-    ky = tt(T.yo[:], T.aw[:, 0:593].indirect(T.q0[:, 0:12]), T.t2[:], A.add, on="so", after=[kq0])
+    ky = tt(T.yo[:], T.aw[:, 0:593].indirect(T.q0[:, 0:12]), T.t2[:], A.add, on="so", after=[kq0, kpw])
     wait(g.sync, "s", *ky)
     g.sync.dma_start(T.y[:], T.yo[:]).then_inc(s.dy, 16)
 
     g.wait_ge(s.dy, 16)
     g.wait_ge(s.did, 32)
-    for x in ("sv", "su", "so", "sz", "sa", "sb", "sk", "sp", "st", "loc"):
+    for x in ("sv", "su", "so", "sz", "sq", "sa", "sb", "sk", "sp", "st", "loc"):
         wait(g, "g", x, cnt[x])

from concourse.bass import DstId, RemoteDMATransfer
from concourse.mybir import dt, AluOpType, ActivationFunctionType

N, CAP, TX = 4, 48, 256
LAND = 3 * CAP
F, B, I, U = "float32", "bfloat16", "int32", "uint16"
CODE, PLANE = "float8_e4m3fn_x4", "uint8"


def _sb(d, *s):
    return ("sbuf", [128] + list(s), d)


SCRATCH = {
    "xb": _sb(B, 1024), "wb": _sb(B, 1536),
    "xq": _sb(CODE, 256), "xs": _sb(PLANE, 256), "cb": _sb(CODE, 400), "cbs": _sb(PLANE, 400), "wq": _sb(CODE, 384), "ws": _sb(PLANE, 384),
    "pk1": _sb(CODE, 144), "ps1": _sb(PLANE, 144), "pk2": _sb(CODE, 288), "ps2": _sb(PLANE, 288),
    "fc1": _sb(CODE, 48), "fs1": _sb(PLANE, 48), "fc2": _sb(CODE, 96), "fs2": _sb(PLANE, 96),
    "fu": _sb(U, 8), "fn": ("dram", [128, 2], I), "natl": ("dram", [8, 128, 2], I),
    "lr": _sb(CODE, 192), "lrs": _sb(PLANE, 192), "lp": _sb(CODE, 176), "lps": _sb(PLANE, 176),
    "pi": _sb(I, 1), "ic": _sb(I, 2), "col": _sb(F, 48), "iob": _sb(F, 16), "io16": _sb(F, 16), "eq": _sb(F, 16), "eqh": _sb(F, 16),
    "io256": _sb(B, 256), "zb": _sb(B, 512), "d01": _sb(B, 128), "offsel": _sb(U, 16), "trc": _sb(F, 16), "ac": _sb(F, 16),
    "data0": _sb(B, 256), "data3": _sb(B, 512), "kc": _sb(F, 12, 3), "rs": _sb(F, 64),
    "stb": _sb(I, 16), "b0": _sb(I, 8), "b1": _sb(I, 8), "sx": _sb(I, 8), "sy": _sb(I, 8), "sz": _sb(I, 8), "sw": _sb(I, 8),
    "q1l": _sb(U, 16), "qst": _sb(U, 8), "p1w": _sb(I, 512), "nd": _sb(F, 256), "tn": _sb(F, 8, 32), "uf": _sb(F, 8),
    "ul": _sb(U, 32), "win2": _sb(B, 2048), "gg1": _sb(B, 128), "gs1": _sb(B, 128), "tg": _sb(B, 4, 32),
    "x1": _sb(F, 16), "y1": _sb(F, 16), "off1": _sb(U, 4),
    "c0l": _sb(B, 128), "vs1": _sb(B, 64), "c0m": _sb(B, 64), "w1": _sb(B, 272),
    "d1": _sb(B, 18, 16), "td1": _sb(B, 9, 32), "l1f": _sb(F, 9), "list1": _sb(U, 10),
    "nxs": _sb(I, 32), "nxt": _sb(I, 32), "nxr": _sb(I, 16), "mk": _sb(B, 16),
    "g2": _sb(B, 512), "s2": _sb(B, 512), "tg2": _sb(B, 16, 32),
    "x2": _sb(F, 64), "y2": _sb(F, 64), "off2": _sb(U, 16),
    "vown": _sb(B, 64), "vsel": _sb(B, 256), "w2": _sb(B, 400), "d2": _sb(B, 18, 16), "td2": _sb(B, 3, 3, 32),
    "nf": _sb(F, 3, 2, 3), "list2": _sb(U, 18),
    "nx4": _sb(I, 32), "nt4": _sb(I, 32), "r4": _sb(I, 16), "mp": _sb(B, 16), "cp4": _sb(B, 16),
    "p3w": _sb(B, 2048), "g3": _sb(B, 512), "s3": _sb(B, 512), "tg3": _sb(B, 16, 32), "e3": _sb(F, 32), "f3": _sb(F, 32), "y3": _sb(F, 32),
    "off3": _sb(U, 16), "val3": _sb(B, 256), "w3": _sb(B, 448),
    "t3": _sb(B, 6, 32), "c3": _sb(B, 6, 32), "pl": _sb(B, 192), "idl": _sb(F, 192),
    "dp": _sb(B, 24, 16), "tp": _sb(B, 12, 32), "yy": _sb(F, 12, 10),
    "x3": _sb(F, 12, 4), "x3m": _sb(F, 48), "y4": _sb(F, 48), "q0": _sb(U, 12), "qbc": _sb(U, 24),
    "ps": ("psum", [128, 2560], F), "aw": _sb(F, 600), "bw": _sb(F, 264), "cw": _sb(F, 264),
    "t1": _sb(F, 192), "t2": _sb(F, 192), "yo": _sb(F, 192),
}
SEMAPHORES = ["sv", "su", "so", "sz", "sq", "sa", "sb", "sk", "sp", "st", "g0", "g1", "g2", "g3", "g4", "dsb", "dnx", "dns", "dn4", "dx", "dw", "dnat",
              "dmk", "dcb", "drow", "dz", "dy", "did", "m0", "m1", "c1", "c2", "c2p", "loc", "f0", "f1", "f1c", "f1s", "f2c", "f2s"]


def order(topo, cores, r):
    return sorted([k for k in range(N) if k != r], key=lambda k: topo.may_write(cores[r], cores[k]))


def forwarders(topo, src, dst):
    near = topo.host(src) == topo.host(dst)
    return [k for k in topo.cores_of(src) if topo.may_write(k, dst) and (topo.die(k) == topo.die(src)) == near][:2]


def mask_of(engines):
    return sum(1 << e for e in engines)


def hand_on(g, core, T, topo):
    for i, src in enumerate(T.cores):
        for j, dst in enumerate(T.cores):
            if i == j or topo.may_write(src, dst) or core not in forwarders(topo, src, dst):
                continue
            h = forwarders(topo, src, dst).index(core)
            k = order(topo, T.cores, j).index(i)
            rid, pid = topo.addr(dst, core)
            e = topo.engines(core, dst)
            s = T.sem
            jobs = [(s.f0, 4, T.natl[2 * i + h], T.fn[:], s.m0)]
            if h:
                jobs += [(s.f1, 8, T.ul[:, 8 * i:8 * i + 8], T.fu[:], s.m1),
                         (s.f1s, 8, T.cbs[:, CAP * k:CAP * k + CAP], T.fs1[:], s.c1),
                         (s.f2s, 8, T.lrs[:, 96 * k:96 * k + 96], T.fs2[:], s.c2)]
            else:
                jobs += [(s.f1c, 8, T.cb[:, CAP * k:CAP * k + CAP].bitcast(dt.uint8), T.fc1[:].bitcast(dt.uint8), s.c1),
                         (s.f2c, 8, T.lr[:, 96 * k:96 * k + 96].bitcast(dt.uint8), T.fc2[:].bitcast(dt.uint8), s.c2)]
            for sem, n, out, in_, to in jobs:
                g.wait_ge(sem, n)
                g.remote_dma(out, in_, to, s.loc, pid, rid, mask_of(e))
            g.wait_ge(s.loc, len(jobs) * len(e))


def rank_program(g, core, T, topo):
    me = T.rank_of(core)
    if me is None:
        hand_on(g, core, T, topo)
        return
    A, C = AluOpType, ActivationFunctionType
    others = order(topo, T.cores, me)
    s, v, a = T.sem, g.vector, g.scalar
    cnt = {}
    known = {}

    def wait(q, name, sem, n):
        if known.get((name, sem), 0) < n:
            q.wait_ge(s[sem], n)
            known[(name, sem)] = n

    def put(q, name, chain, free, after, f, *args, **kw):
        for sem, n in after:
            wait(q, name, sem, n)
        if not free:
            wait(q, name, chain, cnt.get(chain, 0))
        f(*args, **kw).then_inc(s[chain], 1)
        cnt[chain] = cnt.get(chain, 0) + 1
        return (chain, cnt[chain])

    def vec(f, *args, free=False, on="sv", after=()):
        return put(v, "v", on, free, after, f, *args)

    def act(out, in_, func=C.Identity, free=False, on="sk", after=(), **kw):
        return put(a, "a", on, free, after, a.activation, out, in_, func, **kw)

    def mm(*args, free=False, after=()):
        return put(g.tensor, "t", "st", free, after, g.tensor.matmul_mx, *args)

    def ts(out, in_, s1, op0, s2=None, op1=None, **kw):
        if op1 is None:
            return vec(v.tensor_scalar, out, in_, s1, None, op0, **kw)
        return vec(v.tensor_scalar, out, in_, s1, s2, op0, op1, **kw)

    def tt(out, x, y, op, **kw):
        return vec(v.tensor_tensor, out, x, y, op, **kw)

    def cp(out, in_, **kw):
        return vec(v.tensor_copy, out, in_, **kw)

    def fill(out, x, free=True, on="so"):
        return vec(v.memset, out, x, free=free, on=on)

    def scan(out, d0, d1, init, **kw):
        return vec(v.tensor_tensor_scan, out, d0, d1, init, A.mult, A.add, **kw)

    def quant(k):
        return vec(v.quantize_mx, T.wq[:, 128 * k:128 * k + 128], T.ws[:, 128 * k:128 * k + 128], T.wb[:, 512 * k:512 * k + 512], free=True, on="sq",
                   after=[("dw", 16)])

    rest, peer = [0, 1], 2

    def call(items):
        tr = []
        for d, n, of, sem, src, dst in items:
            e = topo.engines(core, d)
            h = len(e) // of
            rid, pid = topo.addr(d, core)
            tr.append(RemoteDMATransfer(dst_ids=[DstId(rid=rid, pnc=pid)], dma_engine_mask=mask_of(e[n * h:n * h + h]), remote_sem=sem, src=src, dst=dst))
            cnt["loc"] = cnt.get("loc", 0) + h
        g.remote_dma_fused(tr, local_sem=s.loc)

    def to_rest(h, after, sem, src, dst):
        wait(g, "g", *after)
        call([(forwarders(topo, core, T.cores[others[k]])[h], k, len(rest), sem, src(k), dst) for k in rest])

    def to_peer(after, sem, src, dst):
        wait(g, "g", *after)
        call([(T.cores[others[peer]], 0, 1, sem, src(peer), dst)])

    col = {}

    def new(name, n=1):
        assert name not in col
        at = sum(col[k][1] for k in col)
        col[name] = (T.col[:, at:at + n], n, at)
        return col[name][0]

    def c(name):
        return col[name][0]

    def eq(r, n=1):
        return T.eq[:, r:r + n]

    g.sync.dma_start(T.natl[2 * me:2 * me + 2], T.nx[:]).then_inc(s.dnat, 16)
    for q in range(8):
        g.sync.dma_start(T.stb[16 * q:16 * q + 16, 0:8], T.st[:]).then_inc(s.dsb, 16)
        a.dma_start(T.stb[16 * q:16 * q + 16, 8:16], T.bt[:]).then_inc(s.dsb, 16)
    k = fill(T.p1w[:], 0, on="sz")
    for q in range(4):
        e, n = (g.sync, "s") if q % 2 else (a, "a")
        wait(e, n, *k)
        e.dma_start(T.p1w[32 * q:32 * q + 1, :], T.nx[:]).then_inc(s.dnx, 16)
    kz = fill(T.zb[:], 0.0, on="sp")
    fill(T.nxs[:], 0, free=False, on="sz")
    k = fill(T.nx4[:], 0, on="sz")
    wait(g.sync, "s", *k)
    for q in range(4):
        g.sync.dma_start(T.nxs[32 * q:32 * q + 16, :], T.nx[:]).then_inc(s.dns, 16)
    a.dma_start(T.xb[:], T.x[:]).then_inc(s.dx, 16)
    g.sync.dma_start(T.nx4[32 * me:32 * me + 16, :], T.nx[:]).then_inc(s.dn4, 16)
    wait(g.sync, "s", *kz)
    for r in range(4):
        g.sync.dma_start(T.p3w[:, 512 * r:512 * r + 512], T.zb[:]).then_inc(s.dz, 16)

    def iota(out, pattern, sem, base=0):
        g.iota(out, pattern, base, 0, allow_small_or_imprecise_dtypes=True).then_inc(sem, 1)
    g.iota(T.pi[:], [[0, 1]], 0, 1).then_inc(s.g0, 1)
    iota(T.io16[:], [[1, 16]], s.g3)
    iota(T.iob[:], [[32, 16]], s.g3)
    iota(T.io256[:], [[1, 256]], s.g1, 1)
    g.wait_ge(s.dnat, 16)
    call([(forwarders(topo, core, T.cores[others[k]])[h], 2 * k + h, 2 * len(rest), s.f0, T.natl[2 * me + h], T.fn[:]) for k in rest for h in (0, 1)])
    call([(T.cores[others[peer]], h, 2, s.m0, T.natl[2 * me + h], T.natl[2 * me + h]) for h in (0, 1)])

    wait(v, "v", "g0", 1)
    ts(T.ic[:, 0:1], T.pi[:], 15, A.bitwise_and, free=True)
    ts(T.ic[:, 1:2], T.pi[:], 31, A.bitwise_and, free=True)
    cp(new("q", 2), T.ic[:])
    q16, q32 = T.col[:, 0:1], T.col[:, 1:2]
    wait(v, "v", "g3", 2)
    ts(T.eq[:], T.io16[:], q16, A.is_equal)
    ts(T.eqh[:], T.io16[:], q32, A.is_equal, free=True)
    ke = ts(new("even"), q32, 16.0, A.is_lt, free=True)
    fill(T.rs[:], 1.0)
    fill(T.w1[:, 128:272], 0.0)
    ko = ts(T.offsel[:], T.iob[:], q32, A.add, on="sp")
    fill(T.f3[:], 0.0)
    kfill = fill(T.rs[:, 0:64:4], 0.0, free=False)
    wait(a, "a", *ke)
    wait(a, "a", *kz)
    kz3 = act(new("z3"), eq(3), bias=eq(14), free=True)
    act(new("z7"), eq(7), bias=eq(14), free=True)
    act(new("u1"), q16, scale=48.0, bias=-193.0, free=True)
    act(T.d01[:], T.zb[:, 0:128], bias=c("even"), free=True)
    act(new("v", 2), eq(4, 2), bias=c("z3"))
    act(new("vme"), eq(8), bias=c("z7"), free=True)
    act(new("init1"), eq(7), scale=-272.0, bias=c("u1"), free=True)
    v0 = col["v"][2]
    for k in range(2):
        act(T.win2[:, 512 * others[k]:512 * others[k] + 512], T.zb[:], bias=T.col[:, v0 + k:v0 + k + 1], free=k > 0)
    wait(a, "a", "g1", 1)
    for h in range(2):
        kw = act(T.win2[:, 512 * me + h:512 * me + 512:2], T.io256[:], scale=eq(9), bias=c("vme"), free=True)

    wait(v, "v", "dsb", 256)
    ts(T.sx[:], T.stb[:, 0:8], 513.0, A.mult, free=True)
    ts(T.b0[:], T.stb[:, 8:16], 32.0, A.mult, free=True)
    kq = cp(T.qst[:], T.stb[:, 0:8], on="sp")
    ts(T.sw[:], T.sx[:], 3, A.logical_shift_right, 511, A.bitwise_and)
    ts(T.sy[:], T.b0[:], 32, A.bitwise_and, free=True)
    ts(T.b1[:], T.stb[:, 8:16], 1, A.logical_shift_right, free=True, on="su")
    tt(T.sz[:], T.sw[:], T.sy[:], A.add)
    ts(T.win2[:, 512 * others[2]:512 * others[2] + 512], T.zb[:], eq(6), A.add, c("z3"), A.add, free=True, on="sp", after=[kz3])
    cp(T.q1l[:, 0:16:2], T.sz[:])
    cp(T.q1l[:, 1:16:2], T.sz[:], free=True)
    wait(v, "v", "dnx", 64)
    ts(T.nd[:], T.p1w[:].indirect(T.q1l[:]), 2.0, A.mult)
    vec(v.transpose, T.tn[:], T.nd[:])
    tt(T.uf[:], T.tn[:, :, 0], T.b1[:], A.add, after=[("su", cnt["su"])])
    ku = cp(T.ul[:, 8 * me:8 * me + 8], T.uf[:])
    mine = T.ul[:, 8 * me:8 * me + 8]
    to_rest(1, ku, s.f1, lambda k: mine, T.fu[:])
    to_peer(ku, s.m1, lambda k: mine, mine)
    iota(T.w2[:, 256:400], [[0, 144]], s.g2)

    act(T.c0l[:], T.io256[:].indirect(T.qst[:, 0:8]), C.Copy, free=True, on="sa", after=[kq])
    kvs1 = act(T.vs1[:], T.c0l[:].indirect(T.offsel[:, 0:4]), C.Copy, on="sa", after=[ko])
    act(new("lh1"), T.eqh[:, 0:1], bias=T.eqh[:, 1:2])
    act(new("l1"), eq(0), bias=eq(1), free=True)
    act(new("init2"), q16, scale=48.0, bias=-1.0, free=True)
    act(new("nt"), eq(3), scale=-1.0, bias=1.0, free=True)
    for k in range(3):
        act(new("t%d" % k), eq(8), C.Copy, scale=float(CAP * k - LAND), free=True)
    act(new("q16m"), q16, bias=-256.0, free=True)
    act(new("b%d" % me), eq(13), C.Copy, scale=me + 1.0, free=True)
    act(new("l2h"), T.eqh[:, 2:3], bias=c("lh1"))
    act(new("l2"), eq(2), bias=c("l1"), free=True)
    for k in range(3):
        act(new("b%d" % others[k]), eq(13), scale=others[k] + 1.0, bias=c("t%d" % k), free=True)
    act(T.trc[:], T.iob[:], scale=0.5, bias=c("q16m"), free=True)
    act(T.c0m[:], T.vs1[:], scale=eq(8), bias=c("b%d" % me), free=True, after=[kvs1])
    act(new("k8"), eq(8), bias=eq(14), free=True)
    act(new("keep"), c("k8"), bias=c("l2h"))
    act(new("nz"), c("l2"), scale=-1.0, bias=c("nt"), free=True)
    act(T.data0[:], T.zb[:, 0:256], bias=c("keep"))
    act(new("nz8"), eq(8), scale=-1.0, bias=c("nz"), free=True)
    kw2 = act(T.data0[:, 0:256:128], T.zb[:, 0:2], bias=c("l2h"))
    act(T.ac[:], T.trc[:], scale=-1.0, bias=-1.0, free=True, on="sb")
    act(T.e3[:, 1:32:2], T.trc[:], C.Copy, free=True, on="sb")
    act(new("kp"), T.eqh[:, 15:16], bias=c("l2"), free=True, on="sb")
    k3 = act(T.data3[:], T.zb[:], bias=c("kp"), on="sb")

    vec(v.transpose, T.nxt[:], T.nxs[:], free=True, on="su", after=[("dns", 64)])
    kg1 = cp(T.gg1[:], T.win2[:].indirect(mine), after=[kw, ("sp", cnt["sp"])])
    ts(T.nxr[:], T.nxt[:, 0:16], 8, A.logical_shift_right, on="su")
    scan(T.gs1[:], T.d01[:], T.gg1[:], c("init1"))
    for r in range(4):
        km = ts(T.mk[32 * r:32 * r + 32, :], T.nxr[32 * r:32 * r + 32, :], float(others[r] if r < 3 else me), A.is_equal, free=r > 0, on="su")
    vec(v.transpose, T.tg[:], T.gs1[:])
    tt(T.x1[:], T.tg[:, :, 4:8], T.tg[:, :, 20:24], A.mult)
    kxq = vec(v.quantize_mx, T.xq[:], T.xs[:], T.xb[:], free=True, on="sz", after=[("dx", 16)])
    scan(T.y1[:], T.rs[:, 0:16], T.x1[:], 0.0, after=[kfill])
    ts(T.off1[:], T.y1[:, 3:16:4], 128.0, A.add)
    cp(T.w1[:].indirect(T.off1[:, 0:4]), T.vs1[:], after=[kvs1])
    cp(T.d1[:, 0:18:2, :], T.w1[:, 128:272])
    cp(T.d1[:, 1:18:2, :], T.w1[:, 128:272], free=True)
    vec(v.transpose, T.td1[:], T.d1[:])
    tt(T.l1f[:], T.td1[:, :, 0], T.td1[:, :, 16], A.add)
    kl = ts(T.list1[:, 0:9], T.l1f[:], -1.0, A.add)
    kpk = cp(T.pk1[:].bitcast(dt.uint32), T.xq[:].bitcast(dt.uint32).indirect(T.list1[:, 0:9]), after=[kxq])
    ksc = act(T.ps1[:], T.xs[:].indirect(T.list1[:, 0:9]), C.Copy, on="sa", after=[kl, kxq])
    at = order(topo, T.cores, others[peer]).index(me)
    to_rest(0, kpk, s.f1c, lambda k: T.pk1[:, CAP * k:CAP * k + CAP].bitcast(dt.uint8), T.fc1[:].bitcast(dt.uint8))
    to_rest(1, ksc, s.f1s, lambda k: T.ps1[:, CAP * k:CAP * k + CAP], T.fs1[:])
    to_peer(kpk, s.c1, lambda k: T.pk1[:, CAP * k:CAP * k + CAP].bitcast(dt.uint8), T.cb[:, CAP * at:CAP * at + CAP].bitcast(dt.uint8))
    to_peer(ksc, s.c1, lambda k: T.ps1[:, CAP * k:CAP * k + CAP], T.cbs[:, CAP * at:CAP * at + CAP])
    iota(T.w3[:, 256:448], [[0, 192]], s.g4)
    iota(T.c3[:], [[0, 192]], s.g4)

    wait(g.sync, "s", *km)
    wait(g.sync, "s", *kg1)
    for b in range(0, 128, 32):
        g.sync.dma_start(T.win2[b:b + 4, 512 * me:512 * me + 512], T.mk[:]).then_inc(s.dmk, 16)
        g.sync.dma_start(T.win2[b + 16:b + 19, 512 * me:512 * me + 512], T.mk[0:96, :]).then_inc(s.dmk, 16)
    g.sync.dma_start(T.wb[:], T.w[:]).then_inc(s.dw, 16)
    g.sync.wait_ge(s.m0, 40)
    for r in others:
        g.sync.dma_start(T.nx4[32 * r:32 * r + 16, :], T.natl[2 * r:2 * r + 2]).then_inc(s.dn4, 16)
    wait(g.sync, "s", *kxq)
    g.sync.dma_start(T.cb[:, LAND:LAND + TX].bitcast(dt.uint8), T.xq[:].bitcast(dt.uint8)).then_inc(s.dcb, 16)
    g.sync.dma_start(T.cbs[:, LAND:LAND + TX], T.xs[:]).then_inc(s.dcb, 16)
    g.sync.dma_start(T.lp[:, 96:176].bitcast(dt.uint8), T.xq[:, 0:80].bitcast(dt.uint8)).then_inc(s.dcb, 16)
    g.sync.dma_start(T.lps[:, 96:176], T.xs[:, 0:80]).then_inc(s.dcb, 16)

    wait(a, "a", "m1", 24)
    wait(a, "a", "dmk", 128)
    kgb = act(T.g2[:, 256:512], T.win2[:].indirect(T.ul[:, 16:32]), C.Copy, on="sa")
    wait(v, "v", "m1", 24)
    wait(v, "v", "dmk", 128)
    wait(v, "v", *kw2)
    cp(T.g2[:, 0:256], T.win2[:].indirect(T.ul[:, 0:16]))
    vec(v.transpose, T.nt4[:], T.nx4[:], free=True, on="su", after=[("dn4", 64)])
    ksA = scan(T.s2[:, 0:256], T.data0[:], T.g2[:, 0:256], c("init2"))
    ts(T.r4[:], T.nt4[:, 0:16], 8, A.logical_shift_right, on="su")
    ts(T.cp4[:], T.nt4[:, 0:16], 1.0 - 256.0 * me, A.add, free=True, on="su")
    ksB = scan(T.s2[:, 256:512], T.data0[:], T.g2[:, 256:512], T.s2[:, 255:256], after=[kgb])
    vec(v.transpose, T.tg2[:, 0:8, :], T.s2[:, 0:256], free=True, on="sz")
    kmp = ts(T.mp[:], T.r4[:], float(me), A.is_equal, on="su")
    vec(v.transpose, T.tg2[:, 8:16, :], T.s2[:, 256:512], free=True, on="sz", after=[ksB])
    quant(0)
    for n, r in enumerate(sorted(range(4), key=lambda r: (r >= 2, r != me))):
        kvsel = act(T.vown[:] if r == me else T.vsel[:, 64 * r:64 * r + 64], T.s2[:, 128 * r:128 * r + 128].indirect(T.offsel[:, 0:4]), free=n > 0, on="sa",
                    after=[ksB if r >= 2 else ksA], scale=c("nz8" if r == me else "nz"), **({} if r == me else {"bias": c("b%d" % r)}))
    tt(T.x2[:, 3:64:4], T.tg2[:, :, 3], T.trc[:], A.mult, on="sz")
    for k in range(3):
        tt(T.x2[:, k:64:4], T.tg2[:, :, k], T.tg2[:, :, 16 + k], A.mult, free=True, on="sz")
    quant(1)
    scan(T.y2[:], T.rs[:], T.x2[:], 0.0, on="sz")
    tt(T.vsel[:, 64 * me:64 * me + 64], T.vown[:], T.c0m[:], A.add, free=True, after=[kvsel])
    ts(T.off2[:], T.y2[:, 3:64:4], 256.0, A.add, on="sz")
    kwq = quant(2)
    wait(v, "v", "g2", 1)
    cp(T.w2[:].indirect(T.off2[:, 0:16]), T.vsel[:], after=[("sz", cnt["sz"])])

    wait(g.sync, "s", "dz", 64)
    wait(g.sync, "s", *kmp)
    for b in (0, 16):
        g.sync.dma_start(T.p3w[b + 15:b + 16, :], T.mp[:]).then_inc(s.drow, 16)
        g.sync.dma_start(T.p3w[b + 3:b + 4, :], T.cp4[:]).then_inc(s.drow, 16)
        for k, r in enumerate(others):
            g.sync.dma_start(T.p3w[b + k:b + k + 1, 512 * r:512 * r + 512], T.mp[32 * r:32 * r + 32, :]).then_inc(s.drow, 16)

    for x in (T.aw, T.bw, T.cw):
        act(x[:, 0:1], T.zb[:, 0:1], C.Copy, free=x is not T.aw, on="sb")
    for k in range(3):
        kkc = act(T.kc[:, :, k], T.zb[:, 0:12], bias=float([400, 496, 544][k]), free=True, on="sb")
    wait(a, "a", "drow", 16 * 10)
    kg3 = act(T.g3[:], T.p3w[:].indirect(T.ul[:]), C.Copy, on="sa")

    cp(T.d2[:, 0:18:2, :], T.w2[:, 256:400])
    cp(T.d2[:, 1:18:2, :], T.w2[:, 256:400], free=True)
    vec(v.transpose, T.td2[:], T.d2[:])
    scan(T.s3[:], T.data3[:], T.g3[:], 0.0, free=True, on="sz", after=[kg3, k3])
    for h in range(2):
        tt(T.nf[:, :, h, :], T.td2[:, :, :, 8 + h], T.td2[:, :, :, 24 + h], A.add, free=h > 0)
    vec(v.transpose, T.tg3[:], T.s3[:], on="sz")
    kl2 = ts(T.list2[:], T.nf[:], LAND - 1.0, A.add)
    tt(T.e3[:, 0:32:2], T.tg3[:, :, 15], T.ac[:], A.add, on="sz")
    cp(T.f3[:, 1:32:2], T.tg3[:, :, 31], free=True, on="sz")
    wait(a, "a", "c1", 48)
    wait(a, "a", "dcb", 64)
    ksa = act(T.ps2[:, 0:192], T.cbs[:].indirect(T.list2[:, 0:12]), C.Copy, on="sa", after=[kl2])
    ksb = act(T.ps2[:, 192:288], T.cbs[:].indirect(T.list2[:, 12:18]), C.Copy, on="sa")
    wait(v, "v", "c1", 48)
    wait(v, "v", "dcb", 64)
    kpa = cp(T.pk2[:, 0:192].bitcast(dt.uint32), T.cb[:].bitcast(dt.uint32).indirect(T.list2[:, 0:12]))
    scan(T.y3[:], T.f3[:], T.e3[:], 0.0, on="sz")
    kpb = cp(T.pk2[:, 192:288].bitcast(dt.uint32), T.cb[:].bitcast(dt.uint32).indirect(T.list2[:, 12:18]), free=True, on="so")
    ts(T.off3[:], T.y3[:, 1:32:2], 256.0, A.add, on="sz")
    to_rest(0, kpa, s.f2c, lambda k: T.pk2[:, 96 * k:96 * k + 96].bitcast(dt.uint8), T.fc2[:].bitcast(dt.uint8))
    to_rest(1, ksa, s.f2s, lambda k: T.ps2[:, 96 * k:96 * k + 96], T.fs2[:])
    to_peer(kpb, s.c2p, lambda k: T.pk2[:, 96 * k:96 * k + 96].bitcast(dt.uint8), T.lp[:, 0:96].bitcast(dt.uint8))
    to_peer(ksb, s.c2p, lambda k: T.ps2[:, 96 * k:96 * k + 96], T.lps[:, 0:96])

    tt(T.val3[:], T.s3[:].indirect(T.offsel[:, 0:16]), T.vsel[:], A.add, free=True)
    wait(v, "v", "g4", 2)
    cp(T.w3[:].indirect(T.off3[:, 0:16]), T.val3[:], after=[("sz", cnt["sz"])])
    cp(T.dp[:, 0:24:2, :], T.w3[:, 256:448])
    cp(T.dp[:, 1:24:2, :], T.w3[:, 256:448], free=True)
    vec(v.transpose, T.t3[:], T.w3[:, 256:448], free=True, on="su")
    vec(v.transpose, T.tp[:], T.dp[:])
    tt(T.c3[:, :, 13:15], T.t3[:, :, 13:15], T.t3[:, :, 29:31], A.add, on="su")
    kyy = tt(T.yy[:], T.tp[:, :, 0:10], T.tp[:, :, 16:26], A.add)
    kpl = vec(v.transpose, T.pl[:], T.c3[:], on="su")
    cp(T.qbc[0:32, 0:12], T.yy[0:32, :, 3], free=True, on="so", after=[kyy])
    cp(T.qbc[0:32, 12:24], T.yy[0:32, :, 9], free=True, on="so")
    tt(T.x3[:, :, 0:3], T.yy[:, :, 0:3], T.kc[:], A.add, after=[kkc])
    ts(T.x3[:, :, 3], T.yy[:, :, 8], float(LAND), A.add, free=True)
    cp(T.qbc[32:64, :], T.qbc[0:32, :], on="so")
    tt(T.x3m[:], T.x3[:], T.yy[:, :, 4:8], A.mult)
    kqbc = cp(T.qbc[64:128, :], T.qbc[0:64, :], on="so")
    ky4 = scan(T.y4[:], T.rs[:, 0:48], T.x3m[:], 0.0)
    for b in range(0, 128, 32):
        kq0 = cp(T.q0[b:b + 32, :], T.y4[0:32, 3:48:4], free=True, on="so", after=[ky4])

    def w(k):
        return T.wq[:, 128 * k:128 * k + 128], T.ws[:, 128 * k:128 * k + 128]
    m2 = mm(T.ps[:, 1024:1280], *w(2), T.xq[:], T.xs[:], True, True, free=True, after=[kwq])
    m1 = mm(T.ps[:, 512:768], *w(1), T.xq[:], T.xs[:], True, True)
    wait(g.tensor, "t", "c1", 48)
    wait(g.tensor, "t", "dcb", 64)
    m0 = mm(T.ps[:, 0:400], *w(0), T.cb[:], T.cbs[:], True, True)
    act(T.cw[:, 1:257], T.ps[:, 1024:1280], C.Copy, on="sb", after=[m2])
    act(T.bw[:, 1:257], T.ps[:, 512:768], C.Copy, free=True, on="sb", after=[m1])
    kaw = act(T.aw[:, 1:401], T.ps[:, 0:400], C.Copy, free=True, on="sb", after=[m0])
    wait(a, "a", *kaw)
    kt1 = act(T.t1[:], T.cw[:, 0:257].indirect(T.qbc[:, 0:12]), C.Copy, on="sa", after=[kqbc])
    kid = act(T.idl[:], T.pl[:], bias=-1.0, on="sa", after=[kpl])
    wait(g.sync, "s", *kid)
    g.sync.dma_start(T.id[0:1, :], T.idl[13:14, :]).then_inc(s.did, 16)
    g.sync.dma_start(T.id[1:2, :], T.idl[14:15, :]).then_inc(s.did, 16)
    tt(T.t2[:], T.bw[:, 0:257].indirect(T.qbc[:, 12:24]), T.t1[:], A.add, on="so", after=[kaw, kqbc, kt1])

    wait(g.tensor, "t", "c2p", 16)
    mm(T.ps[:, 2048:2176], *w(0), T.lp[:, 0:128], T.lps[:, 0:128], True, False)
    mp = mm(T.ps[:, 2048:2176], *w(1), T.lp[:, 48:176], T.lps[:, 48:176], False, True, free=True)
    wait(g.tensor, "t", "c2", 32)
    mm(T.ps[:, 1536:1680], *w(0), T.lr[:, 0:144], T.lrs[:, 0:144], True, False)
    mr = mm(T.ps[:, 1536:1680], *w(1), T.lr[:, 48:192], T.lrs[:, 48:192], False, True, free=True)
    kpw = act(T.aw[:, 545:593], T.ps[:, 2048:2096], C.Copy, free=True, on="sb", after=[mp])
    cp(T.aw[:, 401:545], T.ps[:, 1536:1680], free=True, on="so", after=[mr])
    ky = tt(T.yo[:], T.aw[:, 0:593].indirect(T.q0[:, 0:12]), T.t2[:], A.add, on="so", after=[kq0, kpw])
    wait(g.sync, "s", *ky)
    g.sync.dma_start(T.y[:], T.yo[:]).then_inc(s.dy, 16)

    g.wait_ge(s.dy, 16)
    g.wait_ge(s.did, 32)
    for x in ("sv", "su", "so", "sz", "sq", "sa", "sb", "sk", "sp", "st", "loc"):
        wait(g, "g", x, cnt[x])
